import numpy as np, ml_dtypes
CORES = [3,11,19,27,35,43]
N = 6
BF = ml_dtypes.bfloat16
W, I, B, S, RO, H = 8192, 64, 128, 8, 4, 10
def some(rng, k):
    o = np.argsort(rng.random(k.shape[:-1] + (16,) + k.shape[-1:]), axis=-2)
    return np.where(o < k[..., None, :], 0, 255)
def parts(rng):
    x = rng.integers(0, 256, (N, 8, 16, W)); w = rng.integers(0, 16, (N, 8, 16, 1)); c = rng.integers(0, 128, (N, 8, 16, I))
    l = rng.integers(1, 5, (N, 8, 16, I)); s = rng.integers(0, W, (N, 8, 16, I))
    v = rng.choice(np.array([96, 176, 208, 224, 236, 244, 252]), (N, 8, 1, I))
    return x, w, c, l, s, np.clip(v + rng.integers(-12, 13, (N, 8, 16, I)), 0, 255)
def small(a):
    return np.ascontiguousarray(a.reshape(N, 128, -1)).astype(np.float32).astype(BF)
def pack(x, w, c, l, s, fl):
    return {"x": small(x), "wt": small(w), "ch": small(c), "sp": small(l), "st": np.ascontiguousarray(s.reshape(N, 128, I)).astype(np.int32), "fl": small(fl)}
def setup_inputs(rng):
    return pack(*parts(rng))
def setup_inputs_spread(rng):
    x, w, c, l, s, fl = parts(rng)
    x = (np.exp2(8 * rng.random((N, 8, 1, W))) * rng.random(x.shape)).astype(np.int64)
    w = np.where(rng.random(w.shape) < 0.4, 0, w)
    c = np.where(rng.random((N, 8, 1, I)) < 0.5, c, np.exp2(7 * rng.random(c.shape)).astype(np.int64) - 1)
    l = rng.choice(np.array([1, 1, 1, 2, 3, 4]), l.shape)
    fl = (np.exp2(8 * rng.random((N, 8, 1, I))) * (0.5 + 0.5 * rng.random(fl.shape))).astype(np.int64)
    return pack(x, w, c, l, s, fl)
def setup_inputs_ends(rng):
    x, w, c, l, s, fl = parts(rng)
    d = rng.choice(np.array([0.04, 0.1, 0.3, 0.5]), (N, 8, 1, 1)); d[:, 7] = 0.5
    e = 255 * (rng.random(x.shape) < d); k = rng.random((N, 8, 1, W)); full = np.where(np.arange(8) == 7, 0.3, 0.03).reshape(1, 8, 1, 1)
    e = np.where(k < full, 255, np.where(k > 0.85, 0, e)); x = np.where((k > 0.5) & (k < 0.6), x, e)
    w = 15 * rng.integers(0, 2, w.shape); w[:, 7] = 15; w[:, 1] = 0; w[:, 0, 0] = 0; w[:, 0, 15] = 15
    b = rng.random((N, 8, 1, I)); c = np.where(b < 0.15, 127, np.where(b > 0.85, 0, 127 * rng.integers(0, 2, c.shape)))
    l = 1 + 3 * rng.integers(0, 2, l.shape); s = np.where(rng.random(s.shape) < 0.25, s, (W - 1) * rng.integers(0, 2, s.shape))
    fl = some(rng, rng.integers(0, 17, (N, 8, I))); fl[N - 2:] = some(rng, rng.integers(H, 17, (2, 8, I)))
    x[N - 2, 6, H - 1:] = 0; fl[N - 2, 6, :, I - 1] = np.where(np.arange(16) < H - 1, 0, 255)
    l[N - 1, 7, :, :2] = 4; s[N - 1, 7, :, :2] = W - 1
    l[N - 1, 7, 13:, I - 1] = np.array([1, 4, 4]); s[N - 1, 7, 13:, I - 1] = np.array([(0 - 613) & (W - 1), (W - 1 - 2452) & (W - 1), W - 1])
    c[N - 1, 7, 0, :2] = 127; c[N - 1, 7, 0, I - 1] = 127
    x[:, 7, :, (W - 1 + 2452) & (W - 1)] = 255; x[:, 7, :, W - 1] = 255; x[:, 7, 15] = 255
    return pack(x, w, c, l, s, fl)
def setup_inputs_corners(rng):
    x, w, c, l, s, fl = parts(rng); q = rng.permutation(N); ar = np.arange(16)[:, None]
    w[:, 0] = 0; b = rng.integers(0, 4, (N, 1, I)); c[:, 0] = np.where(b == 0, 3, np.where(b == 1, 0, np.where(b == 2, 127, c[:, 0])))
    x[:, 1] = np.minimum(x[:, 1], 254); fl[:, 1] = some(rng, rng.choice(np.array([0, H - 1, H, 16]), (N, I)))
    v = rng.integers(1, 255, (N, 16, 1)); x[:, 2] = v; fl[:, 2] = v + np.minimum(some(rng, rng.choice(np.array([H - 1, H, 16]), (N, I))), 1)
    w[:, 3] = 0; w[:, 3, 0] = 1; x[:, 3, 0, ::2] = 255; fl[:, 3] = fl[:, 3] // 2
    b = rng.integers(0, 4, (N, 1, I)); l[:, 4] = np.where(b == 0, 4, np.where(b == 1, 1, np.where(b == 2, 1 + 3 * (ar == 15), 1 + 3 * (ar & 1)))); fl[:, 4] = fl[:, 4] // 2
    e = (W - 1) * rng.integers(0, 2, (N, 16, I)); s[:, 5] = np.where(rng.random((N, 16, I)) < 0.5, e, (e - 613 * l[:, 5]) & (W - 1))
    w[:, 6] = 15; x[:, 6] = rng.integers(224, 256, (N, 16, W)); c[:, 6] = rng.choice(np.array([0, 126, 127]), (N, 16, I))
    x[q[0]] = np.minimum(x[q[0]], 254); fl[q[0]] = some(rng, np.full((8, I), H - 1))
    fl[q[1]] = some(rng, rng.integers(H, 17, (8, I))); fl[q[2]] = some(rng, rng.integers(H, 17, (8, I)))
    x[q[2], 7] = np.minimum(x[q[2], 7], 254); fl[q[2], 7, :, I - 1] = some(rng, np.full(1, H - 1))[:, 0]
    return pack(x, w, c, l, s, fl)
def setup_inputs_crowd(rng):
    x, w, c, l, s, fl = parts(rng); q = rng.permutation(N)
    s[:, :7] = rng.integers(0, W, (N, 7, 1, 1)); l[:, :7] = rng.integers(1, 5, (N, 7, 1, 1)); c[:, :7] = rng.integers(0, 128, (N, 7, 16, 1))
    s[:, 4:7, 15, I - 1] = rng.integers(0, W, (N, 3)); c[:, 4:7, :, I - 1] = rng.integers(0, 128, (N, 3, 16))
    fl = some(rng, rng.integers(H, 17, (N, 8, I)))
    for a in q[:N // 2]:
        x[a, 7] = np.minimum(x[a, 7], 254); fl[a, 7, :, I - 1] = some(rng, np.full(1, H - 1))[:, 0]
    return pack(x, w, c, l, s, fl)
def setup_inputs_late(rng):
    x, w, c, l, s, fl = parts(rng); q = rng.permutation(N); a, b = int(q[0]), int(q[1])
    x[a] = np.minimum(x[a], 254); fl[a] = some(rng, np.full((8, I), H - 1)); fl[b] = some(rng, rng.integers(H, 17, (8, I)))
    for r, g, low in ((a, 7, 8), (b, 0, 0)):
        hot = B * int(rng.integers(8, I)); w[r, g] = 0
        x[r, g] = rng.integers(0, 101, (16, W)); x[r, g, :, hot] = rng.integers(200, 255, 16)
        fl[r, g, :, low:] = rng.integers(110, 151, (16, I - low))
        l[r, g] = 1; s[r, g] = (hot - 613) & (W - 1)
        if g == 7: l[(a - 2) % N, 7] = 1; s[(a - 2) % N, 7] = (hot - 613) & (W - 1)
    s[(a - 1) % N, 7] = (16 * rng.integers(0, W // 16, (16, I)) - (I - 8)) & (W - 1)
    l[(b - 1) % N, 0] = 1; s[(b - 1) % N, 0] = W - 613 - 8 * I
    c[(b - 1) % N, 0] = 16 * rng.integers(0, 8, (16, I)) + 4 * rng.integers(1, 4, (16, I))
    return pack(x, w, c, l, s, fl)
def check_inputs(d):
    bad = []
    for k, lo, hi in (("x", 0, 255), ("wt", 0, 15), ("ch", 0, 127), ("sp", 1, 4), ("st", 0, W - 1), ("fl", 0, 255)):
        v = np.asarray(d[k]).astype(np.float64)
        if not (np.all(v >= lo) and np.all(v <= hi)): bad.append("range of " + k)
        if np.any(v != np.floor(v)): bad.append("whole numbers of " + k)
    return bad
def reference(x, wt, ch, sp, st, fl):
    X, Q, C, L, Z, F = [v.astype(np.float32).astype(np.int32).reshape(N, 8, 16, -1) for v in (x, wt, ch, sp, st, fl)]
    A = [0] * N; row = np.arange(16)[:, None]
    for t in range(RO):
        if t > 0: C, L, Z = np.roll(C, 1, axis=0), np.roll(L, 1, axis=0), np.roll(Z, 1, axis=0)
        for a in range(N):
            l = L[a]
            at = np.arange(16)[None, :, None, None]; at = at + np.where(at >= row[None, None], l[:, None], 0)
            e = np.take_along_axis(np.concatenate([C[a], np.zeros((8, 4, I), np.int32)], axis=1)[:, :, None, :], at, 1)
            e = np.concatenate([e, np.zeros((8, 1, 16, I), np.int32)], axis=1)
            s = (Z[a] + 613 * l + A[a]) & (W - 1); p = np.zeros((8, 16, I), np.int64); V = np.zeros((8, 16, 16, I), np.int32); log = []
            for k in range(S):
                z = np.take_along_axis(X[a], s.reshape(8, 1, 16 * I), 2).reshape(8, 16, 16, I)
                V = np.maximum(V, z); c = np.take_along_axis(e, np.minimum(p, 16)[:, None], 1)[:, 0].astype(np.int64)
                u = np.add.reduce(Q[a][..., None] * z, axis=1).astype(np.int64)
                n = 1 + (((u >> 3) + c) & 3); log.append((p, n))
                s = (((u * (2 * c + 1)) >> 3) + 37 * u + c) & (W - 1); p = p + n
            fails = np.add.reduce((V >= F[a][:, :, None, :]).astype(np.int32), axis=1) >= H
            best = np.argmax(np.where(fails, 16 * l + 15 - row[None], 0 - 1), axis=1)[:, None, :]; ok = np.any(fails, axis=1)[:, None, :]
            nl = np.ones((8, 16, I), np.int64)
            for p, n in log: nl = np.where(row[None] == np.take_along_axis(p, best, 1), np.take_along_axis(n, best, 1), nl)
            v = np.take_along_axis(V, best[:, None], 2)[:, :, 0]
            C[a] = np.where(ok, np.take_along_axis(e[:, :16], best[:, None], 2)[:, :, 0], C[a]); L[a] = np.where(ok, nl, l)
            to = B * np.arange(I)[None, None, :] + (np.add.reduce(Q[a] * v, axis=1)[:, None, :] & (B - 1))
            to = np.broadcast_to(to, (8, 16, I)); np.put_along_axis(X[a], to, np.where(ok, v, np.take_along_axis(X[a], to, 2)), 2)
            F[a] = np.where(ok, (F[a] + v) >> 1, F[a]); A[a] = int(np.sum(ok))
    sums = np.add.reduce(X.reshape(N, 128, I, B), axis=3)
    return {"yc": C.reshape(N, 128, I).astype(np.float32).astype(BF), "yl": L.reshape(N, 128, I).astype(np.float32).astype(BF),
            "yf": F.reshape(N, 128, I).astype(np.float32).astype(BF), "ys": sums.astype(np.float32)}

@@ -1,0 +1,516 @@
+from concourse.mybir import dt, AluOpType, AxisListType, ActivationFunctionType
+
+ADD, SUB, MUL, MAX, MIN = AluOpType.add, AluOpType.subtract, AluOpType.mult, AluOpType.max, AluOpType.min
+GE, EQ = AluOpType.is_ge, AluOpType.is_equal
+SHR, AND = AluOpType.arith_shift_right, AluOpType.bitwise_and
+IDT, SIGN = ActivationFunctionType.Identity, ActivationFunctionType.Sign
+COPY = ActivationFunctionType.Copy
+RO, S, W = 4, 8, 8192
+DUMP = W + 64
+RTW = 33 * 64
+
+SCRATCH = {}
+POOL = {}
+
+
+def _d(names, cols, dtype, where="sbuf"):
+    for n in names.split():
+        SCRATCH[n] = (where, [128, cols], dtype)
+
+
+def _pool(buf, names, cols, dtype):
+    for k, n in enumerate(names.split()):
+        POOL[n] = (buf, k * cols, cols)
+    SCRATCH[buf] = ("sbuf", [128, len(names.split()) * cols], dtype)
+
+
+_d("X", DUMP, "bfloat16")
+_d("ZA OA ZB OB", 4096, "bfloat16")
+_d("Z7 CB GEb", 1024, "bfloat16")
+_d("VB", 1040, "bfloat16")
+_d("RT", RTW, "bfloat16")
+_d("Gm Dm Wm GT", 2048, "bfloat16")
+_d("ID BO BO3 BO1 WB8 WB1 SH1 SH2 SH3 SH4 IN1 IN2 R0 NEG ON16 shx", 128, "bfloat16")
+_d("ONE SC PX OK VV OLD DIF LM15", 64, "bfloat16")
+_d("MASK4", 1024, "bfloat16")
+_d("MASK16 SX", 128, "bfloat16")
+_d("LOG OHL", 576, "bfloat16")
+_d("KQ AT SG", 512, "bfloat16")
+_d("MK CM", 256, "bfloat16")
+_d("F0 F1 F2 F3 F4", 64, "bfloat16")
+_d("LND0 LND1 LND2 LND3 SND0 SND1 SND2 SND3", 128, "bfloat16")
+_d("WT", 1, "bfloat16")
+_d("ST0 ST1 ST2 ST3", 64, "int32")
+_pool("INTS", "SA I1 N64 DH YI SI T613 S0 BI LI MI HI HM FVI FH", 64, "int32")
+_d("ROW CQI CGI", 128, "int32")
+_d("KQI", 512, "int32")
+_d("PI QI GI", 1, "int32")
+_d("ROWF CQF CGF", 128, "float32")
+_d("PC QC GC QC64 QN4 C16M ACOL", 1, "float32")
+_d("PCL PCG", 4, "float32")
+_d("EQ16", 16, "float32")
+_d("MC", 8, "float32")
+_pool("FLTS", "CA CBF PR M16F DIAG OFXC PRI FT GG LE DL MD SD X1 OKD X2 SD2 FD FE", 64, "float32")
+_d("I4 BV4 BX4 O4 O4X", 4, "float32")
+_d("L0 QS", 128, "float32")
+_d("DP0 DP1 DP2 DP3 DP4 DP5 DP6 DP7", 128, "float32")
+_d("YS", 64, "float32")
+_d("OFFZ OFFC", 64, "uint16")
+_d("OV OX", 4, "uint16")
+_d("psF0 psF1 psW psC psA psB psY", 512, "float32", "psum")
+_d("psT", 1024, "bfloat16", "psum")
+
+SEMAPHORES = ["qv", "qs", "qt", "qg", "dX", "dW", "dC", "dL", "dS", "dF", "oC", "oL", "oF", "oS", "loc"]
+SEMAPHORES += ["st%d" % t for t in range(1, RO)] + ["arr%d" % t for t in range(1, RO)]
+
+C_SCALAR, Z_SCALAR, Z0_SCALAR = 38, 26, 38
+
+
+class Ap(tuple):
+    pass
+
+
+def rank_program(g, core, T, topo):
+    rank = T.rank_of(core)
+    if rank is None:
+        return
+    n = len(T.cores)
+    queue = {"v": g.vector, "s": g.scalar, "t": g.tensor, "g": g, "y": g.sync}
+    count = {"v": 0, "s": 0, "t": 0, "g": 0}
+    known = {q: {} for q in queue}
+    snap = {}
+    seen = {}
+
+    def A(name, a=None, b=None, step=1, p=128):
+        buf, off, cols = POOL[name] if name in POOL else (name, 0, SCRATCH[name][1][1])
+        a = 0 if a is None else a
+        b = cols if b is None else b
+        ap = T[buf][0:p, off + a:off + b] if step == 1 else T[buf][0:p, off + a:off + b:step]
+        return Ap((ap, ((name, a, b),)))
+
+    def IND(win, off):
+        return Ap((win[0].indirect(off[0]), win[1] + off[1]))
+
+    def wait(q, sem, val):
+        if known[q].get(sem, 0) >= val:
+            return
+        queue[q].wait_ge(T.sem[sem], val)
+        known[q][sem] = val
+        for s, c in snap.get((sem, val), {}).items():
+            if known[q].get(s, 0) < c:
+                known[q][s] = c
+
+    def deps(q, outs, ins):
+        need = {}
+        for w, group in ((True, outs), (False, ins)):
+            for x in group:
+                for name, lo, hi in x[1]:
+                    ps = name.startswith("ps")
+                    for a in seen.get(name, ()):
+                        apart = a[0] >= hi or a[1] <= lo
+                        if apart and not ps:
+                            continue
+                        if a[3] == q:
+                            if q == "t" or apart or not (w or a[2]):
+                                continue
+                        elif not ps and not (w or a[2]):
+                            continue
+                        need[a[4]] = max(need.get(a[4], 0), a[5])
+        for s in sorted(need):
+            wait(q, s, need[s])
+
+    def record(q, outs, ins, sem, val):
+        k = known.get(q, {})
+        for w, group in ((False, ins), (True, outs)):
+            for x in group:
+                for name, lo, hi in x[1]:
+                    lst = seen.setdefault(name, [])
+                    if w:
+                        lst[:] = [a for a in lst if not (lo <= a[0] and a[1] <= hi and k.get(a[4], 0) >= a[5])]
+                    else:
+                        lst[:] = [a for a in lst if not (a[3] == q and not a[2] and (a[0], a[1]) == (lo, hi))]
+                    lst.append([lo, hi, w, q, sem, val])
+
+    def run(q, outs, ins, call):
+        deps(q, outs, ins)
+        sem = "q" + q
+        count[q] += 1
+        snap[(sem, count[q])] = dict(known[q])
+        call().then_inc(T.sem[sem], 1)
+        record(q, outs, ins, sem, count[q])
+
+    def dma(q, sem, out, in_, outs, ins):
+        deps(q, outs, ins)
+        snap[(sem, 16)] = dict(known[q])
+        queue[q].dma_start(out, in_).then_inc(T.sem[sem], 16)
+        record("dma" + sem, outs, ins, sem, 16)
+
+    def landed(name, sem, val):
+        record("net" + sem, [A(name)], [], sem, val)
+
+    def isap(s):
+        return isinstance(s, Ap)
+
+    def tt(out, a, b, op):
+        run("v", [out], [a, b], lambda: g.vector.tensor_tensor(out[0], a[0], b[0], op))
+
+    def ts(out, a, s1, op0, s2=None, op1=None):
+        ins = [a] + [s for s in (s1, s2) if isap(s)]
+        x1 = s1[0] if isap(s1) else s1
+        x2 = s2[0] if isap(s2) else s2
+        if op1 is None:
+            run("v", [out], ins, lambda: g.vector.tensor_scalar(out[0], a[0], x1, None, op0))
+        else:
+            run("v", [out], ins, lambda: g.vector.tensor_scalar(out[0], a[0], x1, x2, op0, op1))
+
+    def cp(out, a):
+        run("v", [out], [a], lambda: g.vector.tensor_copy(out[0], a[0]))
+
+    def fill(out, x):
+        run("v", [out], [], lambda: g.vector.memset(out[0], x))
+
+    def scan(out, d0, d1, op0, op1):
+        run("v", [out], [d0, d1], lambda: g.vector.tensor_tensor_scan(out[0], d0[0], d1[0], 0.0, op0, op1))
+
+    def act(out, a, func, bias, scale=1.0):
+        run("s", [out], [a], lambda: g.scalar.activation(out[0], a[0], func, bias=bias, scale=scale))
+
+    def actcp(out, a):
+        run("s", [out], [a], lambda: g.scalar.activation(out[0], a[0], COPY))
+
+    def mm(out, l, r, start=True, stop=True):
+        run("t", [out], [l, r], lambda: g.tensor.matmul(out[0], l[0], r[0], start, stop))
+
+    dma("s", "dS", T["ST0"][:], T.st[:], [A("ST0")], [])
+    dma("y", "dX", T["X"][:, 0:W], T.x[:], [A("X", 0, W)], [])
+    dma("s", "dL", T["LND0"][:, 64:128], T.sp[:], [A("LND0", 64, 128)], [])
+    dma("s", "dC", T["LND0"][:, 0:64], T.ch[:], [A("LND0", 0, 64)], [])
+    dma("s", "dW", T["WT"][:], T.wt[:], [A("WT")], [])
+    dma("s", "dF", T["F0"][:], T.fl[:], [A("F0")], [])
+
+    def iota(out, pattern, cm):
+        run("g", [out], [], lambda: g.iota(out[0], pattern, 0, cm))
+    iota(A("PI"), [[1, 1]], 1)
+    iota(A("ROW"), [[1, 128]], 0)
+    iota(A("KQI"), [[4, 8], [0, 64]], 0)
+
+    def send(t_from, name_to, sem, dst):
+        rid, pid, _ = topo.addr(dst)
+        deps("g", [], [A(t_from)])
+        g.remote_dma(out_ap=T[name_to][:], in_ap=T[t_from][:], remote_sem=T.sem[sem], local_sem=T.sem.loc,
+                     pid=pid, routing_id=rid, dma_engine_mask=topo.mask(core, dst))
+        return len(topo.engines(core, dst))
+    out_total = 0
+    for t in range(1, RO):
+        out_total += send("ST0", "ST%d" % t, "st%d" % t, T.cores[(rank + t) % n])
+        landed("ST%d" % t, "st%d" % t, len(topo.engines(T.cores[(rank - t) % n], core)))
+
+    fill(A("Dm"), 0.0)
+    fill(A("Wm"), 0.0)
+    ts(A("QI"), A("PI"), 15, AND)
+    ts(A("GI"), A("PI"), 4, SHR)
+    cp(A("PC"), A("PI"))
+    cp(A("ROWF"), A("ROW"))
+    cp(A("QC"), A("QI"))
+    cp(A("GC"), A("GI"))
+    ts(A("CQI"), A("ROW"), 15, AND)
+    ts(A("CGI"), A("ROW"), 4, SHR)
+    cp(A("CQF"), A("CQI"))
+    cp(A("CGF"), A("CGI"))
+    ts(A("ID"), A("ROWF"), A("PC"), EQ)
+    ts(A("BO"), A("CGF"), A("GC"), EQ)
+    ts(A("EQ16"), A("ROWF", 0, 16), A("QC"), EQ)
+    ts(A("QC64"), A("QC"), 64.0, MUL)
+    ts(A("C16M"), A("QC"), -1.0, MUL, 16.0, ADD)
+    fill(A("L0"), 0.0)
+    fill(A("RT", 1024, RTW), 0.0)
+    ts(A("DP0", 0, 128, 2), A("ROWF", 0, 64), 0.0, MUL, A("EQ16", 0, 1), ADD)
+    cp(A("DP0", 1, 128, 2), A("ROWF", 0, 64))
+    ts(A("MC"), A("ROWF", 0, 8), -64.0, MUL, A("QC64"), ADD)
+    for q in range(16):
+        ts(A("GT", q * 128, q * 128 + 128), A("BO"), A("EQ16", q, q + 1), MUL)
+    ts(A("R0"), A("ID"), A("EQ16", 0, 1), MUL)
+    ts(A("PCL"), A("ROWF", 1, 5), -1.0, MUL, A("PC"), ADD)
+    ts(A("PCG"), A("ROWF", 1, 5), -1.0, MUL, A("QC"), ADD)
+    ts(A("PCG"), A("PCG"), 0.0, GE, 1000.0, MUL)
+    tt(A("PCL"), A("PCL"), A("PCG"), ADD)
+    for l in range(1, 5):
+        ts(A("shx"), A("ROWF"), 1000.0, ADD, A("PCL", l - 1, l), EQ)
+        tt(A("SH%d" % l), A("shx"), A("ID"), SUB)
+    for m in range(16):
+        actcp(A("Dm", m * 129, m * 128 + 128, 16), A("ID", m, 128, 16))
+    ts(A("WB8"), A("BO"), A("WT"), MUL, 8.0, MUL)
+    for m in range(16):
+        cp(A("Wm", m * 129, m * 128 + 128, 16), A("WB8", 0, 128, 16))
+    fill(A("LOG", 0, 64), 0.0)
+    fill(A("NEG"), -2048.0)
+    fill(A("ONE"), 1.0)
+    fill(A("X", W, DUMP), 0.0)
+
+    def late_constants(part):
+        if part == 0:
+            fill(A("Gm"), 0.0)
+        elif part == 1:
+            for m in range(16):
+                actcp(A("Gm", m * 129, m * 128 + 128, 16), A("BO", 0, 128, 16))
+            fill(A("MASK4"), 1.0)
+            fill(A("MASK4", 0, 1024, 4), 0.0)
+            fill(A("OHL", 0, 64), 0.0)
+            fill(A("VB", 1024, 1040), 0.0)
+            fill(A("MASK16"), 1.0)
+            fill(A("MASK16", 0, 128, 16), 0.0)
+            fill(A("M16F"), 1.0)
+            fill(A("M16F", 0, 64, 16), 0.0)
+            fill(A("ON16"), 0.0625)
+        else:
+            ts(A("WB1"), A("BO"), A("WT"), MUL)
+            ts(A("BO3"), A("BO"), 3.0 / 64, MUL)
+            ts(A("BO1"), A("BO"), 1.0 / 64, MUL)
+            ts(A("IN1"), A("ID"), -1.0, MUL)
+            ts(A("IN2"), A("ID"), -2.0, MUL)
+            ts(A("QN4"), A("QC"), -4.0, MUL)
+            ts(A("KQ"), A("KQI"), A("QN4"), ADD)
+            ts(A("DIAG"), A("CQF", 0, 64), A("QC"), EQ)
+            ts(A("OFXC"), A("ROWF", 0, 64), 127.0, MUL, -8192.0, ADD)
+            ts(A("I4"), A("ROWF", 0, 4), 16.0, MUL, A("QC"), ADD)
+            ts(A("BV4"), A("I4"), 16.0, MUL, 16.0, ADD)
+            ts(A("BX4"), A("I4"), 8192.0, ADD)
+
+    def zslot(k, i0, i1):
+        if k < 4:
+            return A("ZA", 64 * i0 + k, 64 * i1, 4)
+        if k < 7:
+            return A("ZB", 64 * i0 + k - 3, 64 * i1, 4)
+        return A("Z7", 16 * i0, 16 * i1)
+
+    def zcol(k, m):
+        if k < 4:
+            return A("ZA", 4 * m + k, 4096, 64)
+        if k < 7:
+            return A("ZB", 4 * m + k - 3, 4096, 64)
+        return A("Z7", m, 1024, 16)
+
+    def gz(eng, k, i0, i1):
+        eng(zslot(k, i0, i1), IND(A("X", 0, W), A("OFFZ", i0, i1)))
+
+    def gc(eng, k, i0, i1):
+        eng(A("CB", 16 * i0, 16 * i1), IND(A("RT", 64 * k, RTW), A("OFFC", i0, i1)))
+
+    def entries():
+        act(A("CBF"), A("psC", 0, 64), IDT, 262144.0, 64.0)
+        act(A("CA"), A("psC", 0, 64), IDT, 18.5, 0.125)
+
+    def cwrap():
+        for m in range(16):
+            mm(A("psC", 0, 64), A("Dm", m * 128, m * 128 + 128), A("CB", m, 1024, 16), m == 0, m == 15)
+        entries()
+
+    def uwrap(k):
+        mm(A("psW", 0, 64), A("NEG"), A("ONE"), True, False)
+        for m in range(16):
+            mm(A("psW", 0, 64), A("Wm", m * 128, m * 128 + 128), zcol(k, m), False, m == 15)
+
+    def scan1(q):
+        scan(A("OA", 1024 * q, 1024 * q + 1024), A("MASK4"), A("ZA", 1024 * q, 1024 * q + 1024), MUL, MAX)
+
+    def scan1copy(q):
+        actcp(A("ZB", 1024 * q, 1024 * q + 1024, 4), A("OA", 1024 * q + 3, 1024 * q + 1024, 4))
+
+    def scan2(q):
+        scan(A("OB", 1024 * q, 1024 * q + 1024), A("MASK4"), A("ZB", 1024 * q, 1024 * q + 1024), MUL, MAX)
+
+    def arith(k):
+        old, nx = "DP%d" % k, "DP%d" % (k + 1)
+        tt(A("I1"), A("psW", 0, 64), A("CBF"), ADD)
+        if k == 7:
+            ts(A("N64"), A("I1"), 192, AND)
+            tt(A("LOG", 512, 576), A("LOG", 448, 512), A("N64"), ADD)
+            return
+        tt(A("psA", 0, 64), A("psW", 0, 64), A("CA"), MUL)
+        ts(A("N64"), A("I1"), 192, AND)
+        ts(A("DH"), A("I1"), 4, SHR)
+        tt(A(nx, 1, 128, 2), A(old, 1, 128, 2), A("N64"), ADD)
+        tt(A("YI"), A("psA", 0, 64), A("DH"), ADD)
+        ts(A(nx, 0, 128, 2), A(nx, 1, 128, 2), A("MC", k + 1, k + 2), GE)
+        scan(A("QS"), A("L0"), A(nx), MUL, ADD)
+        ts(A("SI"), A("YI"), 2, SHR, W - 1, AND)
+        cp(A("OFFC"), A("QS", 1, 128, 2))
+        cp(A("OFFZ"), A("SI"))
+
+    def log(k):
+        tt(A("LOG", 64 * (k + 1), 64 * (k + 2)), A("LOG", 64 * k, 64 * (k + 1)), A("N64"), ADD)
+
+    ysn = [0]
+
+    def ysum(cnt):
+        for _ in range(cnt):
+            c = ysn[0]
+            mm(A("psY", 0, 64), A("ID"), A("X", c, W, 128), c == 0, False)
+            ysn[0] += 1
+
+    for t in range(RO):
+        last = t == RO - 1
+        lnd, snd, F = "LND%d" % t, "SND%d" % t, "F%d" % t
+        C, L = A(lnd, 0, 64), A(lnd, 64, 128)
+        for l in range(1, 5):
+            mm(A("psF1", l * 64 - 64, l * 64), A("SH%d" % l), C)
+        for q in range(16):
+            mm(A("psA" if q < 8 else "psB", (q % 8) * 64, (q % 8) * 64 + 64), A("GT", q * 128, q * 128 + 128), C)
+        ts(A("T613"), L, 613.0, MUL)
+        tt(A("S0"), A("T613"), A("SA" if t else "ST0"), ADD)
+        ts(A("SI"), A("S0"), W - 1, AND)
+        cp(A("OFFZ"), A("SI"))
+        gz(actcp, 0, 0, Z0_SCALAR)
+        for l in range(1, 5):
+            ts(A("MK", l * 64 - 64, l * 64), L, float(l), EQ)
+        tt(A("CM"), A("MK"), A("psF1", 0, 256), MUL)
+        mm(A("psC", 0, 64), A("GT", 0, 128), C, True, False)
+        for l in range(1, 5):
+            mm(A("psC", 0, 64), A("R0"), A("CM", l * 64 - 64, l * 64), False, l == 4)
+        entries()
+        actcp(A("RT", 0, 512), A("psA"))
+        actcp(A("RT", 512, 1024), A("psB"))
+        gz(cp, 0, Z0_SCALAR, 64)
+        ts(A("L0", 1, 128, 2), L, 64.0, MUL)
+        uwrap(0)
+        if t == 0:
+            late_constants(0)
+        for m in range(16):
+            for h in range(2):
+                mm(A("psF%d" % h, m, 512, 16), A("ID"), A(F, 32 * h, 32 * h + 32))
+        ts(A("PRI"), L, 32.0, MUL, A("C16M"), ADD)
+        ts(A("LM15"), L, 15.0, ADD)
+        arith(0)
+        for k in range(1, 7):
+            gc(actcp, k, 0, C_SCALAR)
+            gc(cp, k, C_SCALAR, 64)
+            gz(actcp, k, 0, Z_SCALAR)
+            gz(cp, k, Z_SCALAR, 64)
+            log(k - 1)
+            cwrap()
+            uwrap(k)
+            if last:
+                ysum(21)
+            if k == 3:
+                scan1(0)
+            elif k == 4:
+                scan1(1)
+                scan1(2)
+                scan1copy(0)
+            elif k == 5:
+                scan1(3)
+                scan1copy(1)
+                scan1copy(2)
+                scan1copy(3)
+            elif k == 6:
+                scan2(0)
+            elif t == 0:
+                late_constants(k)
+            arith(k)
+        gc(actcp, 7, 0, 64)
+        gz(actcp, 7, 0, 64)
+        for q in range(1, 4):
+            scan2(q)
+        log(6)
+        cwrap()
+        uwrap(7)
+        if last:
+            ysum(128 - ysn[0])
+        for h in range(2):
+            o, i = 512 * h, A("OFFZ", 32 * h, 32 * h + 32)
+            tt(A("VB", o, o + 512), IND(A("X", 0, W), i), A("OB", 4 * o + 3, 4 * o + 2048, 4), MAX)
+        for h in range(2):
+            o = 512 * h
+            tt(A("GEb", o, o + 512), A("VB", o, o + 512), A("psF%d" % h), GE)
+        arith(7)
+        for m in range(16):
+            mm(A("psA", 0, 64), A("Gm", m * 128, m * 128 + 128), A("GEb", m, 1024, 16), m == 0, m == 15)
+        for l in range(1, 5):
+            mm(A("psF0", l * 64 - 64, l * 64), A("SH%d" % l), C)
+        ts(A("FT"), A("psA", 0, 64), 9.5, GE)
+        tt(A("SC"), A("FT"), A("PRI"), MUL)
+        run("t", [A("psT", 0, 128)], [A("SC"), A("ID")],
+            lambda: g.tensor.transpose(T["psT"][0:64, 0:128], T["SC"][:, 0:64], T["ID"][:]))
+        scan(A("SX", 0, 128, 1, 64), A("MASK16", 0, 128, 1, 64), A("psT", 0, 128, 1, 64), MUL, MAX)
+        mm(A("psC", 0, 64), A("SX", 0, 128, 1, 64), A("ID", 0, 64, 1, 64))
+        cp(A("PX"), A("psC", 0, 64))
+        mm(A("psW", 0, 64), A("GT", 15 * 128, 16 * 128), A("PX"))
+        tt(A("psA", 0, 64), A("SC"), A("psW", 0, 64), EQ)
+        cp(A("BI"), A("psW", 0, 64))
+        for h, ps in ((0, "psB"), (1, "psC")):
+            o = 256 * h
+            mm(A(ps, 0, 256), A("ID"), A("KQ", o, o + 256), True, False)
+            for k in range(4 * h + 1, 4 * h + 5):
+                tt(A("OHL", 64 * k, 64 * k + 64), A("LOG", 64 * k, 64 * k + 64), A("psA", 0, 64), MUL)
+            mm(A(ps, 0, 256), A("BO3"), A("OHL", o, o + 256), False, False)
+            mm(A(ps, 0, 256), A("BO1"), A("OHL", o + 64, o + 320), False, True)
+        ts(A("MI"), A("BI"), 31, AND)
+        ts(A("LI"), A("BI"), 5, SHR)
+        ts(A("AT", 0, 256), A("psB", 0, 256), 0.0, MAX, 4.0, MIN)
+        act(A("SG", 256, 512), A("psC", 0, 256), SIGN, -3.5)
+        act(A("SG", 0, 256), A("psB", 0, 256), SIGN, -3.5)
+        ts(A("OK"), A("psW", 0, 64), 0.5, GE)
+        ts(A("GG"), A("MI"), A("C16M"), GE)
+        ts(A("AT", 256, 512), A("psC", 0, 256), 0.0, MAX, 4.0, MIN)
+        tt(A("LE"), A("GG"), A("LI"), MUL)
+        mm(A("psW", 0, 64), A("IN1"), A("LM15"), True, False)
+        for name, lhs, k0 in (("AT", "ID", 0), ("SG", "IN2", 4), ("SG", "IN2", 0), ("AT", "ID", 4)):
+            for k in range(k0, k0 + 4):
+                mm(A("psW", 0, 64), A(lhs), A(name, 64 * k, 64 * k + 64), False, (name, k) == ("AT", 7))
+        for l in range(1, 5):
+            ts(A("MK", l * 64 - 64, l * 64), A("LE"), float(l), EQ)
+        tt(A("CM"), A("MK"), A("psF0", 0, 256), MUL)
+        mm(A("psF1", 0, 64), A("ID"), C, True, False)
+        for l in range(1, 5):
+            mm(A("psF1", 0, 64), A("ID"), A("CM", l * 64 - 64, l * 64), False, l == 4)
+        tt(A("DL"), A("psW", 0, 64), A("OK"), MUL)
+        tt(A(snd, 64, 128), A("DL"), L, ADD)
+        actcp(A(snd, 0, 64), A("psF1", 0, 64))
+        if not last:
+            out_total += send(snd, "LND%d" % (t + 1), "arr%d" % (t + 1), T.cores[(rank + 1) % n])
+            landed("LND%d" % (t + 1), "arr%d" % (t + 1), len(topo.engines(T.cores[(rank - 1) % n], core)))
+            mm(A("psA", 0, 64), A("ON16"), A("OK"))
+        else:
+            dma("y", "oL", T.yl[:], T[snd][:, 64:128], [], [A(snd, 64, 128)])
+            dma("y", "oC", T.yc[:], T[snd][:, 0:64], [], [A(snd, 0, 64)])
+        tt(A("MD"), A("MI"), A("DIAG"), MUL)
+        scan(A("SD"), A("M16F"), A("MD"), MUL, ADD)
+        tt(A("OKD"), A("OK"), A("DIAG"), MUL)
+        tt(A("O4"), A("BV4"), A("SD", 15, 64, 16), SUB)
+        cp(A("OV"), A("O4"))
+        cp(A("VV"), IND(A("VB"), A("OV")))
+        mm(A("psC", 0, 64), A("WB1"), A("VV"))
+        tt(A("FVI"), A(F), A("VV"), ADD)
+        cp(A("HI"), A("psC", 0, 64))
+        ts(A("FH"), A("FVI"), 1, SHR)
+        ts(A("HM"), A("HI"), 127, AND)
+        tt(A("FD"), A("FH"), A(F), SUB)
+        tt(A("X1"), A("HM"), A("OFXC"), ADD)
+        tt(A("FE"), A("FD"), A("OK"), MUL)
+        tt(A("X2"), A("X1"), A("OKD"), MUL)
+        tt(A("F%d" % (t + 1)), A(F), A("FE"), ADD)
+        scan(A("SD2"), A("M16F"), A("X2"), MUL, ADD)
+        tt(A("O4X"), A("BX4"), A("SD2", 15, 64, 16), ADD)
+        cp(A("OX"), A("O4X"))
+        if not last:
+            run("v", [A("ACOL")], [A("psA", 0, 64)],
+                lambda: g.vector.tensor_reduce(T["ACOL"][:], T["psA"][:, 0:64], AxisListType.X, ADD))
+            cp(IND(A("X"), A("OX")), A("VV"))
+            ts(A("SA"), A("ST%d" % (t + 1)), A("ACOL"), ADD)
+        else:
+            cp(A("OLD"), IND(A("X"), A("OX")))
+            tt(A("PR"), A("VV"), A("OLD"), SUB)
+            tt(A("DIF"), A("PR"), A("OK"), MUL)
+            mm(A("psY", 0, 64), A("ID"), A("DIF"), False, True)
+            cp(A("YS"), A("psY", 0, 64))
+            dma("y", "oF", T.yf[:], T["F4"][:], [], [A("F4")])
+            dma("y", "oS", T.ys[:], T["YS"][:], [], [A("YS")])
+
+    for q in "vstg":
+        wait("g", "q" + q, count[q])
+    for s in ("dX", "dW", "dC", "dL", "dS", "dF", "oL", "oC", "oF", "oS"):
+        wait("g", s, 16)
+    wait("g", "loc", out_total)
+    for t in range(1, RO):
+        wait("g", "st%d" % t, len(topo.engines(T.cores[(rank - t) % n], core)))
+        wait("g", "arr%d" % t, len(topo.engines(T.cores[(rank - 1) % n], core)))

@@ -1,13 +1,13 @@
+import math
 from concourse.mybir import dt, AluOpType, AxisListType, ActivationFunctionType
 
 ADD, SUB, MUL, MAX, MIN = AluOpType.add, AluOpType.subtract, AluOpType.mult, AluOpType.max, AluOpType.min
-GE, EQ = AluOpType.is_ge, AluOpType.is_equal
+GE, EQ, LT, LE, GT = AluOpType.is_ge, AluOpType.is_equal, AluOpType.is_lt, AluOpType.is_le, AluOpType.is_gt
 SHR, AND = AluOpType.arith_shift_right, AluOpType.bitwise_and
-IDT, SIGN = ActivationFunctionType.Identity, ActivationFunctionType.Sign
-COPY = ActivationFunctionType.Copy
+IDT, SIGN, ABS = ActivationFunctionType.Identity, ActivationFunctionType.Sign, ActivationFunctionType.Abs
+COPY, EXP = ActivationFunctionType.Copy, ActivationFunctionType.Exp
 RO, S, W = 4, 8, 8192
-DUMP = W + 64
-RTW = 33 * 64
+BIG = 1024.0
 
 SCRATCH = {}
 POOL = {}
@@ -24,46 +24,45 @@ def _pool(buf, names, cols, dtype):
     SCRATCH[buf] = ("sbuf", [128, len(names.split()) * cols], dtype)
 
 
-_d("X", DUMP, "bfloat16")
-_d("ZA OA ZB OB", 4096, "bfloat16")
-_d("Z7 CB GEb", 1024, "bfloat16")
-_d("VB", 1040, "bfloat16")
-_d("RT", RTW, "bfloat16")
-_d("Gm Dm Wm GT", 2048, "bfloat16")
-_d("ID BO BO3 BO1 WB8 WB1 SH1 SH2 SH3 SH4 IN1 IN2 R0 NEG ON16 shx", 128, "bfloat16")
-_d("ONE SC PX OK VV OLD DIF LM15", 64, "bfloat16")
-_d("MASK4", 1024, "bfloat16")
-_d("MASK16 SX", 128, "bfloat16")
-_d("LOG OHL", 576, "bfloat16")
-_d("KQ AT SG", 512, "bfloat16")
-_d("MK CM", 256, "bfloat16")
+_d("X", 2 * W, "bfloat16")
+_d("G0 G1 O0 O1", 3072, "bfloat16")
+_d("G2 O2 D2 Z7", 4096, "bfloat16")
+_d("GEb", 1024, "bfloat16")
+_d("M3", 768, "bfloat16")
+_d("Gm Wm", 2048, "bfloat16")
+_d("TL", 15 * 128, "bfloat16")
+_pool("MATS", "ID BO BO3 BO1 BON WB1 SH1 SH2 SH3 SH4 C01 C02 C03 C04 R0N GT8 NEG ONS H9 H1 I256 ALF TRI MV NID "
+              "tm0 tm1 tm2 tm3 TH2 WD WO L0 QS DP0 DP1 DP2 DP3 DP4 DP5 DP6 DP7", 128, "bfloat16")
+_pool("HMATS", "P64 N64 P32 N32", 128, "float16")
+_pool("SMALL", "ONE SP0 NF EE PRE VV6 VV OLD DIF DG DGX KX YL", 64, "bfloat16")
+_d("UA UB UO", 576, "float16")
+_d("DA DB DO", 512, "float16")
+_d("LG LM OHL", 640, "bfloat16")
+_d("AS AO M8", 512, "bfloat16")
+_d("K5 M5 AL ALO", 320, "bfloat16")
+_d("K0 M4 A0 A0O", 256, "bfloat16")
 _d("F0 F1 F2 F3 F4", 64, "bfloat16")
 _d("LND0 LND1 LND2 LND3 SND0 SND1 SND2 SND3", 128, "bfloat16")
 _d("WT", 1, "bfloat16")
 _d("ST0 ST1 ST2 ST3", 64, "int32")
-_pool("INTS", "SA I1 N64 DH YI SI T613 S0 BI LI MI HI HM FVI FH", 64, "int32")
+_pool("INTS", "N4 DH YI SI T613 S0 HI HM FVI FH", 64, "int32")
 _d("ROW CQI CGI", 128, "int32")
-_d("KQI", 512, "int32")
 _d("PI QI GI", 1, "int32")
 _d("ROWF CQF CGF", 128, "float32")
-_d("PC QC GC QC64 QN4 C16M ACOL", 1, "float32")
+_d("PC QC GC QB MW ACOL", 1, "float32")
 _d("PCL PCG", 4, "float32")
-_d("EQ16", 16, "float32")
+_d("EQ16 COEF", 32, "float32")
 _d("MC", 8, "float32")
-_pool("FLTS", "CA CBF PR M16F DIAG OFXC PRI FT GG LE DL MD SD X1 OKD X2 SD2 FD FE", 64, "float32")
-_d("I4 BV4 BX4 O4 O4X", 4, "float32")
-_d("L0 QS", 128, "float32")
-_d("DP0 DP1 DP2 DP3 DP4 DP5 DP6 DP7", 128, "float32")
+_pool("FLTS", "CA CB4 PR M16F DIAG SD X1 SD2", 64, "float32")
 _d("YS", 64, "float32")
-_d("OFFZ OFFC", 64, "uint16")
+_d("OFFZ", 64, "uint16")
 _d("OV OX", 4, "uint16")
-_d("psF0 psF1 psW psC psA psB psY", 512, "float32", "psum")
-_d("psT", 1024, "bfloat16", "psum")
+_d("psW psC psP ps3 ps4 ps5 ps6 psY", 512, "float32", "psum")
 
 SEMAPHORES = ["qv", "qs", "qt", "qg", "dX", "dW", "dC", "dL", "dS", "dF", "oC", "oL", "oF", "oS", "loc"]
 SEMAPHORES += ["st%d" % t for t in range(1, RO)] + ["arr%d" % t for t in range(1, RO)]
 
-C_SCALAR, Z_SCALAR, Z0_SCALAR = 38, 26, 38
+Z_SCALAR = [32, 36, 48, 48, 48, 48, 48, 62]
 
 
 class Ap(tuple):
@@ -81,12 +80,12 @@ def rank_program(g, core, T, topo):
     snap = {}
     seen = {}
 
-    def A(name, a=None, b=None, step=1, p=128):
+    def A(name, a=None, b=None, step=1):
         buf, off, cols = POOL[name] if name in POOL else (name, 0, SCRATCH[name][1][1])
         a = 0 if a is None else a
         b = cols if b is None else b
-        ap = T[buf][0:p, off + a:off + b] if step == 1 else T[buf][0:p, off + a:off + b:step]
-        return Ap((ap, ((name, a, b),)))
+        ap = T[buf][:, off + a:off + b] if step == 1 else T[buf][:, off + a:off + b:step]
+        return Ap((ap, ((name, a, b, step),)))
 
     def IND(win, off):
         return Ap((win[0].indirect(off[0]), win[1] + off[1]))
@@ -104,18 +103,18 @@ def rank_program(g, core, T, topo):
         need = {}
         for w, group in ((True, outs), (False, ins)):
             for x in group:
-                for name, lo, hi in x[1]:
+                for name, lo, hi, step in x[1]:
                     ps = name.startswith("ps")
                     for a in seen.get(name, ()):
-                        apart = a[0] >= hi or a[1] <= lo
+                        apart = a[0] >= hi or a[1] <= lo or (a[0] - lo) % math.gcd(a[2], step) != 0
                         if apart and not ps:
                             continue
-                        if a[3] == q:
-                            if q == "t" or apart or not (w or a[2]):
+                        if a[4] == q:
+                            if q == "t" or apart or not (w or a[3]):
                                 continue
-                        elif not ps and not (w or a[2]):
+                        elif not ps and not (w or a[3]):
                             continue
-                        need[a[4]] = max(need.get(a[4], 0), a[5])
+                        need[a[5]] = max(need.get(a[5], 0), a[6])
         for s in sorted(need):
             wait(q, s, need[s])
 
@@ -123,13 +122,14 @@ def rank_program(g, core, T, topo):
         k = known.get(q, {})
         for w, group in ((False, ins), (True, outs)):
             for x in group:
-                for name, lo, hi in x[1]:
+                for name, lo, hi, step in x[1]:
                     lst = seen.setdefault(name, [])
                     if w:
-                        lst[:] = [a for a in lst if not (lo <= a[0] and a[1] <= hi and k.get(a[4], 0) >= a[5])]
-                    else:
-                        lst[:] = [a for a in lst if not (a[3] == q and not a[2] and (a[0], a[1]) == (lo, hi))]
-                    lst.append([lo, hi, w, q, sem, val])
+                        lst[:] = [a for a in lst if not (
+                            lo <= a[0] and a[1] <= hi and a[2] % step == 0 and (a[0] - lo) % step == 0
+                            and k.get(a[5], 0) >= a[6])]
+                    lst[:] = [a for a in lst if not (a[4] == q and a[3] == w and a[:3] == [lo, hi, step])]
+                    lst.append([lo, hi, step, w, q, sem, val])
 
     def run(q, outs, ins, call):
         deps(q, outs, ins)
@@ -172,8 +172,14 @@ def rank_program(g, core, T, topo):
     def scan(out, d0, d1, op0, op1):
         run("v", [out], [d0, d1], lambda: g.vector.tensor_tensor_scan(out[0], d0[0], d1[0], 0.0, op0, op1))
 
-    def act(out, a, func, bias, scale=1.0):
-        run("s", [out], [a], lambda: g.scalar.activation(out[0], a[0], func, bias=bias, scale=scale))
+    def act(out, a, func, bias=0.0, scale=1.0, acc=None):
+        b = bias[0] if isap(bias) else bias
+        ins = [a] + ([bias] if isap(bias) else [])
+        if acc is None:
+            run("s", [out], ins, lambda: g.scalar.activation(out[0], a[0], func, bias=b, scale=scale))
+        else:
+            run("s", [out, acc], ins,
+                lambda: g.scalar.activation(out[0], a[0], func, bias=b, scale=scale, accum_out=acc[0]))
 
     def actcp(out, a):
         run("s", [out], [a], lambda: g.scalar.activation(out[0], a[0], COPY))
@@ -181,18 +187,26 @@ def rank_program(g, core, T, topo):
     def mm(out, l, r, start=True, stop=True):
         run("t", [out], [l, r], lambda: g.tensor.matmul(out[0], l[0], r[0], start, stop))
 
-    dma("s", "dS", T["ST0"][:], T.st[:], [A("ST0")], [])
+    def iota(out, pattern, cm, base=0):
+        small = SCRATCH[POOL[out[1][0][0]][0] if out[1][0][0] in POOL else out[1][0][0]][2] != "int32"
+        if small:
+            run("g", [out], [], lambda: g.iota(out[0], pattern, base, cm, allow_small_or_imprecise_dtypes=True))
+        else:
+            run("g", [out], [], lambda: g.iota(out[0], pattern, base, cm))
+
+    def gcp(out, a, cols):
+        run("g", [out], [a], lambda: g.affine_select(out[0], a[0], [[0, cols]], GE, 0.0, 0, 0))
+
     dma("y", "dX", T["X"][:, 0:W], T.x[:], [A("X", 0, W)], [])
-    dma("s", "dL", T["LND0"][:, 64:128], T.sp[:], [A("LND0", 64, 128)], [])
+    dma("s", "dS", T["ST0"][:], T.st[:], [A("ST0")], [])
+    dma("s", "dL", A("SP0")[0], T.sp[:], [A("SP0")], [])
     dma("s", "dC", T["LND0"][:, 0:64], T.ch[:], [A("LND0", 0, 64)], [])
     dma("s", "dW", T["WT"][:], T.wt[:], [A("WT")], [])
     dma("s", "dF", T["F0"][:], T.fl[:], [A("F0")], [])
 
-    def iota(out, pattern, cm):
-        run("g", [out], [], lambda: g.iota(out[0], pattern, 0, cm))
     iota(A("PI"), [[1, 1]], 1)
     iota(A("ROW"), [[1, 128]], 0)
-    iota(A("KQI"), [[4, 8], [0, 64]], 0)
+    iota(A("K0"), [[0, 64], [-256, 4]], 0, 768)
 
     def send(t_from, name_to, sem, dst):
         rid, pid, _ = topo.addr(dst)
@@ -204,9 +218,13 @@ def rank_program(g, core, T, topo):
     for t in range(1, RO):
         out_total += send("ST0", "ST%d" % t, "st%d" % t, T.cores[(rank + t) % n])
         landed("ST%d" % t, "st%d" % t, len(topo.engines(T.cores[(rank - t) % n], core)))
+    iota(A("K5"), [[0, 64], [-256, 5]], 0)
+    iota(A("D2", 0, 4096, 4), [[0, 1024]], 0, -1024)
+    iota(A("D2", 1, 4096, 4), [[0, 1024]], 0)
+    iota(A("D2", 2, 4096, 4), [[0, 1024]], 0)
+    iota(A("G2", 3, 4096, 4), [[0, 1024]], 0, -1)
 
-    fill(A("Dm"), 0.0)
-    fill(A("Wm"), 0.0)
+    fill(A("Gm"), 0.0)
     ts(A("QI"), A("PI"), 15, AND)
     ts(A("GI"), A("PI"), 4, SHR)
     cp(A("PC"), A("PI"))
@@ -217,293 +235,314 @@ def rank_program(g, core, T, topo):
     ts(A("CGI"), A("ROW"), 4, SHR)
     cp(A("CQF"), A("CQI"))
     cp(A("CGF"), A("CGI"))
-    ts(A("ID"), A("ROWF"), A("PC"), EQ)
     ts(A("BO"), A("CGF"), A("GC"), EQ)
-    ts(A("EQ16"), A("ROWF", 0, 16), A("QC"), EQ)
-    ts(A("QC64"), A("QC"), 64.0, MUL)
-    ts(A("C16M"), A("QC"), -1.0, MUL, 16.0, ADD)
-    fill(A("L0"), 0.0)
-    fill(A("RT", 1024, RTW), 0.0)
-    ts(A("DP0", 0, 128, 2), A("ROWF", 0, 64), 0.0, MUL, A("EQ16", 0, 1), ADD)
-    cp(A("DP0", 1, 128, 2), A("ROWF", 0, 64))
-    ts(A("MC"), A("ROWF", 0, 8), -64.0, MUL, A("QC64"), ADD)
-    for q in range(16):
-        ts(A("GT", q * 128, q * 128 + 128), A("BO"), A("EQ16", q, q + 1), MUL)
-    ts(A("R0"), A("ID"), A("EQ16", 0, 1), MUL)
-    ts(A("PCL"), A("ROWF", 1, 5), -1.0, MUL, A("PC"), ADD)
-    ts(A("PCG"), A("ROWF", 1, 5), -1.0, MUL, A("QC"), ADD)
-    ts(A("PCG"), A("PCG"), 0.0, GE, 1000.0, MUL)
-    tt(A("PCL"), A("PCL"), A("PCG"), ADD)
-    for l in range(1, 5):
-        ts(A("shx"), A("ROWF"), 1000.0, ADD, A("PCL", l - 1, l), EQ)
-        tt(A("SH%d" % l), A("shx"), A("ID"), SUB)
+    ts(A("ID"), A("ROWF"), A("PC"), EQ)
+    ts(A("EQ16"), A("ROWF", 0, 32), A("QC"), EQ)
     for m in range(16):
-        actcp(A("Dm", m * 129, m * 128 + 128, 16), A("ID", m, 128, 16))
-    ts(A("WB8"), A("BO"), A("WT"), MUL, 8.0, MUL)
-    for m in range(16):
-        cp(A("Wm", m * 129, m * 128 + 128, 16), A("WB8", 0, 128, 16))
-    fill(A("LOG", 0, 64), 0.0)
-    fill(A("NEG"), -2048.0)
+        act(A("Gm", m * 129, m * 128 + 128, 16), A("BO", 0, 128, 16), IDT, 0.0, 65536.0)
+    fill(A("NEG"), -128.0)
     fill(A("ONE"), 1.0)
-    fill(A("X", W, DUMP), 0.0)
+    fill(A("L0"), 0.0)
+    fill(A("DP0"), 0.0)
+    for name in ("UB", "DB"):
+        fill(A(name), 0.0)
+    fill(A("M4"), 0.0)
+    fill(A("M4", 0, 256, 4), BIG)
+    ts(A("MC"), A("ROWF", 0, 8), -1.0, MUL, A("QC"), ADD)
+    ts(A("MC"), A("MC"), 4.0, MUL)
+    ts(A("tm0"), A("CQF"), 0.0, EQ)
+    tt(A("tm1"), A("tm0"), A("BO"), MUL)
+    tt(A("tm2"), A("BO"), A("tm1"), SUB)
+    ts(A("tm2"), A("tm2"), A("EQ16", 0, 1), MUL)
+    for l in range(1, 5):
+        ts(A("tm3"), A("tm1"), A("EQ16", l, l + 1), MUL)
+        tt(A("C0%d" % l), A("tm3"), A("tm2"), ADD)
+    ts(A("R0N"), A("ID"), A("EQ16", 0, 1), MUL, -256.0, MUL)
+    ts(A("K0"), A("K0"), A("EQ16", 0, 1), MUL)
+    tt(A("COEF", 0, 1), A("EQ16", 8, 9), A("EQ16", 7, 8), SUB)
+    tt(A("COEF", 7, 8), A("EQ16", 9, 10), A("EQ16", 8, 9), SUB)
+    for j in range(2, 8):
+        tt(A("COEF", j - 1, j), A("EQ16", 10 - j, 11 - j), A("EQ16", 8 - j, 9 - j), SUB)
+    tt(A("COEF", 8, 15), A("EQ16", 10, 17), A("EQ16", 8, 15), SUB)
+
+    def stair(k):
+        t = k if k < 7 else k - 7
+        ts(A("TL", 128 * k, 128 * k + 128), A("BO"), A("COEF", k, k + 1), MUL, (1.0 if t % 2 == 0 else -1.0) / 64, MUL)
+    for k in range(15):
+        stair(k)
+    ts(A("GT8"), A("BO"), A("EQ16", 8, 9), MUL)
+    for name, x in (("P64", 64.0), ("N64", -64.0), ("P32", 32.0), ("N32", -32.0), ("H9", 2.25), ("H1", -0.25)):
+        ts(A(name), A("ID"), x, MUL)
+    ts(A("LND0", 64, 128), A("SP0"), -1.0, MUL, 4.0, ADD)
+    ts(A("Wm"), A("Gm"), A("WT"), MUL, 0.5 / 65536, MUL)
+    fill(A("ACOL"), 4.0 * 613)
+    for h in range(2):
+        act(A("Z7", 2048 * h, 2048 * h + 2048), A("Gm"), IDT, 0.0, 0.0)
 
     def late_constants(part):
         if part == 0:
-            fill(A("Gm"), 0.0)
+            fill(A("M3"), 1.0)
+            fill(A("M3", 0, 768, 3), 0.0)
+            for name, cols, step in (("M8", 512, 8), ("M5", 320, 5), ("LM", 640, 10)):
+                fill(A(name), 0.0)
+                fill(A(name, 0, cols, step), BIG)
         elif part == 1:
-            for m in range(16):
-                actcp(A("Gm", m * 129, m * 128 + 128, 16), A("BO", 0, 128, 16))
-            fill(A("MASK4"), 1.0)
-            fill(A("MASK4", 0, 1024, 4), 0.0)
-            fill(A("OHL", 0, 64), 0.0)
-            fill(A("VB", 1024, 1040), 0.0)
-            fill(A("MASK16"), 1.0)
-            fill(A("MASK16", 0, 128, 16), 0.0)
             fill(A("M16F"), 1.0)
             fill(A("M16F", 0, 64, 16), 0.0)
-            fill(A("ON16"), 0.0625)
-        else:
+            fill(A("ONS"), 1.0 / 256)
+            fill(A("WD", 0, 128, 2), -4194304.0)
+            fill(A("TH2"), 0.0)
+            fill(A("TH2", 0, 64, 2), -768.0)
+            fill(A("TH2", 64, 128, 2), -384.0)
+            fill(A("KX"), 16.0)
+            ts(A("NID"), A("ID"), -1.0, MUL)
+            ts(A("I256"), A("ID"), 256.0, MUL)
+            ts(A("QB"), A("QC"), -8.0, MUL, -16.0, ADD)
+            ts(A("MW"), A("QC"), 4.0 / 256, MUL, 2.0 / 256, ADD)
+        elif part == 2:
+            ts(A("PCL"), A("ROWF", 1, 5), -1.0, MUL, A("PC"), ADD)
+            ts(A("PCG"), A("ROWF", 1, 5), -1.0, MUL, A("QC"), ADD)
+            ts(A("PCG"), A("PCG"), 0.0, GE, 1000.0, MUL)
+            tt(A("PCL"), A("PCL"), A("PCG"), ADD)
+            for l in range(1, 5):
+                ts(A("SH%d" % l), A("ROWF"), 1000.0, ADD, A("PCL", l - 1, l), EQ)
             ts(A("WB1"), A("BO"), A("WT"), MUL)
-            ts(A("BO3"), A("BO"), 3.0 / 64, MUL)
-            ts(A("BO1"), A("BO"), 1.0 / 64, MUL)
-            ts(A("IN1"), A("ID"), -1.0, MUL)
-            ts(A("IN2"), A("ID"), -2.0, MUL)
-            ts(A("QN4"), A("QC"), -4.0, MUL)
-            ts(A("KQ"), A("KQI"), A("QN4"), ADD)
+            ts(A("BO3"), A("BO"), 3.0 / 256, MUL)
+            ts(A("BO1"), A("BO"), 1.0 / 256, MUL)
+            ts(A("BON"), A("BO"), -32.0, MUL)
+            ts(A("MV"), A("BO"), A("MW"), MUL)
+        elif part == 3:
+            ts(A("tm0"), A("CQF"), A("QC"), GE, 256.0, MUL)
+            tt(A("TRI"), A("tm0"), A("BO"), MUL)
+            ts(A("tm1"), A("CQF"), A("QC"), GT, 15.0 / 16, MUL)
+            ts(A("tm1"), A("tm1"), 1.0 / 16, ADD)
+            ts(A("tm2"), A("ID"), -33.0 / 32, MUL)
+            tt(A("tm3"), A("tm1"), A("BO"), MUL)
+            tt(A("ALF"), A("tm3"), A("tm2"), ADD)
+        elif part == 4:
             ts(A("DIAG"), A("CQF", 0, 64), A("QC"), EQ)
-            ts(A("OFXC"), A("ROWF", 0, 64), 127.0, MUL, -8192.0, ADD)
-            ts(A("I4"), A("ROWF", 0, 4), 16.0, MUL, A("QC"), ADD)
-            ts(A("BV4"), A("I4"), 16.0, MUL, 16.0, ADD)
-            ts(A("BX4"), A("I4"), 8192.0, ADD)
+            ts(A("X1"), A("ROWF", 0, 64), 64.0, MUL, 32768.0, ADD)
+            tt(A("X1"), A("X1"), A("DIAG"), MUL)
+            ts(A("DG"), A("X1"), -32768.0, ADD)
+            ts(A("SD"), A("ROWF", 0, 64), 128.0, MUL, 8192.0 + 32768.0, ADD)
+            tt(A("SD"), A("SD"), A("DIAG"), MUL)
+            ts(A("DGX"), A("SD"), -32768.0, ADD)
 
-    def zslot(k, i0, i1):
-        if k < 4:
-            return A("ZA", 64 * i0 + k, 64 * i1, 4)
-        if k < 7:
-            return A("ZB", 64 * i0 + k - 3, 64 * i1, 4)
-        return A("Z7", 16 * i0, 16 * i1)
-
-    def zcol(k, m):
-        if k < 4:
-            return A("ZA", 4 * m + k, 4096, 64)
-        if k < 7:
-            return A("ZB", 4 * m + k - 3, 4096, 64)
-        return A("Z7", m, 1024, 16)
+    ZAT = [("G0", 3, 0), ("G0", 3, 1), ("G0", 3, 2), ("G1", 3, 1), ("G1", 3, 2), ("G2", 4, 1), ("G2", 4, 2),
+           ("Z7", 4, 2)]
 
     def gz(eng, k, i0, i1):
-        eng(zslot(k, i0, i1), IND(A("X", 0, W), A("OFFZ", i0, i1)))
+        if i0 < i1:
+            b, s, o = ZAT[k]
+            eng(A(b, 16 * s * i0 + o, 16 * s * i1, s), IND(A("X", 0, W), A("OFFZ", i0, i1)))
 
-    def gc(eng, k, i0, i1):
-        eng(A("CB", 16 * i0, 16 * i1), IND(A("RT", 64 * k, RTW), A("OFFC", i0, i1)))
-
-    def entries():
-        act(A("CBF"), A("psC", 0, 64), IDT, 262144.0, 64.0)
-        act(A("CA"), A("psC", 0, 64), IDT, 18.5, 0.125)
-
-    def cwrap():
-        for m in range(16):
-            mm(A("psC", 0, 64), A("Dm", m * 128, m * 128 + 128), A("CB", m, 1024, 16), m == 0, m == 15)
-        entries()
+    def ustart():
+        mm(A("psW", 0, 64), A("NEG"), A("ONE"), True, False)
 
     def uwrap(k):
-        mm(A("psW", 0, 64), A("NEG"), A("ONE"), True, False)
+        b, s, o = ZAT[k]
         for m in range(16):
-            mm(A("psW", 0, 64), A("Wm", m * 128, m * 128 + 128), zcol(k, m), False, m == 15)
+            mm(A("psW", 0, 64), A("Wm", m * 128, m * 128 + 128), A(b, s * m + o, 1024 * s, 16 * s), False, m == 15)
 
-    def scan1(q):
-        scan(A("OA", 1024 * q, 1024 * q + 1024), A("MASK4"), A("ZA", 1024 * q, 1024 * q + 1024), MUL, MAX)
+    def entries(src, off):
+        act(A("CB4"), src, IDT, 16383.75 + 4 * off, 4.0)
+        act(A("CA"), src, IDT, 296.0 + 2 * off, 2.0)
 
-    def scan1copy(q):
-        actcp(A("ZB", 1024 * q, 1024 * q + 1024, 4), A("OA", 1024 * q + 3, 1024 * q + 1024, 4))
-
-    def scan2(q):
-        scan(A("OB", 1024 * q, 1024 * q + 1024), A("MASK4"), A("ZB", 1024 * q, 1024 * q + 1024), MUL, MAX)
+    def maxima(j, q):
+        if j < 2:
+            r = (768 * q, 768 * q + 768)
+            scan(A("O%d" % j, *r), A("M3"), A("G%d" % j, *r), MUL, MAX)
+            s = 3 + j
+            gcp(A("G%d" % (j + 1), 256 * s * q, 256 * s * (q + 1), s), A("O%d" % j, r[0] + 2, r[1], 3), 256)
+        else:
+            r = (1024 * q, 1024 * q + 1024)
+            scan(A("O2", *r), A("D2", *r), A("G2", *r), ADD, MAX)
 
     def arith(k):
         old, nx = "DP%d" % k, "DP%d" % (k + 1)
-        tt(A("I1"), A("psW", 0, 64), A("CBF"), ADD)
-        if k == 7:
-            ts(A("N64"), A("I1"), 192, AND)
-            tt(A("LOG", 512, 576), A("LOG", 448, 512), A("N64"), ADD)
-            return
-        tt(A("psA", 0, 64), A("psW", 0, 64), A("CA"), MUL)
-        ts(A("N64"), A("I1"), 192, AND)
-        ts(A("DH"), A("I1"), 4, SHR)
-        tt(A(nx, 1, 128, 2), A(old, 1, 128, 2), A("N64"), ADD)
-        tt(A("YI"), A("psA", 0, 64), A("DH"), ADD)
-        ts(A(nx, 0, 128, 2), A(nx, 1, 128, 2), A("MC", k + 1, k + 2), GE)
-        scan(A("QS"), A("L0"), A(nx), MUL, ADD)
+        tt(A("DH"), A("psW", 0, 64), A("CB4"), ADD)
+        tt(A("psP", 0, 64), A("psW", 0, 64), A("CA"), MUL)
+        ts(A("N4"), A("DH"), 12, AND)
+        tt(A("YI"), A("psP", 0, 64), A("DH"), ADD)
+        tt(A(nx, 1, 128, 2), A(old, 1, 128, 2), A("N4"), ADD)
         ts(A("SI"), A("YI"), 2, SHR, W - 1, AND)
-        cp(A("OFFC"), A("QS", 1, 128, 2))
+        ts(A(nx, 0, 128, 2), A(nx, 1, 128, 2), A("MC", k + 1, k + 2), GE)
         cp(A("OFFZ"), A("SI"))
 
-    def log(k):
-        tt(A("LOG", 64 * (k + 1), 64 * (k + 2)), A("LOG", 64 * k, 64 * (k + 1)), A("N64"), ADD)
+    def stairs(k):
+        scan(A("QS"), A("L0"), A("DP%d" % k), MUL, ADD)
+        ts(A("DB", 0, 512, 8), A("QS", 1, 128, 2), -1.0, MUL, 34.0 - 4 * k, ADD)
+        if k > 1:
+            ts(A("UB", 0, 576, 9), A("QS", 1, 128, 2), 4.0 * k - 30, ADD, 34.0, MIN)
+        scan(A("DO"), A("DA"), A("DB"), ADD, MAX)
+        if k > 1:
+            scan(A("UO"), A("UA"), A("UB"), ADD, MAX)
+
+    def csum(k, C):
+        terms = [(A("GT8"), C)]
+        terms += [(A("N64" if j % 2 else "P64"), A("DO", j, 512, 8)) for j in range(1, 9 - k)]
+        if k == 1:
+            terms += [(A("P32"), A("DO", 0, 512, 8))]
+        else:
+            terms += [(A("N32"), A("UO", 0, 576, 9))]
+            terms += [(A("P64" if j % 2 else "N64"), A("UO", j, 576, 9)) for j in range(1, 5 if k == 2 else 9)]
+        for j, (l, r) in enumerate(terms):
+            mm(A("psC", 0, 64), l, r, j == 0, j == len(terms) - 1)
+
+    def logmm(k):
+        mm(A("ps3", 0, 64), A("H9"), A("DP%d" % k, 1, 128, 2), True, False)
+        mm(A("ps3", 0, 64), A("H1"), A("DP%d" % (k + 1), 1, 128, 2), False, True)
+
+    def logact(k):
+        act(A("LG", 8 - k, 640, 10), A("ps3", 0, 64), IDT, 8.0 * k + 19)
 
     ysn = [0]
 
     def ysum(cnt):
         for _ in range(cnt):
             c = ysn[0]
-            mm(A("psY", 0, 64), A("ID"), A("X", c, W, 128), c == 0, False)
-            ysn[0] += 1
+            if c < 128:
+                mm(A("psY", 0, 64), A("ID"), A("X", c, W, 128), c == 0, False)
+                ysn[0] += 1
+
+    PLAN = {2: ([], [(0, 0), (0, 1)]), 3: ([], [(0, 2), (0, 3)]), 4: ([], [(1, 0), (1, 1)]),
+            5: ([], [(1, 2), (1, 3)]), 6: ([], [(2, 0), (2, 1)]), 7: ([(2, 2), (2, 3)], [])}
 
     for t in range(RO):
         last = t == RO - 1
         lnd, snd, F = "LND%d" % t, "SND%d" % t, "F%d" % t
-        C, L = A(lnd, 0, 64), A(lnd, 64, 128)
+        C, LB = A(lnd, 0, 64), A(lnd, 64, 128)
+        ustart()
+        mm(A("ps4", 0, 256), A("ID"), A("K0"), True, False)
+        mm(A("ps5", 0, 512, 8), A("NEG"), A("ONE"))
         for l in range(1, 5):
-            mm(A("psF1", l * 64 - 64, l * 64), A("SH%d" % l), C)
-        for q in range(16):
-            mm(A("psA" if q < 8 else "psB", (q % 8) * 64, (q % 8) * 64 + 64), A("GT", q * 128, q * 128 + 128), C)
-        ts(A("T613"), L, 613.0, MUL)
-        tt(A("S0"), A("T613"), A("SA" if t else "ST0"), ADD)
+            mm(A("ps4", l - 1, 256, 4), A("C0%d" % l), C, False, False)
+            mm(A("ps4", l - 1, 256, 4), A("R0N"), LB, False, l == 4)
+        for j in range(1, 8):
+            mm(A("ps5", j, 512, 8), A("TL", 128 * (j - 1), 128 * j), C)
+        ts(A("T613"), LB, -613.0, MUL, A("ACOL"), ADD)
+        tt(A("S0"), A("T613"), A("ST%d" % t), ADD)
+        ts(A("L0", 1, 128, 2), LB, -4.0, MUL, 16.0, ADD)
         ts(A("SI"), A("S0"), W - 1, AND)
         cp(A("OFFZ"), A("SI"))
-        gz(actcp, 0, 0, Z0_SCALAR)
-        for l in range(1, 5):
-            ts(A("MK", l * 64 - 64, l * 64), L, float(l), EQ)
-        tt(A("CM"), A("MK"), A("psF1", 0, 256), MUL)
-        mm(A("psC", 0, 64), A("GT", 0, 128), C, True, False)
-        for l in range(1, 5):
-            mm(A("psC", 0, 64), A("R0"), A("CM", l * 64 - 64, l * 64), False, l == 4)
-        entries()
-        actcp(A("RT", 0, 512), A("psA"))
-        actcp(A("RT", 512, 1024), A("psB"))
-        gz(cp, 0, Z0_SCALAR, 64)
-        ts(A("L0", 1, 128, 2), L, 64.0, MUL)
+        act(A("A0"), A("ps4", 0, 256), ABS)
+        gz(actcp, 0, 0, Z_SCALAR[0])
+        gz(cp, 0, Z_SCALAR[0], 64)
+        scan(A("A0O"), A("M4"), A("A0"), ADD, MIN)
+        entries(A("A0O", 3, 256, 4), 0)
         uwrap(0)
-        if t == 0:
-            late_constants(0)
+        for h, ps in enumerate(("ps6", "ps3")):
+            mm(A(ps, 0, 288, 9), A("NEG"), A("ONE", 0, 32))
+            for j in range(1, 9):
+                mm(A(ps, j, 288, 9), A("TL", 128 * (6 + j), 128 * (7 + j)), A(lnd, 32 * h, 32 * h + 32))
+        ts(A("DA"), A("ps5"), -4.0, ADD)
+        act(A("NF"), A(F), IDT, 0.0, -1.0)
+        act(A("UA", 288, 576), A("ps3", 0, 288), IDT, -4.0)
         for m in range(16):
-            for h in range(2):
-                mm(A("psF%d" % h, m, 512, 16), A("ID"), A(F, 32 * h, 32 * h + 32))
-        ts(A("PRI"), L, 32.0, MUL, A("C16M"), ADD)
-        ts(A("LM15"), L, 15.0, ADD)
-        arith(0)
-        for k in range(1, 7):
-            gc(actcp, k, 0, C_SCALAR)
-            gc(cp, k, C_SCALAR, 64)
-            gz(actcp, k, 0, Z_SCALAR)
-            gz(cp, k, Z_SCALAR, 64)
-            log(k - 1)
-            cwrap()
-            uwrap(k)
+            gcp(A("D2", 4 * m + 3, 4096, 64), A("NF"), 64)
+        for k in range(1, 8):
+            arith(k - 1)
+            gz(actcp, k, 0, Z_SCALAR[k] if k < 7 else 32)
+            if k == 7:
+                gz(actcp, k, 32, Z_SCALAR[k])
+            ustart()
+            logmm(k - 1)
             if last:
-                ysum(21)
-            if k == 3:
-                scan1(0)
-            elif k == 4:
-                scan1(1)
-                scan1(2)
-                scan1copy(0)
-            elif k == 5:
-                scan1(3)
-                scan1copy(1)
-                scan1copy(2)
-                scan1copy(3)
-            elif k == 6:
-                scan2(0)
-            elif t == 0:
-                late_constants(k)
-            arith(k)
-        gc(actcp, 7, 0, 64)
-        gz(actcp, 7, 0, 64)
-        for q in range(1, 4):
-            scan2(q)
-        log(6)
-        cwrap()
+                ysum(19)
+            if k == 6:
+                for h, ps in enumerate(("ps4", "ps5")):
+                    mm(A(ps), A("ID"), A("D2", 2048 * h + 3, 2048 * h + 2048, 4), True, False)
+            if k == 7:
+                mm(A("ps4"), A("I256"), A("O2", 3, 2048, 4), False, False)
+            stairs(k)
+            csum(k, C)
+            for j, q in PLAN.get(k, ([], []))[0]:
+                maxima(j, q)
+            gz(cp, k, Z_SCALAR[k], 64)
+            entries(A("psC", 0, 64), -64 if k == 1 else 64)
+            logact(k - 1)
+            if k == 7:
+                break
+            uwrap(k)
+            if k == 1:
+                ts(A("UA", 0, 288), A("ps6", 0, 288), -4.0, ADD)
+                act(A("LG", 9, 640, 10), LB, IDT, 4.0, -1.0)
+            if k == 2:
+                act(A("WD", 1, 128, 2), LB, EXP, 9.0, -3.0)
+            for j, q in PLAN.get(k, ([], []))[1]:
+                maxima(j, q)
+            if t == 0 and k <= 5:
+                late_constants(k - 1)
+        mm(A("ps4"), A("ID"), A("Z7", 2, 2048, 4), False, True)
+        for q in (2, 3):
+            mm(A("ps5", 256 * q - 512, 256 * q - 256), A("I256"), A("O2", 1024 * q + 3, 1024 * q + 1024, 4),
+               False, False)
+        mm(A("ps5"), A("ID"), A("Z7", 2050, 4096, 4), False, True)
+        act(A("GEb", 0, 512), A("ps4"), SIGN, 256.5)
+        ts(A("GEb", 512, 1024), A("ps5"), -256.5, GE, -0.5, ADD)
         uwrap(7)
-        if last:
-            ysum(128 - ysn[0])
-        for h in range(2):
-            o, i = 512 * h, A("OFFZ", 32 * h, 32 * h + 32)
-            tt(A("VB", o, o + 512), IND(A("X", 0, W), i), A("OB", 4 * o + 3, 4 * o + 2048, 4), MAX)
-        for h in range(2):
-            o = 512 * h
-            tt(A("GEb", o, o + 512), A("VB", o, o + 512), A("psF%d" % h), GE)
-        arith(7)
+        mm(A("ps6", 0, 128), A("I256"), A("TH2"), True, False)
         for m in range(16):
-            mm(A("psA", 0, 64), A("Gm", m * 128, m * 128 + 128), A("GEb", m, 1024, 16), m == 0, m == 15)
-        for l in range(1, 5):
-            mm(A("psF0", l * 64 - 64, l * 64), A("SH%d" % l), C)
-        ts(A("FT"), A("psA", 0, 64), 9.5, GE)
-        tt(A("SC"), A("FT"), A("PRI"), MUL)
-        run("t", [A("psT", 0, 128)], [A("SC"), A("ID")],
-            lambda: g.tensor.transpose(T["psT"][0:64, 0:128], T["SC"][:, 0:64], T["ID"][:]))
-        scan(A("SX", 0, 128, 1, 64), A("MASK16", 0, 128, 1, 64), A("psT", 0, 128, 1, 64), MUL, MAX)
-        mm(A("psC", 0, 64), A("SX", 0, 128, 1, 64), A("ID", 0, 64, 1, 64))
-        cp(A("PX"), A("psC", 0, 64))
-        mm(A("psW", 0, 64), A("GT", 15 * 128, 16 * 128), A("PX"))
-        tt(A("psA", 0, 64), A("SC"), A("psW", 0, 64), EQ)
-        cp(A("BI"), A("psW", 0, 64))
-        for h, ps in ((0, "psB"), (1, "psC")):
-            o = 256 * h
-            mm(A(ps, 0, 256), A("ID"), A("KQ", o, o + 256), True, False)
-            for k in range(4 * h + 1, 4 * h + 5):
-                tt(A("OHL", 64 * k, 64 * k + 64), A("LOG", 64 * k, 64 * k + 64), A("psA", 0, 64), MUL)
-            mm(A(ps, 0, 256), A("BO3"), A("OHL", o, o + 256), False, False)
-            mm(A(ps, 0, 256), A("BO1"), A("OHL", o + 64, o + 320), False, True)
-        ts(A("MI"), A("BI"), 31, AND)
-        ts(A("LI"), A("BI"), 5, SHR)
-        ts(A("AT", 0, 256), A("psB", 0, 256), 0.0, MAX, 4.0, MIN)
-        act(A("SG", 256, 512), A("psC", 0, 256), SIGN, -3.5)
-        act(A("SG", 0, 256), A("psB", 0, 256), SIGN, -3.5)
-        ts(A("OK"), A("psW", 0, 64), 0.5, GE)
-        ts(A("GG"), A("MI"), A("C16M"), GE)
-        ts(A("AT", 256, 512), A("psC", 0, 256), 0.0, MAX, 4.0, MIN)
-        tt(A("LE"), A("GG"), A("LI"), MUL)
-        mm(A("psW", 0, 64), A("IN1"), A("LM15"), True, False)
-        for name, lhs, k0 in (("AT", "ID", 0), ("SG", "IN2", 4), ("SG", "IN2", 0), ("AT", "ID", 4)):
-            for k in range(k0, k0 + 4):
-                mm(A("psW", 0, 64), A(lhs), A(name, 64 * k, 64 * k + 64), False, (name, k) == ("AT", 7))
-        for l in range(1, 5):
-            ts(A("MK", l * 64 - 64, l * 64), A("LE"), float(l), EQ)
-        tt(A("CM"), A("MK"), A("psF0", 0, 256), MUL)
-        mm(A("psF1", 0, 64), A("ID"), C, True, False)
-        for l in range(1, 5):
-            mm(A("psF1", 0, 64), A("ID"), A("CM", l * 64 - 64, l * 64), False, l == 4)
-        tt(A("DL"), A("psW", 0, 64), A("OK"), MUL)
-        tt(A(snd, 64, 128), A("DL"), L, ADD)
-        actcp(A(snd, 0, 64), A("psF1", 0, 64))
+            mm(A("ps6", 0, 128, 2), A("Gm", m * 128, m * 128 + 128), A("GEb", m, 1024, 16), False, m == 15)
+        act(A("PRE"), A("DP7", 1, 128, 2), IDT, 75.0, 2.0)
+        actcp(A("O2", 0, 4096, 64), A(F))
+        tt(A("DH"), A("psW", 0, 64), A("CB4"), ADD)
+        ts(A("N4"), A("DH"), 2, SHR, 3, AND)
+        tt(A("LG", 1, 640, 10), A("PRE"), A("N4"), SUB)
+        scan(A("WO"), A("WD"), A("ps6", 0, 128), MIN, MAX)
+        mm(A("ps4", 0, 320), A("ID"), A("K5"), True, False)
+        mm(A("psC", 0, 64), A("ALF"), A("WO", 1, 128, 2))
+        OH = A("LG", 0, 640, 10)
+        ts(OH, A("psC", 0, 64), 0.0, LT, 256.0, MUL)
+        for l in range(5):
+            mm(A("ps4", l, 320, 5), A("SH%d" % l if l else "ID"), C, False, False)
+        scan(A("OHL"), A("LM"), A("LG"), ADD, MIN)
+        mm(A("psW", 0, 64), A("ID"), A("DG"), True, False)
+        mm(A("psW", 0, 64), A("MV"), OH, False, True)
+        mm(A("psW", 64, 128), A("BO3"), OH)
+        for l in range(5):
+            mm(A("ps4", l, 320, 5), A("TRI"), A("OHL", 9, 640, 10), False, l == 4)
+        for s in range(8):
+            mm(A("ps5", s, 512, 8), A("BO"), A("OHL", 1 + s, 640, 10))
+        scan(A("SD"), A("M16F"), A("psW", 0, 64), MUL, MAX)
+        tt(A("EE"), A("psW", 64, 128), LB, MAX)
+        cp(A("OV"), A("SD", 15, 64, 16))
+        act(A("AL"), A("ps4", 0, 320), ABS)
+        act(A("AS"), A("ps5"), ABS, A("QB"))
+        mm(A("ps6", 0, 64), A("ID"), A("DGX"), True, False)
+        mm(A("ps6", 0, 64), A("BON"), A("KX") if last else OH, False, True)
+        mm(A("psP", 0, 64), A("BO1" if last else "ONS"), OH)
+        cp(A("VV6"), IND(A("O2"), A("OV")))
+        scan(A("ALO"), A("M5"), A("AL"), ADD, MIN)
+        tt(A("VV"), IND(A("Z7"), A("OV")), A("VV6"), MAX)
+        cp(A(snd, 0, 64), A("ALO", 4, 320, 5))
+        mm(A("psC", 0, 64), A("WB1"), A("VV"))
+        scan(A("AO"), A("M8"), A("AS"), ADD, MIN)
+        tt(A(snd, 64, 128), A("AO", 7, 512, 8), A("EE"), MIN)
         if not last:
             out_total += send(snd, "LND%d" % (t + 1), "arr%d" % (t + 1), T.cores[(rank + 1) % n])
             landed("LND%d" % (t + 1), "arr%d" % (t + 1), len(topo.engines(T.cores[(rank - 1) % n], core)))
-            mm(A("psA", 0, 64), A("ON16"), A("OK"))
+            act(A("PR"), A("psP", 0, 64), IDT, 4 * 613 / 64, 1.0, A("ACOL"))
         else:
-            dma("y", "oL", T.yl[:], T[snd][:, 64:128], [], [A(snd, 64, 128)])
+            act(A("YL"), A(snd, 64, 128), IDT, 4.0, -1.0)
             dma("y", "oC", T.yc[:], T[snd][:, 0:64], [], [A(snd, 0, 64)])
-        tt(A("MD"), A("MI"), A("DIAG"), MUL)
-        scan(A("SD"), A("M16F"), A("MD"), MUL, ADD)
-        tt(A("OKD"), A("OK"), A("DIAG"), MUL)
-        tt(A("O4"), A("BV4"), A("SD", 15, 64, 16), SUB)
-        cp(A("OV"), A("O4"))
-        cp(A("VV"), IND(A("VB"), A("OV")))
-        mm(A("psC", 0, 64), A("WB1"), A("VV"))
-        tt(A("FVI"), A(F), A("VV"), ADD)
+            dma("y", "oL", T.yl[:], A("YL")[0], [], [A("YL")])
         cp(A("HI"), A("psC", 0, 64))
-        ts(A("FH"), A("FVI"), 1, SHR)
+        tt(A("FVI"), A(F), A("VV"), ADD)
         ts(A("HM"), A("HI"), 127, AND)
-        tt(A("FD"), A("FH"), A(F), SUB)
-        tt(A("X1"), A("HM"), A("OFXC"), ADD)
-        tt(A("FE"), A("FD"), A("OK"), MUL)
-        tt(A("X2"), A("X1"), A("OKD"), MUL)
-        tt(A("F%d" % (t + 1)), A(F), A("FE"), ADD)
-        scan(A("SD2"), A("M16F"), A("X2"), MUL, ADD)
-        tt(A("O4X"), A("BX4"), A("SD2", 15, 64, 16), ADD)
-        cp(A("OX"), A("O4X"))
+        ts(A("FH"), A("FVI"), 1, SHR)
+        tt(A("X1"), A("ps6", 0, 64), A("HM"), ADD)
+        cp(A("F%d" % (t + 1)), A("FH"))
+        scan(A("SD2"), A("M16F"), A("X1"), MUL, MAX)
+        cp(A("OX"), A("SD2", 15, 64, 16))
         if not last:
-            run("v", [A("ACOL")], [A("psA", 0, 64)],
-                lambda: g.vector.tensor_reduce(T["ACOL"][:], T["psA"][:, 0:64], AxisListType.X, ADD))
             cp(IND(A("X"), A("OX")), A("VV"))
-            ts(A("SA"), A("ST%d" % (t + 1)), A("ACOL"), ADD)
         else:
-            cp(A("OLD"), IND(A("X"), A("OX")))
-            tt(A("PR"), A("VV"), A("OLD"), SUB)
-            tt(A("DIF"), A("PR"), A("OK"), MUL)
-            mm(A("psY", 0, 64), A("ID"), A("DIF"), False, True)
-            cp(A("YS"), A("psY", 0, 64))
             dma("y", "oF", T.yf[:], T["F4"][:], [], [A("F4")])
+            tt(A("PR"), IND(A("X", 0, W), A("OX")), A("VV"), SUB)
+            tt(A("DIF"), A("PR"), A("psP", 0, 64), MUL)
+            mm(A("psY", 0, 64), A("NID"), A("DIF"), False, True)
+            cp(A("YS"), A("psY", 0, 64))
             dma("y", "oS", T.ys[:], T["YS"][:], [], [A("YS")])
 
     for q in "vstg":

@@ -2,7 +2,7 @@ import math
 from concourse.mybir import dt, AluOpType, AxisListType, ActivationFunctionType
 
 ADD, SUB, MUL, MAX, MIN = AluOpType.add, AluOpType.subtract, AluOpType.mult, AluOpType.max, AluOpType.min
-GE, EQ, LT, LE, GT = AluOpType.is_ge, AluOpType.is_equal, AluOpType.is_lt, AluOpType.is_le, AluOpType.is_gt
+GE, EQ, LT, GT, NE = AluOpType.is_ge, AluOpType.is_equal, AluOpType.is_lt, AluOpType.is_gt, AluOpType.not_equal
 SHR, AND = AluOpType.arith_shift_right, AluOpType.bitwise_and
 IDT, SIGN, ABS = ActivationFunctionType.Identity, ActivationFunctionType.Sign, ActivationFunctionType.Abs
 COPY, EXP = ActivationFunctionType.Copy, ActivationFunctionType.Exp
@@ -30,39 +30,41 @@ _d("G2 O2 D2 Z7", 4096, "bfloat16")
 _d("GEb", 1024, "bfloat16")
 _d("M3", 768, "bfloat16")
 _d("Gm Wm", 2048, "bfloat16")
-_d("TL", 15 * 128, "bfloat16")
-_pool("MATS", "ID BO BO3 BO1 BON WB1 SH1 SH2 SH3 SH4 C01 C02 C03 C04 R0N GT8 NEG ONS H9 H1 I256 ALF TRI MV NID "
-              "tm0 tm1 tm2 tm3 TH2 WD WO L0 QS DP0 DP1 DP2 DP3 DP4 DP5 DP6 DP7", 128, "bfloat16")
+_pool("TL", " ".join("TL%d" % k for k in range(15)), 128, "bfloat16")
+_pool("MATS", "ID BO BO3 BO1 BON B256 WB1 SH1 SH2 SH3 SH4 C01 C02 C03 C04 R0N GT8 NEG ONS H9 H1 I256 ALF TRI MV NID "
+              "tm7 tm8 TH2 WD WO L0 QS DP0 DP1 DP2 DP3 DP4 DP5 DP6 DP7", 128, "bfloat16")
 _pool("HMATS", "P64 N64 P32 N32", 128, "float16")
-_pool("SMALL", "ONE SP0 NF EE PRE VV6 VV OLD DIF DG DGX KX YL", 64, "bfloat16")
+_pool("SMALL", "ONE SP0 NF EE PRE VV6 VV DIF DG DGX KX YL", 64, "bfloat16")
 _d("UA UB UO", 576, "float16")
 _d("DA DB DO", 512, "float16")
 _d("LG LM OHL", 640, "bfloat16")
-_d("AS AO M8", 512, "bfloat16")
+_d("AS AO", 512, "bfloat16")
 _d("K5 M5 AL ALO", 320, "bfloat16")
-_d("K0 M4 A0 A0O", 256, "bfloat16")
+_d("K0 M4 M8 A0 A0O", 256, "bfloat16")
 _d("F0 F1 F2 F3 F4", 64, "bfloat16")
-_d("LND0 LND1 LND2 LND3 SND0 SND1 SND2 SND3", 128, "bfloat16")
+_d("C0 C1 C2 C3 SC0 SC1 SC2 SC3 LB0 LB1 LB2 LB3 SL0 SL1 SL2 SL3", 64, "bfloat16")
 _d("WT", 1, "bfloat16")
 _d("ST0 ST1 ST2 ST3", 64, "int32")
 _pool("INTS", "N4 DH YI SI T613 S0 HI HM FVI FH", 64, "int32")
-_d("ROW CQI CGI", 128, "int32")
 _d("PI QI GI", 1, "int32")
 _d("ROWF CQF CGF", 128, "float32")
-_d("PC QC GC QB MW ACOL", 1, "float32")
-_d("PCL PCG", 4, "float32")
-_d("EQ16 COEF", 32, "float32")
-_d("MC", 8, "float32")
-_pool("FLTS", "CA CB4 PR M16F DIAG SD X1 SD2", 64, "float32")
+_d("QC GC PC QB MW ACOL", 1, "float32")
+_d("EQ16", 32, "float32")
+_pool("COEF", "CD0 CD1 CD2 CD3 CD4 CD5 CD6 CU0", 1, "float32")
+_d("CU MC", 8, "float32")
+_pool("FLTS", "CA CB4 PR M16F DIAG SD X1 X2 SD2", 64, "float32")
 _d("YS", 64, "float32")
 _d("OFFZ", 64, "uint16")
 _d("OV OX", 4, "uint16")
 _d("psW psC psP ps3 ps4 ps5 ps6 psY", 512, "float32", "psum")
 
 SEMAPHORES = ["qv", "qs", "qt", "qg", "dX", "dW", "dC", "dL", "dS", "dF", "oC", "oL", "oF", "oS", "loc"]
-SEMAPHORES += ["st%d" % t for t in range(1, RO)] + ["arr%d" % t for t in range(1, RO)]
+SEMAPHORES += ["%s%d" % (s, t) for s in ("st", "arC", "arL") for t in range(1, RO)]
 
-Z_SCALAR = [32, 36, 48, 48, 48, 48, 48, 62]
+Z_SCALAR = {0: [0, 16, 34], 1: [0, 38], 7: [0, 32, 48, 54]}
+Z_VECTOR = {0: [34, 64], 1: [38, 44, 50, 64], 7: [54, 64]}
+for _k in range(2, 7):
+    Z_SCALAR[_k], Z_VECTOR[_k] = [0, 46], [46, 52, 58, 64]
 
 
 class Ap(tuple):
@@ -79,6 +81,7 @@ def rank_program(g, core, T, topo):
     known = {q: {} for q in queue}
     snap = {}
     seen = {}
+    held = []
 
     def A(name, a=None, b=None, step=1):
         buf, off, cols = POOL[name] if name in POOL else (name, 0, SCRATCH[name][1][1])
@@ -132,6 +135,9 @@ def rank_program(g, core, T, topo):
                     lst.append([lo, hi, step, w, q, sem, val])
 
     def run(q, outs, ins, call):
+        if held:
+            held[0].append((q, outs, ins, call))
+            return
         deps(q, outs, ins)
         sem = "q" + q
         count[q] += 1
@@ -139,14 +145,27 @@ def rank_program(g, core, T, topo):
         call().then_inc(T.sem[sem], 1)
         record(q, outs, ins, sem, count[q])
 
+    def weave(make, gap=4):
+        held.append([])
+        make()
+        calls = held.pop()
+
+        def names(group):
+            return {r[0] for x in group for r in x[1]}
+        before = [[j for j in range(i) if names(calls[j][1]) & (names(c[1]) | names(c[2]))
+                   or names(calls[j][2]) & names(c[1])] for i, c in enumerate(calls)]
+        done = {}
+        while len(done) < len(calls):
+            free = [i for i in range(len(calls)) if i not in done and all(j in done for j in before[i])]
+            i = min(free, key=lambda i: (max([len(done)] + [done[j] + gap for j in before[i]]), i))
+            done[i] = len(done)
+            run(*calls[i])
+
     def dma(q, sem, out, in_, outs, ins):
         deps(q, outs, ins)
         snap[(sem, 16)] = dict(known[q])
         queue[q].dma_start(out, in_).then_inc(T.sem[sem], 16)
         record("dma" + sem, outs, ins, sem, 16)
-
-    def landed(name, sem, val):
-        record("net" + sem, [A(name)], [], sem, val)
 
     def isap(s):
         return isinstance(s, Ap)
@@ -187,151 +206,140 @@ def rank_program(g, core, T, topo):
     def mm(out, l, r, start=True, stop=True):
         run("t", [out], [l, r], lambda: g.tensor.matmul(out[0], l[0], r[0], start, stop))
 
-    def iota(out, pattern, cm, base=0):
-        small = SCRATCH[POOL[out[1][0][0]][0] if out[1][0][0] in POOL else out[1][0][0]][2] != "int32"
-        if small:
-            run("g", [out], [], lambda: g.iota(out[0], pattern, base, cm, allow_small_or_imprecise_dtypes=True))
-        else:
+    def iota(out, pattern, cm=0, base=0):
+        if SCRATCH[out[1][0][0]][2] == "int32":
             run("g", [out], [], lambda: g.iota(out[0], pattern, base, cm))
+        else:
+            run("g", [out], [], lambda: g.iota(out[0], pattern, base, cm, allow_small_or_imprecise_dtypes=True))
+
+    def pick(out, a, pattern, op, other, base, cm):
+        run("g", [out], [a], lambda: g.affine_select(out[0], a[0], pattern, op, other, base, cm))
 
     def gcp(out, a, cols):
-        run("g", [out], [a], lambda: g.affine_select(out[0], a[0], [[0, cols]], GE, 0.0, 0, 0))
+        pick(out, a, [[0, cols]], GE, 0.0, 0, 0)
 
-    dma("y", "dX", T["X"][:, 0:W], T.x[:], [A("X", 0, W)], [])
+    def resets(name, cols, step, first, other):
+        iota(A(name), [[0, cols]], 0, other)
+        iota(A(name, 0, cols, step), [[0, cols // step]], 0, first)
+
+    sent = [0]
+
+    def send(src, name, sem, hop):
+        dst = T.cores[(rank + hop) % n]
+        rid, pid, _ = topo.addr(dst)
+        deps("g", [], [A(src)])
+        g.remote_dma(out_ap=T[name][:], in_ap=T[src][:], remote_sem=T.sem[sem], local_sem=T.sem.loc,
+                     pid=pid, routing_id=rid, dma_engine_mask=topo.mask(core, dst))
+        sent[0] += len(topo.engines(core, dst))
+        record("net" + sem, [A(name)], [], sem, len(topo.engines(T.cores[(rank - hop) % n], core)))
+
     dma("s", "dS", T["ST0"][:], T.st[:], [A("ST0")], [])
+    dma("y", "dW", T["WT"][:], T.wt[:], [A("WT")], [])
     dma("s", "dL", A("SP0")[0], T.sp[:], [A("SP0")], [])
-    dma("s", "dC", T["LND0"][:, 0:64], T.ch[:], [A("LND0", 0, 64)], [])
-    dma("s", "dW", T["WT"][:], T.wt[:], [A("WT")], [])
+    dma("y", "dC", T["C0"][:], T.ch[:], [A("C0")], [])
+    dma("y", "dX", T["X"][:, 0:W], T.x[:], [A("X", 0, W)], [])
     dma("s", "dF", T["F0"][:], T.fl[:], [A("F0")], [])
 
     iota(A("PI"), [[1, 1]], 1)
-    iota(A("ROW"), [[1, 128]], 0)
+    iota(A("CGF"), [[1, 8], [0, 16]])
+    iota(A("ROWF"), [[1, 128]])
+    iota(A("CQF"), [[0, 8], [1, 16]])
     iota(A("K0"), [[0, 64], [-256, 4]], 0, 768)
-
-    def send(t_from, name_to, sem, dst):
-        rid, pid, _ = topo.addr(dst)
-        deps("g", [], [A(t_from)])
-        g.remote_dma(out_ap=T[name_to][:], in_ap=T[t_from][:], remote_sem=T.sem[sem], local_sem=T.sem.loc,
-                     pid=pid, routing_id=rid, dma_engine_mask=topo.mask(core, dst))
-        return len(topo.engines(core, dst))
-    out_total = 0
     for t in range(1, RO):
-        out_total += send("ST0", "ST%d" % t, "st%d" % t, T.cores[(rank + t) % n])
-        landed("ST%d" % t, "st%d" % t, len(topo.engines(T.cores[(rank - t) % n], core)))
-    iota(A("K5"), [[0, 64], [-256, 5]], 0)
-    iota(A("D2", 0, 4096, 4), [[0, 1024]], 0, -1024)
-    iota(A("D2", 1, 4096, 4), [[0, 1024]], 0)
-    iota(A("D2", 2, 4096, 4), [[0, 1024]], 0)
-    iota(A("G2", 3, 4096, 4), [[0, 1024]], 0, -1)
+        send("ST0", "ST%d" % t, "st%d" % t, t)
 
-    fill(A("Gm"), 0.0)
-    ts(A("QI"), A("PI"), 15, AND)
-    ts(A("GI"), A("PI"), 4, SHR)
-    cp(A("PC"), A("PI"))
-    cp(A("ROWF"), A("ROW"))
-    cp(A("QC"), A("QI"))
-    cp(A("GC"), A("GI"))
-    ts(A("CQI"), A("ROW"), 15, AND)
-    ts(A("CGI"), A("ROW"), 4, SHR)
-    cp(A("CQF"), A("CQI"))
-    cp(A("CGF"), A("CGI"))
-    ts(A("BO"), A("CGF"), A("GC"), EQ)
-    ts(A("ID"), A("ROWF"), A("PC"), EQ)
-    ts(A("EQ16"), A("ROWF", 0, 32), A("QC"), EQ)
+    def constants():
+        fill(A("Gm"), 0.0)
+        ts(A("GI"), A("PI"), 4, SHR)
+        ts(A("QI"), A("PI"), 15, AND)
+        cp(A("PC"), A("PI"))
+        cp(A("GC"), A("GI"))
+        cp(A("QC"), A("QI"))
+        ts(A("BO"), A("CGF"), A("GC"), EQ)
+        ts(A("ID"), A("ROWF"), A("PC"), EQ)
+        ts(A("EQ16"), A("ROWF", 0, 32), A("QC"), EQ)
+        for name, x in (("NEG", -128.0), ("ONE", 1.0), ("L0", 0.0), ("DP0", 0.0), ("UB", 0.0), ("DB", 0.0),
+                        ("ACOL", 4.0 * 613)):
+            fill(A(name), x)
+        ts(A("MC"), A("ROWF", 0, 8), -1.0, MUL, A("QC"), ADD)
+        ts(A("MC"), A("MC"), 4.0, MUL)
+        for l in range(1, 5):
+            ts(A("C0%d" % l), A("BO"), A("EQ16", 0, 1), MUL)
+            ts(A("C0%d" % l, 0, 128, 16), A("BO", 0, 128, 16), A("EQ16", l, l + 1), MUL)
+        ts(A("R0N"), A("ID"), A("EQ16", 0, 1), MUL, -256.0, MUL)
+        ts(A("K0"), A("K0"), A("EQ16", 0, 1), MUL)
+        tt(A("CD0"), A("EQ16", 8, 9), A("EQ16", 7, 8), SUB)
+        for j in range(1, 7):
+            tt(A("CD%d" % j), A("EQ16", 9 - j, 10 - j), A("EQ16", 7 - j, 8 - j), SUB)
+        tt(A("CU0"), A("EQ16", 9, 10), A("EQ16", 8, 9), SUB)
+        tt(A("CU", 1, 8), A("EQ16", 10, 17), A("EQ16", 8, 15), SUB)
+        for k in range(15):
+            j = k if k < 7 else k - 7
+            col = A("CD%d" % j) if k < 7 else A("CU", j, j + 1) if j else A("CU0")
+            ts(A("TL%d" % k), A("BO"), col, MUL, (-1.0) ** j / 64, MUL)
+        ts(A("GT8"), A("BO"), A("EQ16", 8, 9), MUL)
+        for name, x in (("P64", 64.0), ("N64", -64.0), ("P32", 32.0), ("N32", -32.0), ("H9", 2.25), ("H1", -0.25)):
+            ts(A(name), A("ID"), x, MUL)
+        ts(A("B256"), A("BO"), 256.0, MUL)
+        ts(A("LB0"), A("SP0"), -1.0, MUL, 4.0, ADD)
+
+    def more_constants():
+        for name, x in (("ONS", 1.0 / 256), ("KX", 16.0), ("M16F", 1.0), ("TH2", 0.0)):
+            fill(A(name), x)
+        fill(A("M16F", 0, 64, 16), 0.0)
+        fill(A("WD", 0, 128, 2), -4194304.0)
+        fill(A("TH2", 0, 64, 2), -768.0)
+        fill(A("TH2", 64, 128, 2), -384.0)
+        for name, x in (("NID", -1.0), ("I256", 256.0)):
+            ts(A(name), A("ID"), x, MUL)
+        for name, x in (("BO3", 3.0 / 256), ("BO1", 1.0 / 256), ("BON", -32.0)):
+            ts(A(name), A("BO"), x, MUL)
+
+    def last_constants():
+        ts(A("QB"), A("QC"), -8.0, MUL, -16.0, ADD)
+        ts(A("MW"), A("QC"), 4.0 / 256, MUL, 2.0 / 256, ADD)
+        ts(A("MV"), A("BO"), A("MW"), MUL)
+        ts(A("WB1"), A("BO"), A("WT"), MUL)
+        ts(A("DIAG"), A("CQF", 0, 64), A("QC"), EQ)
+        for name, x, y, tmp in (("DG", 64.0, 0.0, "X1"), ("DGX", 128.0, 8192.0, "X2")):
+            ts(A(tmp), A("ROWF", 0, 64), x, MUL, y + 32768.0, ADD)
+            tt(A(tmp), A(tmp), A("DIAG"), MUL)
+            ts(A(name), A(tmp), -32768.0, ADD)
+    weave(constants)
     for m in range(16):
         act(A("Gm", m * 129, m * 128 + 128, 16), A("BO", 0, 128, 16), IDT, 0.0, 65536.0)
-    fill(A("NEG"), -128.0)
-    fill(A("ONE"), 1.0)
-    fill(A("L0"), 0.0)
-    fill(A("DP0"), 0.0)
-    for name in ("UB", "DB"):
-        fill(A(name), 0.0)
-    fill(A("M4"), 0.0)
-    fill(A("M4", 0, 256, 4), BIG)
-    ts(A("MC"), A("ROWF", 0, 8), -1.0, MUL, A("QC"), ADD)
-    ts(A("MC"), A("MC"), 4.0, MUL)
-    ts(A("tm0"), A("CQF"), 0.0, EQ)
-    tt(A("tm1"), A("tm0"), A("BO"), MUL)
-    tt(A("tm2"), A("BO"), A("tm1"), SUB)
-    ts(A("tm2"), A("tm2"), A("EQ16", 0, 1), MUL)
-    for l in range(1, 5):
-        ts(A("tm3"), A("tm1"), A("EQ16", l, l + 1), MUL)
-        tt(A("C0%d" % l), A("tm3"), A("tm2"), ADD)
-    ts(A("R0N"), A("ID"), A("EQ16", 0, 1), MUL, -256.0, MUL)
-    ts(A("K0"), A("K0"), A("EQ16", 0, 1), MUL)
-    tt(A("COEF", 0, 1), A("EQ16", 8, 9), A("EQ16", 7, 8), SUB)
-    tt(A("COEF", 7, 8), A("EQ16", 9, 10), A("EQ16", 8, 9), SUB)
-    for j in range(2, 8):
-        tt(A("COEF", j - 1, j), A("EQ16", 10 - j, 11 - j), A("EQ16", 8 - j, 9 - j), SUB)
-    tt(A("COEF", 8, 15), A("EQ16", 10, 17), A("EQ16", 8, 15), SUB)
-
-    def stair(k):
-        t = k if k < 7 else k - 7
-        ts(A("TL", 128 * k, 128 * k + 128), A("BO"), A("COEF", k, k + 1), MUL, (1.0 if t % 2 == 0 else -1.0) / 64, MUL)
-    for k in range(15):
-        stair(k)
-    ts(A("GT8"), A("BO"), A("EQ16", 8, 9), MUL)
-    for name, x in (("P64", 64.0), ("N64", -64.0), ("P32", 32.0), ("N32", -32.0), ("H9", 2.25), ("H1", -0.25)):
-        ts(A(name), A("ID"), x, MUL)
-    ts(A("LND0", 64, 128), A("SP0"), -1.0, MUL, 4.0, ADD)
     ts(A("Wm"), A("Gm"), A("WT"), MUL, 0.5 / 65536, MUL)
-    fill(A("ACOL"), 4.0 * 613)
     for h in range(2):
         act(A("Z7", 2048 * h, 2048 * h + 2048), A("Gm"), IDT, 0.0, 0.0)
+    resets("M4", 256, 4, 1024, 0)
+    resets("M3", 768, 3, 0, 1)
+    for l in range(1, 5):
+        pick(A("SH%d" % l), A("BO"), [[-1, 128]], EQ, 0.0, -l, 1)
+    pick(A("TRI"), A("B256"), [[1, 128]], GE, 0.0, 0, -1)
+    pick(A("tm7"), A("BO"), [[1, 128]], GT, 1.0 / 16, 0, -1)
+    pick(A("tm8"), A("tm7"), [[1, 128]], NE, -31.0 / 32, 0, -1)
+    iota(A("K5"), [[0, 64], [-256, 5]])
+    resets("M5", 320, 5, 1024, 0)
+    iota(A("D2", 0, 4096, 4), [[0, 1024]], 0, -1024)
 
-    def late_constants(part):
-        if part == 0:
-            fill(A("M3"), 1.0)
-            fill(A("M3", 0, 768, 3), 0.0)
-            for name, cols, step in (("M8", 512, 8), ("M5", 320, 5), ("LM", 640, 10)):
-                fill(A(name), 0.0)
-                fill(A(name, 0, cols, step), BIG)
-        elif part == 1:
-            fill(A("M16F"), 1.0)
-            fill(A("M16F", 0, 64, 16), 0.0)
-            fill(A("ONS"), 1.0 / 256)
-            fill(A("WD", 0, 128, 2), -4194304.0)
-            fill(A("TH2"), 0.0)
-            fill(A("TH2", 0, 64, 2), -768.0)
-            fill(A("TH2", 64, 128, 2), -384.0)
-            fill(A("KX"), 16.0)
-            ts(A("NID"), A("ID"), -1.0, MUL)
-            ts(A("I256"), A("ID"), 256.0, MUL)
-            ts(A("QB"), A("QC"), -8.0, MUL, -16.0, ADD)
-            ts(A("MW"), A("QC"), 4.0 / 256, MUL, 2.0 / 256, ADD)
-        elif part == 2:
-            ts(A("PCL"), A("ROWF", 1, 5), -1.0, MUL, A("PC"), ADD)
-            ts(A("PCG"), A("ROWF", 1, 5), -1.0, MUL, A("QC"), ADD)
-            ts(A("PCG"), A("PCG"), 0.0, GE, 1000.0, MUL)
-            tt(A("PCL"), A("PCL"), A("PCG"), ADD)
-            for l in range(1, 5):
-                ts(A("SH%d" % l), A("ROWF"), 1000.0, ADD, A("PCL", l - 1, l), EQ)
-            ts(A("WB1"), A("BO"), A("WT"), MUL)
-            ts(A("BO3"), A("BO"), 3.0 / 256, MUL)
-            ts(A("BO1"), A("BO"), 1.0 / 256, MUL)
-            ts(A("BON"), A("BO"), -32.0, MUL)
-            ts(A("MV"), A("BO"), A("MW"), MUL)
-        elif part == 3:
-            ts(A("tm0"), A("CQF"), A("QC"), GE, 256.0, MUL)
-            tt(A("TRI"), A("tm0"), A("BO"), MUL)
-            ts(A("tm1"), A("CQF"), A("QC"), GT, 15.0 / 16, MUL)
-            ts(A("tm1"), A("tm1"), 1.0 / 16, ADD)
-            ts(A("tm2"), A("ID"), -33.0 / 32, MUL)
-            tt(A("tm3"), A("tm1"), A("BO"), MUL)
-            tt(A("ALF"), A("tm3"), A("tm2"), ADD)
-        elif part == 4:
-            ts(A("DIAG"), A("CQF", 0, 64), A("QC"), EQ)
-            ts(A("X1"), A("ROWF", 0, 64), 64.0, MUL, 32768.0, ADD)
-            tt(A("X1"), A("X1"), A("DIAG"), MUL)
-            ts(A("DG"), A("X1"), -32768.0, ADD)
-            ts(A("SD"), A("ROWF", 0, 64), 128.0, MUL, 8192.0 + 32768.0, ADD)
-            tt(A("SD"), A("SD"), A("DIAG"), MUL)
-            ts(A("DGX"), A("SD"), -32768.0, ADD)
+    def late_constants(k):
+        if k == 1:
+            iota(A("D2", 1, 4096, 4), [[0, 1024]])
+            resets("M8", 256, 8, 1024, 0)
+            weave(more_constants)
+        if k == 2:
+            iota(A("D2", 2, 4096, 4), [[0, 1024]])
+            tt(A("ALF"), A("tm8"), A("BO"), MUL)
+        if k == 3:
+            iota(A("G2", 3, 4096, 4), [[0, 1024]], 0, -1)
+        if k == 4:
+            resets("LM", 640, 10, 1024, 0)
 
     ZAT = [("G0", 3, 0), ("G0", 3, 1), ("G0", 3, 2), ("G1", 3, 1), ("G1", 3, 2), ("G2", 4, 1), ("G2", 4, 2),
            ("Z7", 4, 2)]
 
-    def gz(eng, k, i0, i1):
+    def gz(eng, k, piece):
+        i0, i1 = (Z_SCALAR if eng is actcp else Z_VECTOR)[k][piece:piece + 2]
         if i0 < i1:
             b, s, o = ZAT[k]
             eng(A(b, 16 * s * i0 + o, 16 * s * i1, s), IND(A("X", 0, W), A("OFFZ", i0, i1)))
@@ -344,48 +352,55 @@ def rank_program(g, core, T, topo):
         for m in range(16):
             mm(A("psW", 0, 64), A("Wm", m * 128, m * 128 + 128), A(b, s * m + o, 1024 * s, 16 * s), False, m == 15)
 
-    def entries(src, off):
-        act(A("CB4"), src, IDT, 16383.75 + 4 * off, 4.0)
-        act(A("CA"), src, IDT, 296.0 + 2 * off, 2.0)
+    def entries(k, src, off):
+        ts(A("CB4"), src, 4.0, MUL, 16383.75 + 4 * off, ADD)
+        if k < 7:
+            ts(A("CA"), src, 2.0, MUL, 296.0 + 2 * off, ADD)
+            ts(A("psP", 64, 128), A("DP%d" % k, 1, 128, 2), -1.0, MUL, A("MC", k + 1, k + 2), ADD)
 
-    def maxima(j, q):
+    def maxima(j, q, parts=4):
         if j < 2:
             r = (768 * q, 768 * q + 768)
             scan(A("O%d" % j, *r), A("M3"), A("G%d" % j, *r), MUL, MAX)
             s = 3 + j
             gcp(A("G%d" % (j + 1), 256 * s * q, 256 * s * (q + 1), s), A("O%d" % j, r[0] + 2, r[1], 3), 256)
         else:
-            r = (1024 * q, 1024 * q + 1024)
+            r = (4096 // parts * q, 4096 // parts * (q + 1))
             scan(A("O2", *r), A("D2", *r), A("G2", *r), ADD, MAX)
 
-    def arith(k):
+    def arith(k, between):
         old, nx = "DP%d" % k, "DP%d" % (k + 1)
         tt(A("DH"), A("psW", 0, 64), A("CB4"), ADD)
         tt(A("psP", 0, 64), A("psW", 0, 64), A("CA"), MUL)
+        between(0)
         ts(A("N4"), A("DH"), 12, AND)
         tt(A("YI"), A("psP", 0, 64), A("DH"), ADD)
-        tt(A(nx, 1, 128, 2), A(old, 1, 128, 2), A("N4"), ADD)
+        between(1)
+        tt(A(nx, 0, 128, 2), A("N4"), A("psP", 64, 128), GE)
         ts(A("SI"), A("YI"), 2, SHR, W - 1, AND)
-        ts(A(nx, 0, 128, 2), A(nx, 1, 128, 2), A("MC", k + 1, k + 2), GE)
+        tt(A(nx, 1, 128, 2), A(old, 1, 128, 2), A("N4"), ADD)
         cp(A("OFFZ"), A("SI"))
 
-    def stairs(k):
+    def stairs(k, between):
         scan(A("QS"), A("L0"), A("DP%d" % k), MUL, ADD)
-        ts(A("DB", 0, 512, 8), A("QS", 1, 128, 2), -1.0, MUL, 34.0 - 4 * k, ADD)
+        between(0)
         if k > 1:
             ts(A("UB", 0, 576, 9), A("QS", 1, 128, 2), 4.0 * k - 30, ADD, 34.0, MIN)
-        scan(A("DO"), A("DA"), A("DB"), ADD, MAX)
+        ts(A("DB", 0, 512, 8), A("QS", 1, 128, 2), -1.0, MUL, 34.0 - 4 * k, ADD)
+        between(1)
         if k > 1:
             scan(A("UO"), A("UA"), A("UB"), ADD, MAX)
+        scan(A("DO"), A("DA"), A("DB"), ADD, MAX)
+        between(2)
 
     def csum(k, C):
         terms = [(A("GT8"), C)]
-        terms += [(A("N64" if j % 2 else "P64"), A("DO", j, 512, 8)) for j in range(1, 9 - k)]
         if k == 1:
             terms += [(A("P32"), A("DO", 0, 512, 8))]
         else:
             terms += [(A("N32"), A("UO", 0, 576, 9))]
             terms += [(A("P64" if j % 2 else "N64"), A("UO", j, 576, 9)) for j in range(1, 5 if k == 2 else 9)]
+        terms += [(A("N64" if j % 2 else "P64"), A("DO", j, 512, 8)) for j in range(1, 9 - k)]
         for j, (l, r) in enumerate(terms):
             mm(A("psC", 0, 64), l, r, j == 0, j == len(terms) - 1)
 
@@ -405,87 +420,102 @@ def rank_program(g, core, T, topo):
                 mm(A("psY", 0, 64), A("ID"), A("X", c, W, 128), c == 0, False)
                 ysn[0] += 1
 
-    PLAN = {2: ([], [(0, 0), (0, 1)]), 3: ([], [(0, 2), (0, 3)]), 4: ([], [(1, 0), (1, 1)]),
-            5: ([], [(1, 2), (1, 3)]), 6: ([], [(2, 0), (2, 1)]), 7: ([(2, 2), (2, 3)], [])}
+    PLAN = {2: [(0, 0), (0, 1)], 3: [(0, 2), (0, 3)], 4: [(1, 0), (1, 1)], 5: [(1, 2), (1, 3)]}
 
     for t in range(RO):
         last = t == RO - 1
-        lnd, snd, F = "LND%d" % t, "SND%d" % t, "F%d" % t
-        C, LB = A(lnd, 0, 64), A(lnd, 64, 128)
+        C, LB, F = A("C%d" % t), A("LB%d" % t), A("F%d" % t)
+        sndC, sndL = "SC%d" % t, "SL%d" % t
         ustart()
         mm(A("ps4", 0, 256), A("ID"), A("K0"), True, False)
         mm(A("ps5", 0, 512, 8), A("NEG"), A("ONE"))
         for l in range(1, 5):
-            mm(A("ps4", l - 1, 256, 4), A("C0%d" % l), C, False, False)
-            mm(A("ps4", l - 1, 256, 4), A("R0N"), LB, False, l == 4)
+            mm(A("ps4", l - 1, 256, 4), A("R0N"), LB, False, False)
+        for l in range(1, 5):
+            mm(A("ps4", l - 1, 256, 4), A("C0%d" % l), C, False, l == 4)
         for j in range(1, 8):
-            mm(A("ps5", j, 512, 8), A("TL", 128 * (j - 1), 128 * j), C)
-        ts(A("T613"), LB, -613.0, MUL, A("ACOL"), ADD)
-        tt(A("S0"), A("T613"), A("ST%d" % t), ADD)
-        ts(A("L0", 1, 128, 2), LB, -4.0, MUL, 16.0, ADD)
-        ts(A("SI"), A("S0"), W - 1, AND)
-        cp(A("OFFZ"), A("SI"))
-        act(A("A0"), A("ps4", 0, 256), ABS)
-        gz(actcp, 0, 0, Z_SCALAR[0])
-        gz(cp, 0, Z_SCALAR[0], 64)
-        scan(A("A0O"), A("M4"), A("A0"), ADD, MIN)
-        entries(A("A0O", 3, 256, 4), 0)
-        uwrap(0)
+            mm(A("ps5", j, 512, 8), A("TL%d" % (j - 1)), C)
         for h, ps in enumerate(("ps6", "ps3")):
             mm(A(ps, 0, 288, 9), A("NEG"), A("ONE", 0, 32))
             for j in range(1, 9):
-                mm(A(ps, j, 288, 9), A("TL", 128 * (6 + j), 128 * (7 + j)), A(lnd, 32 * h, 32 * h + 32))
-        ts(A("DA"), A("ps5"), -4.0, ADD)
-        act(A("NF"), A(F), IDT, 0.0, -1.0)
+                mm(A(ps, j, 288, 9), A("TL%d" % (6 + j)), A("C%d" % t, 32 * h, 32 * h + 32))
+        ts(A("T613"), LB, -613.0, MUL, A("ACOL"), ADD)
+        ts(A("L0", 1, 128, 2), LB, -4.0, MUL, 16.0, ADD)
+        tt(A("S0"), A("T613"), A("ST%d" % t), ADD)
+        ts(A("SI"), A("S0"), W - 1, AND)
+        cp(A("OFFZ"), A("SI"))
+        if t == 0:
+            weave(last_constants)
+        gz(actcp, 0, 0)
+        act(A("A0"), A("ps4", 0, 256), ABS)
+        gz(actcp, 0, 1)
+        gz(cp, 0, 0)
+        scan(A("A0O"), A("M4"), A("A0"), ADD, MIN)
+        uwrap(0)
+        ts(A("DA", 0, 256), A("ps5", 0, 256), -4.0, ADD)
+        entries(0, A("A0O", 3, 256, 4), 0)
+        ts(A("DA", 256, 512), A("ps5", 256, 512), -4.0, ADD)
         act(A("UA", 288, 576), A("ps3", 0, 288), IDT, -4.0)
+        act(A("NF"), F, IDT, 0.0, -1.0)
         for m in range(16):
             gcp(A("D2", 4 * m + 3, 4096, 64), A("NF"), 64)
         for k in range(1, 8):
-            arith(k - 1)
-            gz(actcp, k, 0, Z_SCALAR[k] if k < 7 else 32)
-            if k == 7:
-                gz(actcp, k, 32, Z_SCALAR[k])
+            arith(k - 1, lambda piece: maxima(2, 3 + piece, 8) if k == 7 else None)
+            for piece in range(len(Z_SCALAR[k]) - 1):
+                gz(actcp, k, piece)
             ustart()
             logmm(k - 1)
             if last:
                 ysum(19)
             if k == 6:
-                for h, ps in enumerate(("ps4", "ps5")):
-                    mm(A(ps), A("ID"), A("D2", 2048 * h + 3, 2048 * h + 2048, 4), True, False)
-            if k == 7:
+                mm(A("ps4"), A("ID"), A("D2", 3, 2048, 4), True, False)
+                mm(A("ps5", 0, 256), A("ID"), A("D2", 2048 + 3, 3072, 4), True, False)
+            if k < 7:
+                stairs(k, lambda piece: gz(cp, k, piece))
+            else:
                 mm(A("ps4"), A("I256"), A("O2", 3, 2048, 4), False, False)
-            stairs(k)
-            csum(k, C)
-            for j, q in PLAN.get(k, ([], []))[0]:
-                maxima(j, q)
-            gz(cp, k, Z_SCALAR[k], 64)
-            entries(A("psC", 0, 64), -64 if k == 1 else 64)
-            logact(k - 1)
-            if k == 7:
+                mm(A("psP", 0, 256), A("ID"), A("D2", 3072 + 3, 4096, 4), True, False)
+                stairs(k, lambda piece: maxima(2, 5 + piece, 8))
+                gz(cp, k, 0)
                 break
+            csum(k, C)
+            logact(k - 1)
             uwrap(k)
+            for j, q in PLAN.get(k, ())[:1]:
+                maxima(j, q)
+            if k == 6:
+                maxima(2, 0, 8)
+                maxima(2, 1, 8)
+            entries(k, A("psC", 0, 64), -64 if k == 1 else 64)
             if k == 1:
-                ts(A("UA", 0, 288), A("ps6", 0, 288), -4.0, ADD)
+                act(A("UA", 0, 288), A("ps6", 0, 288), IDT, -4.0)
                 act(A("LG", 9, 640, 10), LB, IDT, 4.0, -1.0)
             if k == 2:
                 act(A("WD", 1, 128, 2), LB, EXP, 9.0, -3.0)
-            for j, q in PLAN.get(k, ([], []))[1]:
+            for j, q in PLAN.get(k, ())[1:]:
                 maxima(j, q)
-            if t == 0 and k <= 5:
-                late_constants(k - 1)
+            if k == 6:
+                maxima(2, 2, 8)
+            if t == 0:
+                late_constants(k)
         mm(A("ps4"), A("ID"), A("Z7", 2, 2048, 4), False, True)
-        for q in (2, 3):
-            mm(A("ps5", 256 * q - 512, 256 * q - 256), A("I256"), A("O2", 1024 * q + 3, 1024 * q + 1024, 4),
-               False, False)
-        mm(A("ps5"), A("ID"), A("Z7", 2050, 4096, 4), False, True)
+        for q, ps in ((2, "ps5"), (3, "psP")):
+            if q == 3:
+                csum(7, C)
+            mm(A(ps, 0, 256), A("I256"), A("O2", 1024 * q + 3, 1024 * q + 1024, 4), False, False)
+            mm(A(ps, 0, 256), A("ID"), A("Z7", 1024 * q + 2, 1024 * q + 1024, 4), False, True)
         act(A("GEb", 0, 512), A("ps4"), SIGN, 256.5)
-        ts(A("GEb", 512, 1024), A("ps5"), -256.5, GE, -0.5, ADD)
+        for q, ps in ((2, "ps5"), (3, "psP")):
+            ts(A("GEb", 256 * q, 256 * q + 256), A(ps, 0, 256), -256.5, GE, -0.5, ADD)
+            if q == 2:
+                entries(7, A("psC", 0, 64), 64)
         uwrap(7)
         mm(A("ps6", 0, 128), A("I256"), A("TH2"), True, False)
         for m in range(16):
             mm(A("ps6", 0, 128, 2), A("Gm", m * 128, m * 128 + 128), A("GEb", m, 1024, 16), False, m == 15)
+        logact(6)
         act(A("PRE"), A("DP7", 1, 128, 2), IDT, 75.0, 2.0)
-        actcp(A("O2", 0, 4096, 64), A(F))
+        actcp(A("O2", 0, 4096, 64), F)
         tt(A("DH"), A("psW", 0, 64), A("CB4"), ADD)
         ts(A("N4"), A("DH"), 2, SHR, 3, AND)
         tt(A("LG", 1, 640, 10), A("PRE"), A("N4"), SUB)
@@ -500,39 +530,41 @@ def rank_program(g, core, T, topo):
         mm(A("psW", 0, 64), A("ID"), A("DG"), True, False)
         mm(A("psW", 0, 64), A("MV"), OH, False, True)
         mm(A("psW", 64, 128), A("BO3"), OH)
-        for l in range(5):
-            mm(A("ps4", l, 320, 5), A("TRI"), A("OHL", 9, 640, 10), False, l == 4)
         for s in range(8):
             mm(A("ps5", s, 512, 8), A("BO"), A("OHL", 1 + s, 640, 10))
+        for l in range(5):
+            mm(A("ps4", l, 320, 5), A("TRI"), A("OHL", 9, 640, 10), False, l == 4)
         scan(A("SD"), A("M16F"), A("psW", 0, 64), MUL, MAX)
         tt(A("EE"), A("psW", 64, 128), LB, MAX)
         cp(A("OV"), A("SD", 15, 64, 16))
+        for h in range(2):
+            act(A("AS", 256 * h, 256 * h + 256), A("ps5", 256 * h, 256 * h + 256), ABS, A("QB"))
         act(A("AL"), A("ps4", 0, 320), ABS)
-        act(A("AS"), A("ps5"), ABS, A("QB"))
         mm(A("ps6", 0, 64), A("ID"), A("DGX"), True, False)
         mm(A("ps6", 0, 64), A("BON"), A("KX") if last else OH, False, True)
         mm(A("psP", 0, 64), A("BO1" if last else "ONS"), OH)
         cp(A("VV6"), IND(A("O2"), A("OV")))
-        scan(A("ALO"), A("M5"), A("AL"), ADD, MIN)
+        scan(A("AO", 0, 256), A("M8", 0, 256), A("AS", 0, 256), ADD, MIN)
         tt(A("VV"), IND(A("Z7"), A("OV")), A("VV6"), MAX)
-        cp(A(snd, 0, 64), A("ALO", 4, 320, 5))
+        scan(A("AO", 256, 512), A("M8", 0, 256), A("AS", 256, 512), ADD, MIN)
         mm(A("psC", 0, 64), A("WB1"), A("VV"))
-        scan(A("AO"), A("M8"), A("AS"), ADD, MIN)
-        tt(A(snd, 64, 128), A("AO", 7, 512, 8), A("EE"), MIN)
+        tt(A("FVI"), F, A("VV"), ADD)
+        tt(A(sndL), A("AO", 7, 512, 8), A("EE"), MIN)
+        scan(A("ALO"), A("M5"), A("AL"), ADD, MIN)
+        cp(A("HI"), A("psC", 0, 64))
+        ts(A("FH"), A("FVI"), 1, SHR)
+        cp(A(sndC), A("ALO", 4, 320, 5))
         if not last:
-            out_total += send(snd, "LND%d" % (t + 1), "arr%d" % (t + 1), T.cores[(rank + 1) % n])
-            landed("LND%d" % (t + 1), "arr%d" % (t + 1), len(topo.engines(T.cores[(rank - 1) % n], core)))
+            send(sndL, "LB%d" % (t + 1), "arL%d" % (t + 1), 1)
+            send(sndC, "C%d" % (t + 1), "arC%d" % (t + 1), 1)
             act(A("PR"), A("psP", 0, 64), IDT, 4 * 613 / 64, 1.0, A("ACOL"))
         else:
-            act(A("YL"), A(snd, 64, 128), IDT, 4.0, -1.0)
-            dma("y", "oC", T.yc[:], T[snd][:, 0:64], [], [A(snd, 0, 64)])
+            act(A("YL"), A(sndL), IDT, 4.0, -1.0)
+            dma("y", "oC", T.yc[:], T[sndC][:], [], [A(sndC)])
             dma("y", "oL", T.yl[:], A("YL")[0], [], [A("YL")])
-        cp(A("HI"), A("psC", 0, 64))
-        tt(A("FVI"), A(F), A("VV"), ADD)
         ts(A("HM"), A("HI"), 127, AND)
-        ts(A("FH"), A("FVI"), 1, SHR)
-        tt(A("X1"), A("ps6", 0, 64), A("HM"), ADD)
         cp(A("F%d" % (t + 1)), A("FH"))
+        tt(A("X1"), A("ps6", 0, 64), A("HM"), ADD)
         scan(A("SD2"), A("M16F"), A("X1"), MUL, MAX)
         cp(A("OX"), A("SD2", 15, 64, 16))
         if not last:
@@ -549,7 +581,8 @@ def rank_program(g, core, T, topo):
         wait("g", "q" + q, count[q])
     for s in ("dX", "dW", "dC", "dL", "dS", "dF", "oL", "oC", "oF", "oS"):
         wait("g", s, 16)
-    wait("g", "loc", out_total)
+    wait("g", "loc", sent[0])
     for t in range(1, RO):
         wait("g", "st%d" % t, len(topo.engines(T.cores[(rank - t) % n], core)))
-        wait("g", "arr%d" % t, len(topo.engines(T.cores[(rank - 1) % n], core)))
+        for s in ("arC", "arL"):
+            wait("g", "%s%d" % (s, t), len(topo.engines(T.cores[(rank - 1) % n], core)))

@@ -7,7 +7,8 @@ SHR, AND = AluOpType.arith_shift_right, AluOpType.bitwise_and
 IDT, SIGN, ABS = ActivationFunctionType.Identity, ActivationFunctionType.Sign, ActivationFunctionType.Abs
 COPY, EXP = ActivationFunctionType.Copy, ActivationFunctionType.Exp
 RO, S, W = 4, 8, 8192
-BIG = 1024.0
+AGAIN = 3072
+DUMP = 2 * W
 
 SCRATCH = {}
 POOL = {}
@@ -24,47 +25,53 @@ def _pool(buf, names, cols, dtype):
     SCRATCH[buf] = ("sbuf", [128, len(names.split()) * cols], dtype)
 
 
-_d("X", 2 * W, "bfloat16")
+_d("X", DUMP + 2 * W, "bfloat16")
 _d("G0 G1 O0 O1", 3072, "bfloat16")
-_d("G2 O2 D2 Z7", 4096, "bfloat16")
+_d("G2 O2 D2", 4096, "bfloat16")
+_d("Z7", 2050, "bfloat16")
 _d("GEb", 1024, "bfloat16")
 _d("M3", 768, "bfloat16")
 _d("Gm Wm", 2048, "bfloat16")
 _pool("TL", " ".join("TL%d" % k for k in range(15)), 128, "bfloat16")
-_pool("MATS", "ID BO BO3 BO1 BON B256 WB1 SH1 SH2 SH3 SH4 C01 C02 C03 C04 R0N GT8 NEG ONS H9 H1 I256 ALF TRI MV NID "
-              "tm7 tm8 TH2 WD WO L0 QS DP0 DP1 DP2 DP3 DP4 DP5 DP6 DP7", 128, "bfloat16")
+_pool("MATS", "ID BO BO3 BO1 BON B256 WB1 SH1 SH2 SH3 SH4 GT0 GTN BM0 GT8 NEG ONS H9 H1 I256 ALF TRI T255 MV NID "
+              "N512 N101 tm7 tm8 TH2 WD WO L0 QS DP0 DP1 DP2 DP3 DP4 DP5 DP6 DP7", 128, "bfloat16")
 _pool("HMATS", "P64 N64 P32 N32", 128, "float16")
-_pool("SMALL", "ONE SP0 NF EE PRE VV6 VV DIF DG DGX KX YL", 64, "bfloat16")
+_pool("SMALL", "ONE SP0 NF EE PRE VV6 VV VW DIF DG DGX KX YL EQ0 SEL STH STL N4C NOK", 64, "bfloat16")
 _d("UA UB UO", 576, "float16")
 _d("DA DB DO", 512, "float16")
+_d("EA EB EO", 320, "float16")
 _d("LG LM OHL", 640, "bfloat16")
 _d("AS AO", 512, "bfloat16")
-_d("K5 M5 AL ALO", 320, "bfloat16")
-_d("K0 M4 M8 A0 A0O", 256, "bfloat16")
+_d("K5 M5 AL", 320, "bfloat16")
+_d("ALO", 320, "float16")
+_d("M8", 256, "bfloat16")
 _d("F0 F1 F2 F3 F4", 64, "bfloat16")
-_d("C0 C1 C2 C3 SC0 SC1 SC2 SC3 LB0 LB1 LB2 LB3 SL0 SL1 SL2 SL3", 64, "bfloat16")
+for _t in range(RO):
+    _pool("LND%d" % _t, "LB%d C%d" % (_t, _t), 64, "bfloat16")
+    _pool("SND%d" % _t, "SL%d SC%d" % (_t, _t), 64, "bfloat16")
 _d("WT", 1, "bfloat16")
 _d("ST0 ST1 ST2 ST3", 64, "int32")
-_pool("INTS", "N4 DH YI SI T613 S0 HI HM FVI FH", 64, "int32")
+_pool("INTS", "N4 DH YI SI S0 HI HM FVI FH SIH SIL", 64, "int32")
 _d("PI QI GI", 1, "int32")
 _d("ROWF CQF CGF", 128, "float32")
-_d("QC GC PC QB MW ACOL", 1, "float32")
+_d("QC GC PC QB MW Q4 XU XD HB PB ACOL", 1, "float32")
 _d("EQ16", 32, "float32")
 _pool("COEF", "CD0 CD1 CD2 CD3 CD4 CD5 CD6 CU0", 1, "float32")
 _d("CU MC", 8, "float32")
 _pool("FLTS", "CA CB4 PR M16F DIAG SD X1 X2 SD2", 64, "float32")
 _d("YS", 64, "float32")
 _d("OFFZ", 64, "uint16")
-_d("OV OX", 4, "uint16")
+_d("OV OZ", 4, "uint16")
+_d("OX", 8, "uint16")
 _d("psW psC psP ps3 ps4 ps5 ps6 psY", 512, "float32", "psum")
 
 SEMAPHORES = ["qv", "qs", "qt", "qg", "dX", "dW", "dC", "dL", "dS", "dF", "oC", "oL", "oF", "oS", "loc"]
-SEMAPHORES += ["%s%d" % (s, t) for s in ("st", "arC", "arL") for t in range(1, RO)]
+SEMAPHORES += ["%s%d" % (s, t) for s in ("st", "arr") for t in range(1, RO)]
 
-Z_SCALAR = {0: [0, 16, 34], 1: [0, 38], 7: [0, 32, 48, 54]}
-Z_VECTOR = {0: [34, 64], 1: [38, 44, 50, 64], 7: [54, 64]}
+Z_SCALAR = {0: [0, 34], 1: [0, 40], 7: [0, 32, 46]}
+Z_VECTOR = {0: [34, 50, 64], 1: [40, 48, 64], 7: [46, 64]}
 for _k in range(2, 7):
-    Z_SCALAR[_k], Z_VECTOR[_k] = [0, 46], [46, 52, 58, 64]
+    Z_SCALAR[_k], Z_VECTOR[_k] = [0, 44] if _k % 2 else [0, 16, 44], [44, 54, 64]
 
 
 class Ap(tuple):
@@ -145,10 +152,13 @@ def rank_program(g, core, T, topo):
         call().then_inc(T.sem[sem], 1)
         record(q, outs, ins, sem, count[q])
 
-    def weave(make, gap=4):
+    def collect(make):
         held.append([])
         make()
-        calls = held.pop()
+        return held.pop()
+
+    def spaced(make, gap=4):
+        calls = collect(make)
 
         def names(group):
             return {r[0] for x in group for r in x[1]}
@@ -159,7 +169,11 @@ def rank_program(g, core, T, topo):
             free = [i for i in range(len(calls)) if i not in done and all(j in done for j in before[i])]
             i = min(free, key=lambda i: (max([len(done)] + [done[j] + gap for j in before[i]]), i))
             done[i] = len(done)
-            run(*calls[i])
+        return [calls[i] for i in done]
+
+    def weave(make, gap=4):
+        for c in spaced(make, gap):
+            run(*c)
 
     def dma(q, sem, out, in_, outs, ins):
         deps(q, outs, ins)
@@ -224,29 +238,32 @@ def rank_program(g, core, T, topo):
 
     sent = [0]
 
-    def send(src, name, sem, hop):
+    def send(src, name, sem, hop, ins, outs):
         dst = T.cores[(rank + hop) % n]
         rid, pid, _ = topo.addr(dst)
-        deps("g", [], [A(src)])
+        deps("g", [], ins)
         g.remote_dma(out_ap=T[name][:], in_ap=T[src][:], remote_sem=T.sem[sem], local_sem=T.sem.loc,
                      pid=pid, routing_id=rid, dma_engine_mask=topo.mask(core, dst))
         sent[0] += len(topo.engines(core, dst))
-        record("net" + sem, [A(name)], [], sem, len(topo.engines(T.cores[(rank - hop) % n], core)))
+        record("net" + sem, outs, [], sem, len(topo.engines(T.cores[(rank - hop) % n], core)))
 
-    dma("s", "dS", T["ST0"][:], T.st[:], [A("ST0")], [])
-    dma("y", "dW", T["WT"][:], T.wt[:], [A("WT")], [])
+    dma("y", "dS", T["ST0"][:], T.st[:], [A("ST0")], [])
     dma("s", "dL", A("SP0")[0], T.sp[:], [A("SP0")], [])
-    dma("y", "dC", T["C0"][:], T.ch[:], [A("C0")], [])
     dma("y", "dX", T["X"][:, 0:W], T.x[:], [A("X", 0, W)], [])
+    dma("s", "dW", T["WT"][:], T.wt[:], [A("WT")], [])
+    dma("s", "dC", A("C0")[0], T.ch[:], [A("C0")], [])
     dma("s", "dF", T["F0"][:], T.fl[:], [A("F0")], [])
 
     iota(A("PI"), [[1, 1]], 1)
     iota(A("CGF"), [[1, 8], [0, 16]])
     iota(A("ROWF"), [[1, 128]])
     iota(A("CQF"), [[0, 8], [1, 16]])
-    iota(A("K0"), [[0, 64], [-256, 4]], 0, 768)
-    for t in range(1, RO):
-        send("ST0", "ST%d" % t, "st%d" % t, t)
+
+    def starts(t):
+        ts(A("SIH"), A("ST%d" % t), W - 128, AND)
+        ts(A("SIL"), A("ST%d" % t), 127, AND)
+        cp(A("STH"), A("SIH"))
+        cp(A("STL"), A("SIL"))
 
     def constants():
         fill(A("Gm"), 0.0)
@@ -257,17 +274,25 @@ def rank_program(g, core, T, topo):
         cp(A("QC"), A("QI"))
         ts(A("BO"), A("CGF"), A("GC"), EQ)
         ts(A("ID"), A("ROWF"), A("PC"), EQ)
+        ts(A("B256"), A("BO"), 256.0, MUL)
         ts(A("EQ16"), A("ROWF", 0, 32), A("QC"), EQ)
-        for name, x in (("NEG", -128.0), ("ONE", 1.0), ("L0", 0.0), ("DP0", 0.0), ("UB", 0.0), ("DB", 0.0),
-                        ("ACOL", 4.0 * 613)):
+        for name, x in (("NEG", -128.0), ("ONE", 1.0), ("L0", 0.0), ("N4C", -4.0), ("UB", 0.0), ("DB", 0.0), ("EB", 0.0),
+                        ("ACOL", 4.0 * 613), ("BM0", 0.0)):
             fill(A(name), x)
-        ts(A("MC"), A("ROWF", 0, 8), -1.0, MUL, A("QC"), ADD)
-        ts(A("MC"), A("MC"), 4.0, MUL)
-        for l in range(1, 5):
-            ts(A("C0%d" % l), A("BO"), A("EQ16", 0, 1), MUL)
-            ts(A("C0%d" % l, 0, 128, 16), A("BO", 0, 128, 16), A("EQ16", l, l + 1), MUL)
-        ts(A("R0N"), A("ID"), A("EQ16", 0, 1), MUL, -256.0, MUL)
-        ts(A("K0"), A("K0"), A("EQ16", 0, 1), MUL)
+        fill(A("Z7", 0, 2050, 2049), 0.0)
+        for name, x in (("NID", -1.0), ("N512", -512.0), ("N101", -101.0)):
+            ts(A(name), A("ID"), x, MUL)
+        ts(A("DP0", 1, 128, 2), A("ONE"), A("QC"), MUL, -4.0, MUL)
+        ts(A("GT0"), A("BO"), A("EQ16", 0, 1), MUL)
+        ts(A("LB0"), A("SP0"), -1.0, MUL, 4.0, ADD)
+        starts(0)
+
+    def first_places():
+        ts(A("S0"), A("psC", 0, 64), A("ACOL"), ADD)
+        ts(A("SI"), A("S0"), W - 1, AND)
+        cp(A("OFFZ"), A("SI"))
+
+    def step_constants():
         tt(A("CD0"), A("EQ16", 8, 9), A("EQ16", 7, 8), SUB)
         for j in range(1, 7):
             tt(A("CD%d" % j), A("EQ16", 9 - j, 10 - j), A("EQ16", 7 - j, 8 - j), SUB)
@@ -277,130 +302,145 @@ def rank_program(g, core, T, topo):
             j = k if k < 7 else k - 7
             col = A("CD%d" % j) if k < 7 else A("CU", j, j + 1) if j else A("CU0")
             ts(A("TL%d" % k), A("BO"), col, MUL, (-1.0) ** j / 64, MUL)
+        ts(A("GTN"), A("BO"), A("EQ16", 0, 1), MUL)
+        fill(A("GTN", 0, 128, 16), 0.0)
+        cp(A("BM0", 0, 128, 16), A("BO", 0, 128, 16))
+        ts(A("Q4"), A("QC"), -1.0, MUL, 4.0, ADD)
+        for name, x, y in (("XU", 4.0, -30.0), ("XD", -4.0, 34.0), ("HB", 8.0, 20.0), ("PB", 8.0, 19.0)):
+            ts(A(name), A("QC"), x, MUL, y, ADD)
         ts(A("GT8"), A("BO"), A("EQ16", 8, 9), MUL)
         for name, x in (("P64", 64.0), ("N64", -64.0), ("P32", 32.0), ("N32", -32.0), ("H9", 2.25), ("H1", -0.25)):
             ts(A(name), A("ID"), x, MUL)
-        ts(A("B256"), A("BO"), 256.0, MUL)
-        ts(A("LB0"), A("SP0"), -1.0, MUL, 4.0, ADD)
 
     def more_constants():
-        for name, x in (("ONS", 1.0 / 256), ("KX", 16.0), ("M16F", 1.0), ("TH2", 0.0)):
-            fill(A(name), x)
-        fill(A("M16F", 0, 64, 16), 0.0)
-        fill(A("WD", 0, 128, 2), -4194304.0)
-        fill(A("TH2", 0, 64, 2), -768.0)
-        fill(A("TH2", 64, 128, 2), -384.0)
-        for name, x in (("NID", -1.0), ("I256", 256.0)):
-            ts(A(name), A("ID"), x, MUL)
-        for name, x in (("BO3", 3.0 / 256), ("BO1", 1.0 / 256), ("BON", -32.0)):
-            ts(A(name), A("BO"), x, MUL)
-
-    def last_constants():
         ts(A("QB"), A("QC"), -8.0, MUL, -16.0, ADD)
         ts(A("MW"), A("QC"), 4.0 / 256, MUL, 2.0 / 256, ADD)
         ts(A("MV"), A("BO"), A("MW"), MUL)
         ts(A("WB1"), A("BO"), A("WT"), MUL)
         ts(A("DIAG"), A("CQF", 0, 64), A("QC"), EQ)
-        for name, x, y, tmp in (("DG", 64.0, 0.0, "X1"), ("DGX", 128.0, 8192.0, "X2")):
+        for name, x, y, tmp in (("DG", 64.0, 0.0, "X1"), ("DGX", 128.0, DUMP, "X2")):
             ts(A(tmp), A("ROWF", 0, 64), x, MUL, y + 32768.0, ADD)
             tt(A(tmp), A(tmp), A("DIAG"), MUL)
             ts(A(name), A(tmp), -32768.0, ADD)
+        for name, x in (("ONS", 1.0 / 256), ("KX", 16.0), ("M16F", 1.0), ("TH2", 0.0)):
+            fill(A(name), x)
+        fill(A("WD", 0, 128, 2), -4194304.0)
+        ts(A("I256"), A("ID"), 256.0, MUL)
+        ts(A("T255"), A("TRI"), 255.0 / 256, MUL)
+        for name, x in (("BO3", 3.0 / 256), ("BO1", 1.0 / 256), ("BON", -DUMP / 256)):
+            ts(A(name), A("BO"), x, MUL)
+        fill(A("M16F", 0, 64, 16), 0.0)
+        fill(A("TH2", 0, 64, 2), -768.0)
+        fill(A("TH2", 64, 128, 2), -384.0)
+        starts(1)
     weave(constants)
     for m in range(16):
         act(A("Gm", m * 129, m * 128 + 128, 16), A("BO", 0, 128, 16), IDT, 0.0, 65536.0)
-    ts(A("Wm"), A("Gm"), A("WT"), MUL, 0.5 / 65536, MUL)
-    for h in range(2):
-        act(A("Z7", 2048 * h, 2048 * h + 2048), A("Gm"), IDT, 0.0, 0.0)
-    resets("M4", 256, 4, 1024, 0)
-    resets("M3", 768, 3, 0, 1)
-    for l in range(1, 5):
-        pick(A("SH%d" % l), A("BO"), [[-1, 128]], EQ, 0.0, -l, 1)
     pick(A("TRI"), A("B256"), [[1, 128]], GE, 0.0, 0, -1)
     pick(A("tm7"), A("BO"), [[1, 128]], GT, 1.0 / 16, 0, -1)
     pick(A("tm8"), A("tm7"), [[1, 128]], NE, -31.0 / 32, 0, -1)
+    for t in range(1, RO):
+        send("ST0", "ST%d" % t, "st%d" % t, t, [A("ST0")], [A("ST%d" % t)])
+    resets("M3", 768, 3, 0, 1)
+    for l in range(1, 5):
+        pick(A("SH%d" % l), A("BO"), [[-1, 128]], EQ, 0.0, -l, 1)
     iota(A("K5"), [[0, 64], [-256, 5]])
-    resets("M5", 320, 5, 1024, 0)
-    iota(A("D2", 0, 4096, 4), [[0, 1024]], 0, -1024)
+    resets("M5", 320, 5, 0, 1)
+    resets("M8", 256, 8, 1024, 0)
+    resets("LM", 640, 10, 1024, 0)
+    waiting = spaced(more_constants)
+
+    def spare():
+        for _ in range(min(2, len(waiting))):
+            run(*waiting.pop(0))
 
     def late_constants(k):
         if k == 1:
-            iota(A("D2", 1, 4096, 4), [[0, 1024]])
-            resets("M8", 256, 8, 1024, 0)
-            weave(more_constants)
-        if k == 2:
-            iota(A("D2", 2, 4096, 4), [[0, 1024]])
             tt(A("ALF"), A("tm8"), A("BO"), MUL)
-        if k == 3:
-            iota(A("G2", 3, 4096, 4), [[0, 1024]], 0, -1)
-        if k == 4:
-            resets("LM", 640, 10, 1024, 0)
+            spare()
+            spare()
+        if k in (0, 1, 2, 4):
+            name, slot, x = {0: ("D2", 0, -1024.0), 1: ("D2", 1, 0.0), 2: ("D2", 2, 0.0), 4: ("G2", 3, -1.0)}[k]
+            act(A(name, slot, 4096, 4), A("Gm", 0, 1024), IDT, x, 0.0)
+        if k >= 5:
+            a = 1024 * (k - 5)
+            actcp(A("X", W + a, W + a + 1024), A("X", a, a + 1024))
 
     ZAT = [("G0", 3, 0), ("G0", 3, 1), ("G0", 3, 2), ("G1", 3, 1), ("G1", 3, 2), ("G2", 4, 1), ("G2", 4, 2),
-           ("Z7", 4, 2)]
+           ("Z7", 2, 2)]
 
-    def gz(eng, k, piece):
+    def gz(eng, k, piece, width=W):
         i0, i1 = (Z_SCALAR if eng is actcp else Z_VECTOR)[k][piece:piece + 2]
-        if i0 < i1:
-            b, s, o = ZAT[k]
-            eng(A(b, 16 * s * i0 + o, 16 * s * i1, s), IND(A("X", 0, W), A("OFFZ", i0, i1)))
+        b, s, o = ZAT[k]
+        eng(A(b, 16 * s * i0 + o, 16 * s * i1 + o - s + 1, s), IND(A("X", 0, width), A("OFFZ", i0, i1)))
 
-    def ustart():
+    def ustart(k):
+        if k < 7:
+            mm(A("psW", 64, 128), A("NID"), A("DP%d" % k, 1, 128, 2), True, False)
+            mm(A("psW", 64, 128), A("ID"), A("N4C"), False, True)
         mm(A("psW", 0, 64), A("NEG"), A("ONE"), True, False)
 
     def uwrap(k):
         b, s, o = ZAT[k]
         for m in range(16):
-            mm(A("psW", 0, 64), A("Wm", m * 128, m * 128 + 128), A(b, s * m + o, 1024 * s, 16 * s), False, m == 15)
+            mm(A("psW", 0, 64), A("Wm", m * 128, m * 128 + 128), A(b, s * m + o, 1024 * s + o - s + 1, 16 * s),
+               False, m == 15)
 
     def entries(k, src, off):
         ts(A("CB4"), src, 4.0, MUL, 16383.75 + 4 * off, ADD)
         if k < 7:
             ts(A("CA"), src, 2.0, MUL, 296.0 + 2 * off, ADD)
-            ts(A("psP", 64, 128), A("DP%d" % k, 1, 128, 2), -1.0, MUL, A("MC", k + 1, k + 2), ADD)
 
-    def maxima(j, q, parts=4):
+    def maxima(j, q):
         if j < 2:
             r = (768 * q, 768 * q + 768)
             scan(A("O%d" % j, *r), A("M3"), A("G%d" % j, *r), MUL, MAX)
             s = 3 + j
             gcp(A("G%d" % (j + 1), 256 * s * q, 256 * s * (q + 1), s), A("O%d" % j, r[0] + 2, r[1], 3), 256)
         else:
-            r = (4096 // parts * q, 4096 // parts * (q + 1))
+            r = (512 * q, 512 * q + 512)
             scan(A("O2", *r), A("D2", *r), A("G2", *r), ADD, MAX)
 
     def arith(k, between):
-        old, nx = "DP%d" % k, "DP%d" % (k + 1)
+        nx = "DP%d" % (k + 1)
         tt(A("DH"), A("psW", 0, 64), A("CB4"), ADD)
         tt(A("psP", 0, 64), A("psW", 0, 64), A("CA"), MUL)
         between(0)
         ts(A("N4"), A("DH"), 12, AND)
         tt(A("YI"), A("psP", 0, 64), A("DH"), ADD)
         between(1)
-        tt(A(nx, 0, 128, 2), A("N4"), A("psP", 64, 128), GE)
-        ts(A("SI"), A("YI"), 2, SHR, W - 1, AND)
-        tt(A(nx, 1, 128, 2), A(old, 1, 128, 2), A("N4"), ADD)
-        cp(A("OFFZ"), A("SI"))
+        tt(A(nx, 0, 128, 2), A("N4"), A("psW", 64, 128), GE)
+        entry = collect(lambda: (
+            tt(A(nx, 1, 128, 2), A("N4"), A("psW", 64, 128), SUB),
+            scan(A("QS"), A("L0"), A(nx), MUL, ADD)))
+        place = collect(lambda: (ts(A("SI"), A("YI"), 2, SHR, W - 1, AND), cp(A("OFFZ"), A("SI"))))
+        for pair in zip(entry, place) if k < 6 else zip(place, entry):
+            for call in pair:
+                run(*call)
 
-    def stairs(k, between):
-        scan(A("QS"), A("L0"), A("DP%d" % k), MUL, ADD)
+    def heights(k, between):
         between(0)
         if k > 1:
-            ts(A("UB", 0, 576, 9), A("QS", 1, 128, 2), 4.0 * k - 30, ADD, 34.0, MIN)
-        ts(A("DB", 0, 512, 8), A("QS", 1, 128, 2), -1.0, MUL, 34.0 - 4 * k, ADD)
+            ts(A("UB", 0, 576, 9), A("QS", 1, 128, 2), A("XU"), ADD, 34.0, MIN)
+        d, s = ("D", 8) if k < 4 else ("E", 5)
+        ts(A(d + "B", 0, 64 * s, s), A("QS", 1, 128, 2), -1.0, MUL, A("XD"), ADD)
         between(1)
+
+    def stairs(k):
         if k > 1:
             scan(A("UO"), A("UA"), A("UB"), ADD, MAX)
-        scan(A("DO"), A("DA"), A("DB"), ADD, MAX)
-        between(2)
+        d = "D" if k < 4 else "E"
+        scan(A(d + "O"), A(d + "A"), A(d + "B"), ADD, MAX)
 
     def csum(k, C):
         terms = [(A("GT8"), C)]
         if k == 1:
-            terms += [(A("P32"), A("DO", 0, 512, 8))]
+            terms += [(A("P32"), A("DB", 0, 512, 8))]
         else:
-            terms += [(A("N32"), A("UO", 0, 576, 9))]
+            terms += [(A("N32"), A("UB", 0, 576, 9))]
             terms += [(A("P64" if j % 2 else "N64"), A("UO", j, 576, 9)) for j in range(1, 5 if k == 2 else 9)]
-        terms += [(A("N64" if j % 2 else "P64"), A("DO", j, 512, 8)) for j in range(1, 9 - k)]
+        terms += [(A("N64" if j % 2 else "P64"), A("DO", j, 512, 8) if k < 4 else A("EO", j, 320, 5))
+                  for j in range(1, 9 - k)]
         for j, (l, r) in enumerate(terms):
             mm(A("psC", 0, 64), l, r, j == 0, j == len(terms) - 1)
 
@@ -409,180 +449,233 @@ def rank_program(g, core, T, topo):
         mm(A("ps3", 0, 64), A("H1"), A("DP%d" % (k + 1), 1, 128, 2), False, True)
 
     def logact(k):
-        act(A("LG", 8 - k, 640, 10), A("ps3", 0, 64), IDT, 8.0 * k + 19)
+        act(A("LG", 8 - k, 640, 10), A("ps3", 0, 64), IDT, A("HB"))
 
     ysn = [0]
 
     def ysum(cnt):
-        for _ in range(cnt):
+        for _ in range(min(cnt, 128 - ysn[0])):
             c = ysn[0]
-            if c < 128:
-                mm(A("psY", 0, 64), A("ID"), A("X", c, W, 128), c == 0, False)
-                ysn[0] += 1
+            mm(A("psY", 0, 64), A("ID"), A("X", c, W, 128), c == 0, c == 127)
+            ysn[0] += 1
 
-    PLAN = {2: [(0, 0), (0, 1)], 3: [(0, 2), (0, 3)], 4: [(1, 0), (1, 1)], 5: [(1, 2), (1, 3)]}
+    PLAN = {2: [(0, 0), (0, 1)], 3: [(0, 2), (0, 3)], 4: [(1, 0), (1, 1)], 5: [(1, 2), (1, 3)],
+            6: [(2, 0), (2, 1), (2, 2)]}
 
     for t in range(RO):
         last = t == RO - 1
         C, LB, F = A("C%d" % t), A("LB%d" % t), A("F%d" % t)
         sndC, sndL = "SC%d" % t, "SL%d" % t
-        ustart()
-        mm(A("ps4", 0, 256), A("ID"), A("K0"), True, False)
+        ustart(0)
         mm(A("ps5", 0, 512, 8), A("NEG"), A("ONE"))
-        for l in range(1, 5):
-            mm(A("ps4", l - 1, 256, 4), A("R0N"), LB, False, False)
-        for l in range(1, 5):
-            mm(A("ps4", l - 1, 256, 4), A("C0%d" % l), C, False, l == 4)
+        mm(A("psC", 0, 64), A("ID"), A("STH"), True, False)
+        mm(A("psC", 0, 64), A("ID"), A("STL"), False, False)
+        mm(A("psC", 0, 64), A("N512"), LB, False, False)
+        mm(A("psC", 0, 64), A("N101"), LB, False, True)
+        mm(A("ps4", 0, 64), A("GT0"), LB)
+        act(A("NF"), F, IDT, 0.0, -1.0)
+        if t == 0:
+            rest = spaced(step_constants)
+            for j, call in enumerate(collect(first_places)):
+                for c in [call] + rest[4 * j:4 * j + 4 if j < 2 else None]:
+                    run(*c)
+            act(A("WD", 1, 128, 2), LB, EXP, 9.0, -3.0)
+            late_constants(0)
+        else:
+            ts(A("OFFZ"), A("psC", 0, 64), A("ACOL"), ADD)
         for j in range(1, 8):
             mm(A("ps5", j, 512, 8), A("TL%d" % (j - 1)), C)
         for h, ps in enumerate(("ps6", "ps3")):
             mm(A(ps, 0, 288, 9), A("NEG"), A("ONE", 0, 32))
             for j in range(1, 9):
                 mm(A(ps, j, 288, 9), A("TL%d" % (6 + j)), A("C%d" % t, 32 * h, 32 * h + 32))
-        ts(A("T613"), LB, -613.0, MUL, A("ACOL"), ADD)
         ts(A("L0", 1, 128, 2), LB, -4.0, MUL, 16.0, ADD)
-        tt(A("S0"), A("T613"), A("ST%d" % t), ADD)
-        ts(A("SI"), A("S0"), W - 1, AND)
-        cp(A("OFFZ"), A("SI"))
+        ts(A("EQ0"), A("ps4", 0, 64), A("Q4"), EQ)
         if t == 0:
-            weave(last_constants)
-        gz(actcp, 0, 0)
-        act(A("A0"), A("ps4", 0, 256), ABS)
-        gz(actcp, 0, 1)
-        gz(cp, 0, 0)
-        scan(A("A0O"), A("M4"), A("A0"), ADD, MIN)
+            ts(A("Wm"), A("Gm"), A("WT"), MUL, 0.5 / 65536, MUL)
+        gz(actcp, 0, 0, W + AGAIN if t else W)
+        gz(cp, 0, 0, W + AGAIN if t else W)
+        tt(A("SEL"), A("EQ0"), C, MUL)
+        gz(cp, 0, 1, W + AGAIN if t else W)
+        mm(A("ps4", 0, 64), A("GTN"), C, True, False)
+        mm(A("ps4", 0, 64), A("BM0"), A("SEL"), False, True)
         uwrap(0)
         ts(A("DA", 0, 256), A("ps5", 0, 256), -4.0, ADD)
-        entries(0, A("A0O", 3, 256, 4), 0)
+        entries(0, A("ps4", 0, 64), 0)
         ts(A("DA", 256, 512), A("ps5", 256, 512), -4.0, ADD)
         act(A("UA", 288, 576), A("ps3", 0, 288), IDT, -4.0)
-        act(A("NF"), F, IDT, 0.0, -1.0)
+        if t == 0:
+            act(A("Z7", 1, 2049, 2), A("Gm", 0, 1024), IDT, 0.0, 0.0)
         for m in range(16):
             gcp(A("D2", 4 * m + 3, 4096, 64), A("NF"), 64)
         for k in range(1, 8):
-            arith(k - 1, lambda piece: maxima(2, 3 + piece, 8) if k == 7 else None)
+            arith(k - 1, lambda piece: maxima(2, 3 + piece) if k == 7 else spare())
             for piece in range(len(Z_SCALAR[k]) - 1):
                 gz(actcp, k, piece)
-            ustart()
+            ustart(k)
             logmm(k - 1)
             if last:
                 ysum(19)
             if k == 6:
                 mm(A("ps4"), A("ID"), A("D2", 3, 2048, 4), True, False)
                 mm(A("ps5", 0, 256), A("ID"), A("D2", 2048 + 3, 3072, 4), True, False)
-            if k < 7:
-                stairs(k, lambda piece: gz(cp, k, piece))
-            else:
-                mm(A("ps4"), A("I256"), A("O2", 3, 2048, 4), False, False)
-                mm(A("psP", 0, 256), A("ID"), A("D2", 3072 + 3, 4096, 4), True, False)
-                stairs(k, lambda piece: maxima(2, 5 + piece, 8))
-                gz(cp, k, 0)
+            if k == 7:
                 break
+            heights(k, lambda piece: gz(cp, k, 0) if piece else None)
+            stairs(k)
+            gz(cp, k, 1)
             csum(k, C)
-            logact(k - 1)
+            if k < 6:
+                logact(k - 1)
             uwrap(k)
-            for j, q in PLAN.get(k, ())[:1]:
+            for j, q in PLAN.get(k, ())[:-1]:
                 maxima(j, q)
-            if k == 6:
-                maxima(2, 0, 8)
-                maxima(2, 1, 8)
-            entries(k, A("psC", 0, 64), -64 if k == 1 else 64)
+            if k < 6:
+                entries(k, A("psC", 0, 64), -64 if k == 1 else 64)
+            else:
+                act(A("CB4"), A("psC", 0, 64), IDT, 16383.75 + 4 * 64, 4.0)
+                act(A("CA"), A("psC", 0, 64), IDT, 296.0 + 2 * 64, 2.0)
+                logact(5)
             if k == 1:
                 act(A("UA", 0, 288), A("ps6", 0, 288), IDT, -4.0)
                 act(A("LG", 9, 640, 10), LB, IDT, 4.0, -1.0)
-            if k == 2:
+                if t and not last:
+                    weave(lambda: starts(t + 1), 2)
+            if k == 2 and t:
                 act(A("WD", 1, 128, 2), LB, EXP, 9.0, -3.0)
-            for j, q in PLAN.get(k, ())[1:]:
+            if k == 3:
+                for j in range(5):
+                    actcp(A("EA", j, 320, 5), A("DA", j, 512, 8))
+            for j, q in PLAN.get(k, ())[-1:]:
                 maxima(j, q)
-            if k == 6:
-                maxima(2, 2, 8)
             if t == 0:
                 late_constants(k)
-        mm(A("ps4"), A("ID"), A("Z7", 2, 2048, 4), False, True)
+        mm(A("ps6", 0, 128), A("I256"), A("TH2"), True, False)
+        mm(A("ps4"), A("I256"), A("O2", 3, 2048, 4), False, False)
+        mm(A("psP", 0, 256), A("ID"), A("D2", 3072 + 3, 4096, 4), True, False)
+        heights(7, lambda piece: maxima(2, 5 + piece))
+        maxima(2, 7)
+        gz(cp, 7, 0)
+        stairs(7)
+        mm(A("ps5", 0, 256), A("I256"), A("O2", 2048 + 3, 3072, 4), False, False)
+        mm(A("ps4"), A("ID"), A("Z7", 2, 1025, 2), False, True)
+        mm(A("psP", 0, 256), A("I256"), A("O2", 3072 + 3, 4096, 4), False, False)
         for q, ps in ((2, "ps5"), (3, "psP")):
-            if q == 3:
-                csum(7, C)
-            mm(A(ps, 0, 256), A("I256"), A("O2", 1024 * q + 3, 1024 * q + 1024, 4), False, False)
-            mm(A(ps, 0, 256), A("ID"), A("Z7", 1024 * q + 2, 1024 * q + 1024, 4), False, True)
+            mm(A(ps, 0, 256), A("ID"), A("Z7", 512 * q + 2, 512 * q + 513, 2), False, True)
         act(A("GEb", 0, 512), A("ps4"), SIGN, 256.5)
         for q, ps in ((2, "ps5"), (3, "psP")):
             ts(A("GEb", 256 * q, 256 * q + 256), A(ps, 0, 256), -256.5, GE, -0.5, ADD)
-            if q == 2:
-                entries(7, A("psC", 0, 64), 64)
+        csum(7, C)
         uwrap(7)
-        mm(A("ps6", 0, 128), A("I256"), A("TH2"), True, False)
+        entries(7, A("psC", 0, 64), 64)
         for m in range(16):
             mm(A("ps6", 0, 128, 2), A("Gm", m * 128, m * 128 + 128), A("GEb", m, 1024, 16), False, m == 15)
         logact(6)
-        act(A("PRE"), A("DP7", 1, 128, 2), IDT, 75.0, 2.0)
+        act(A("PRE"), A("DP7", 1, 128, 2), IDT, A("PB"), 2.0)
         actcp(A("O2", 0, 4096, 64), F)
+        if t == 0:
+            late_constants(7)
         tt(A("DH"), A("psW", 0, 64), A("CB4"), ADD)
         ts(A("N4"), A("DH"), 2, SHR, 3, AND)
-        tt(A("LG", 1, 640, 10), A("PRE"), A("N4"), SUB)
         scan(A("WO"), A("WD"), A("ps6", 0, 128), MIN, MAX)
+        tt(A("LG", 1, 640, 10), A("PRE"), A("N4"), SUB)
         mm(A("ps4", 0, 320), A("ID"), A("K5"), True, False)
+        mm(A("psW", 0, 64), A("ID"), A("DG"), True, False)
         mm(A("psC", 0, 64), A("ALF"), A("WO", 1, 128, 2))
         OH = A("LG", 0, 640, 10)
         ts(OH, A("psC", 0, 64), 0.0, LT, 256.0, MUL)
         for l in range(5):
             mm(A("ps4", l, 320, 5), A("SH%d" % l if l else "ID"), C, False, False)
-        scan(A("OHL"), A("LM"), A("LG"), ADD, MIN)
-        mm(A("psW", 0, 64), A("ID"), A("DG"), True, False)
+        mm(A("ps6", 0, 64), A("ID"), A("DGX"), True, False)
         mm(A("psW", 0, 64), A("MV"), OH, False, True)
         mm(A("psW", 64, 128), A("BO3"), OH)
-        for s in range(8):
-            mm(A("ps5", s, 512, 8), A("BO"), A("OHL", 1 + s, 640, 10))
-        for l in range(5):
-            mm(A("ps4", l, 320, 5), A("TRI"), A("OHL", 9, 640, 10), False, l == 4)
-        scan(A("SD"), A("M16F"), A("psW", 0, 64), MUL, MAX)
-        tt(A("EE"), A("psW", 64, 128), LB, MAX)
-        cp(A("OV"), A("SD", 15, 64, 16))
-        for h in range(2):
-            act(A("AS", 256 * h, 256 * h + 256), A("ps5", 256 * h, 256 * h + 256), ABS, A("QB"))
-        act(A("AL"), A("ps4", 0, 320), ABS)
-        mm(A("ps6", 0, 64), A("ID"), A("DGX"), True, False)
         mm(A("ps6", 0, 64), A("BON"), A("KX") if last else OH, False, True)
         mm(A("psP", 0, 64), A("BO1" if last else "ONS"), OH)
-        cp(A("VV6"), IND(A("O2"), A("OV")))
-        scan(A("AO", 0, 256), A("M8", 0, 256), A("AS", 0, 256), ADD, MIN)
-        tt(A("VV"), IND(A("Z7"), A("OV")), A("VV6"), MAX)
-        scan(A("AO", 256, 512), A("M8", 0, 256), A("AS", 256, 512), ADD, MIN)
-        mm(A("psC", 0, 64), A("WB1"), A("VV"))
-        tt(A("FVI"), F, A("VV"), ADD)
-        tt(A(sndL), A("AO", 7, 512, 8), A("EE"), MIN)
-        scan(A("ALO"), A("M5"), A("AL"), ADD, MIN)
-        cp(A("HI"), A("psC", 0, 64))
-        ts(A("FH"), A("FVI"), 1, SHR)
-        cp(A(sndC), A("ALO", 4, 320, 5))
+
+        def choose():
+            scan(A("OHL"), A("LM"), A("LG"), ADD, MIN)
+            for s in range(8):
+                mm(A("ps5", s, 512, 8), A("BO"), A("OHL", 1 + s, 640, 10))
+            for l in range(5):
+                mm(A("ps4", l, 320, 5), A("TRI"), A("OHL", 9, 640, 10), False, l == 4)
+            mm(A("ps4", 320, 384), A("T255"), A("OHL", 9, 640, 10))
+            for h in range(2):
+                act(A("AS", 256 * h, 256 * h + 256), A("ps5", 256 * h, 256 * h + 256), ABS, A("QB"))
+
+        def spans(h):
+            scan(A("AO", 256 * h, 256 * h + 256), A("M8"), A("AS", 256 * h, 256 * h + 256), ADD, MIN)
+
         if not last:
-            send(sndL, "LB%d" % (t + 1), "arL%d" % (t + 1), 1)
-            send(sndC, "C%d" % (t + 1), "arC%d" % (t + 1), 1)
+            choose()
+            scan(A("SD"), A("M16F"), A("psW", 0, 64), MUL, MAX)
+            tt(A("ps3", 0, 64), A("psW", 64, 128), LB, MAX)
+            cp(A("OV"), A("SD", 15, 64, 16))
+            ts(A("OZ"), A("SD", 15, 64, 16), 0.5, MUL, 1.0, ADD)
             act(A("PR"), A("psP", 0, 64), IDT, 4 * 613 / 64, 1.0, A("ACOL"))
+            cp(A("VV6"), IND(A("O2"), A("OV")))
+            ts(A("AL"), A("ps4", 0, 320), 0.0, MAX, 255.0, MIN)
+            tt(A("VV"), IND(A("Z7"), A("OZ")), A("VV6"), MAX)
+            mm(A("psC", 0, 64), A("WB1"), A("VV"))
+            spans(0)
+            scan(A("ALO"), A("M5"), A("AL"), MUL, ADD)
+            spans(1)
+            actcp(A("VW"), A("VV"))
+            tt(A(sndC), A("ALO", 4, 320, 5), A("ps4", 320, 384), SUB)
+            cp(A("HI"), A("psC", 0, 64))
+            tt(A(sndL), A("AO", 7, 512, 8), A("ps3", 0, 64), MIN)
+            send("SND%d" % t, "LND%d" % (t + 1), "arr%d" % (t + 1), 1, [A(sndL), A(sndC)],
+                 [A("LB%d" % (t + 1)), A("C%d" % (t + 1))])
+            ts(A("HM"), A("HI"), 127, AND)
+            tt(A("FVI"), F, A("VV"), ADD)
+            tt(A("X1"), A("ps6", 0, 64), A("HM"), ADD)
+            ts(A("FH"), A("FVI"), 1, SHR)
+            scan(A("SD2"), A("M16F"), A("X1"), MUL, MAX)
+            cp(A("F%d" % (t + 1)), A("FH"))
+            cp(A("OX", 0, 4), A("SD2", 15, 64, 16))
+            ts(A("OX", 4, 8), A("SD2", 15, 64, 16), float(W), ADD)
+            twice = Ap((T["SMALL"][:, POOL["VV"][1]:POOL["VV"][1] + 128], A("VV")[1] + A("VW")[1]))
+            cp(IND(A("X"), A("OX")), twice)
         else:
+            scan(A("SD"), A("M16F"), A("psW", 0, 64), MUL, MAX)
+            choose()
+            cp(A("OV"), A("SD", 15, 64, 16))
+            ts(A("OZ"), A("SD", 15, 64, 16), 0.5, MUL, 1.0, ADD)
+            tt(A("EE"), A("psW", 64, 128), LB, MAX)
+            cp(A("VV6"), IND(A("O2"), A("OV")))
+            cp(A("NOK"), A("psP", 0, 64))
+            tt(A("VV"), IND(A("Z7"), A("OZ")), A("VV6"), MAX)
+            mm(A("psC", 0, 64), A("WB1"), A("VV"))
+            ts(A("AL"), A("ps4", 0, 320), 0.0, MAX, 255.0, MIN)
+            tt(A("FVI"), F, A("VV"), ADD)
+            cp(A("HI"), A("psC", 0, 64))
+            spans(0)
+            ts(A("FH"), A("FVI"), 1, SHR)
+            ts(A("HM"), A("HI"), 127, AND)
+            tt(A("DIF"), A("VV"), A("psP", 0, 64), MUL)
+            spans(1)
+            tt(A("X1"), A("ps6", 0, 64), A("HM"), ADD)
+            cp(A("F4"), A("FH"))
+            scan(A("ALO"), A("M5"), A("AL"), MUL, ADD)
+            scan(A("SD2"), A("M16F"), A("X1"), MUL, MAX)
+            tt(A(sndL), A("AO", 7, 512, 8), A("EE"), MIN)
+            tt(A(sndC), A("ALO", 4, 320, 5), A("ps4", 320, 384), SUB)
+            cp(A("OX", 0, 4), A("SD2", 15, 64, 16))
+            tt(A("psP", 64, 128), A("psY", 0, 64), A("DIF"), ADD)
             act(A("YL"), A(sndL), IDT, 4.0, -1.0)
-            dma("y", "oC", T.yc[:], T[sndC][:], [], [A(sndC)])
-            dma("y", "oL", T.yl[:], A("YL")[0], [], [A("YL")])
-        ts(A("HM"), A("HI"), 127, AND)
-        cp(A("F%d" % (t + 1)), A("FH"))
-        tt(A("X1"), A("ps6", 0, 64), A("HM"), ADD)
-        scan(A("SD2"), A("M16F"), A("X1"), MUL, MAX)
-        cp(A("OX"), A("SD2", 15, 64, 16))
-        if not last:
-            cp(IND(A("X"), A("OX")), A("VV"))
-        else:
+            tt(A("SEL"), IND(A("X", 0, W), A("OX", 0, 4)), A("NOK"), MUL)
+            tt(A("YS"), A("psP", 64, 128), A("SEL"), SUB)
             dma("y", "oF", T.yf[:], T["F4"][:], [], [A("F4")])
-            tt(A("PR"), IND(A("X", 0, W), A("OX")), A("VV"), SUB)
-            tt(A("DIF"), A("PR"), A("psP", 0, 64), MUL)
-            mm(A("psY", 0, 64), A("NID"), A("DIF"), False, True)
-            cp(A("YS"), A("psY", 0, 64))
+            dma("y", "oC", T.yc[:], A(sndC)[0], [], [A(sndC)])
+            dma("s", "oL", T.yl[:], A("YL")[0], [], [A("YL")])
             dma("y", "oS", T.ys[:], T["YS"][:], [], [A("YS")])
 
-    for q in "vstg":
-        wait("g", "q" + q, count[q])
-    for s in ("dX", "dW", "dC", "dL", "dS", "dF", "oL", "oC", "oF", "oS"):
-        wait("g", s, 16)
     wait("g", "loc", sent[0])
     for t in range(1, RO):
         wait("g", "st%d" % t, len(topo.engines(T.cores[(rank - t) % n], core)))
-        for s in ("arC", "arL"):
-            wait("g", "%s%d" % (s, t), len(topo.engines(T.cores[(rank - 1) % n], core)))
+        wait("g", "arr%d" % t, len(topo.engines(T.cores[(rank - 1) % n], core)))
+    for s in ("dX", "dW", "dC", "dL", "dS", "dF"):
+        wait("g", s, 16)
+    for q in "gtsv":
+        wait("g", "q" + q, count[q])
+    for s in ("oF", "oC", "oL", "oS"):
+        wait("g", s, 16)

@@ -32,14 +32,14 @@ _d("Z7", 2050, "bfloat16")
 _d("GEb", 1024, "bfloat16")
 _d("M3", 768, "bfloat16")
 _d("Gm Wm", 2048, "bfloat16")
-_pool("TL", " ".join("TL%d" % k for k in range(15)), 128, "bfloat16")
-_pool("MATS", "ID BO BO3 BO1 BON B256 WB1 SH1 SH2 SH3 SH4 GT0 GTN BM0 GT8 NEG ONS H9 H1 I256 ALF TRI T255 MV NID "
-              "N512 N101 tm7 tm8 TH2 WD WO L0 QS DP0 DP1 DP2 DP3 DP4 DP5 DP6 DP7", 128, "bfloat16")
-_pool("HMATS", "P64 N64 P32 N32", 128, "float16")
-_pool("SMALL", "ONE SP0 NF EE PRE VV6 VV VW DIF DG DGX KX YL EQ0 SEL STH STL N4C NOK", 64, "bfloat16")
-_d("UA UB UO", 576, "float16")
-_d("DA DB DO", 512, "float16")
-_d("EA EB EO", 320, "float16")
+_pool("TL", " ".join("TL%d" % k for k in range(16)), 128, "bfloat16")
+_pool("MATS", "ID BO BO3 BO1 BON B256 WB1 SH1 SH2 SH3 SH4 GT0 GTN BM0 GT8 NEG ALT ONS I256 ALF TRI T255 MV I025 "
+              "N512 N101 tm7 tm8 TH2 WD WO DM0 DM1 DM2", 128, "bfloat16")
+_pool("HMATS", "I1 I4 N32 P512 P1K N1K", 128, "float16")
+_pool("SMALL", "ONE SP0 NF EE PRE VV6 VV VW DIF DG DGX KX YL EQ0 SEL STH STL NOK", 64, "bfloat16")
+STAIRS = {"K": 10, "T": 17, "U": 14}
+for _n, _s in STAIRS.items():
+    _d("%sA %sB %sO" % (_n, _n, _n), 64 * _s, "float16")
 _d("LG LM OHL", 640, "bfloat16")
 _d("AS AO", 512, "bfloat16")
 _d("K5 M5 AL", 320, "bfloat16")
@@ -51,14 +51,14 @@ for _t in range(RO):
     _pool("SND%d" % _t, "SL%d SC%d" % (_t, _t), 64, "bfloat16")
 _d("WT", 1, "bfloat16")
 _d("ST0 ST1 ST2 ST3", 64, "int32")
-_pool("INTS", "N4 DH YI SI S0 HI HM FVI FH SIH SIL", 64, "int32")
+_pool("INTS", "N4 DH SI S0 HI HM FVI FH SIH SIL", 64, "int32")
+_d("YI", 128, "int32")
 _d("PI QI GI", 1, "int32")
-_d("ROWF CQF CGF", 128, "float32")
-_d("QC GC PC QB MW Q4 XU XD HB PB ACOL", 1, "float32")
+_d("ROWF CQF CGF AD", 128, "float32")
+_d("QC GC PC QB MW Q4 CN C78 ACOL M0 M1 M2", 1, "float32")
 _d("EQ16", 32, "float32")
-_pool("COEF", "CD0 CD1 CD2 CD3 CD4 CD5 CD6 CU0", 1, "float32")
-_d("CU MC", 8, "float32")
-_pool("FLTS", "CA CB4 PR M16F DIAG SD X1 X2 SD2", 64, "float32")
+_d("CU", 16, "float32")
+_pool("FLTS", "CB PR M16F DIAG SD X1 X2 SD2", 64, "float32")
 _d("YS", 64, "float32")
 _d("OFFZ", 64, "uint16")
 _d("OV OZ", 4, "uint16")
@@ -71,7 +71,7 @@ SEMAPHORES += ["%s%d" % (s, t) for s in ("st", "arr") for t in range(1, RO)]
 Z_SCALAR = {0: [0, 34], 1: [0, 40], 7: [0, 32, 46]}
 Z_VECTOR = {0: [34, 50, 64], 1: [40, 48, 64], 7: [46, 64]}
 for _k in range(2, 7):
-    Z_SCALAR[_k], Z_VECTOR[_k] = [0, 44] if _k % 2 else [0, 16, 44], [44, 54, 64]
+    Z_SCALAR[_k], Z_VECTOR[_k] = [0, 42] if _k % 2 else [0, 16, 42], [42, 46, 64]
 
 
 class Ap(tuple):
@@ -96,6 +96,9 @@ def rank_program(g, core, T, topo):
         b = cols if b is None else b
         ap = T[buf][:, off + a:off + b] if step == 1 else T[buf][:, off + a:off + b:step]
         return Ap((ap, ((name, a, b, step),)))
+
+    def A3(name, a):
+        return A(name, a, None, SCRATCH[name][1][1] // 64)
 
     def IND(win, off):
         return Ap((win[0].indirect(off[0]), win[1] + off[1]))
@@ -276,13 +279,17 @@ def rank_program(g, core, T, topo):
         ts(A("ID"), A("ROWF"), A("PC"), EQ)
         ts(A("B256"), A("BO"), 256.0, MUL)
         ts(A("EQ16"), A("ROWF", 0, 32), A("QC"), EQ)
-        for name, x in (("NEG", -128.0), ("ONE", 1.0), ("L0", 0.0), ("N4C", -4.0), ("UB", 0.0), ("DB", 0.0), ("EB", 0.0),
-                        ("ACOL", 4.0 * 613), ("BM0", 0.0)):
+        for name, x in (("ONE", 1.0), ("ALT", 1.0), ("ACOL", 4.0 * 613), ("BM0", 0.0)):
             fill(A(name), x)
+        fill(A("ALT", 0, 128, 2), 0.0)
+        ts(A("CN"), A("PC"), 0.0, EQ, -2.0, MUL)
+        ts(A("NEG"), A("ROWF"), 0.0, MUL, A("CN"), ADD)
+        ts(A("NEG"), A("NEG"), -256.0, ADD)
         fill(A("Z7", 0, 2050, 2049), 0.0)
-        for name, x in (("NID", -1.0), ("N512", -512.0), ("N101", -101.0)):
+        for name, x in (("N512", -512.0), ("N101", -101.0)):
             ts(A(name), A("ID"), x, MUL)
-        ts(A("DP0", 1, 128, 2), A("ONE"), A("QC"), MUL, -4.0, MUL)
+        ts(A("M0"), A("QC"), -1.0, ADD)
+        ts(A("DM0"), A("ID"), A("M0"), MUL)
         ts(A("GT0"), A("BO"), A("EQ16", 0, 1), MUL)
         ts(A("LB0"), A("SP0"), -1.0, MUL, 4.0, ADD)
         starts(0)
@@ -293,23 +300,25 @@ def rank_program(g, core, T, topo):
         cp(A("OFFZ"), A("SI"))
 
     def step_constants():
-        tt(A("CD0"), A("EQ16", 8, 9), A("EQ16", 7, 8), SUB)
-        for j in range(1, 7):
-            tt(A("CD%d" % j), A("EQ16", 9 - j, 10 - j), A("EQ16", 7 - j, 8 - j), SUB)
-        tt(A("CU0"), A("EQ16", 9, 10), A("EQ16", 8, 9), SUB)
-        tt(A("CU", 1, 8), A("EQ16", 10, 17), A("EQ16", 8, 15), SUB)
-        for k in range(15):
-            j = k if k < 7 else k - 7
-            col = A("CD%d" % j) if k < 7 else A("CU", j, j + 1) if j else A("CU0")
-            ts(A("TL%d" % k), A("BO"), col, MUL, (-1.0) ** j / 64, MUL)
+        tt(A("CU"), A("EQ16", 0, 16), A("EQ16", 2, 18), SUB)
+        tt(A("C78"), A("EQ16", 7, 8), A("EQ16", 8, 9), SUB)
+        for i in range(16):
+            ts(A("TL%d" % i), A("BO"), A("CU", 16 - i, 17 - i) if i else A("C78"), MUL, (-1.0) ** max(i, 1) / 1024, MUL)
+        for d in STAIRS:
+            fill(A(d + "B"), -2.0)
+            fill(A3(d + "A", 0), -64.0)
+            fill(A3(d + "B", 2), -1.875)
+        fill(A3("KB", 0), -1.125)
         ts(A("GTN"), A("BO"), A("EQ16", 0, 1), MUL)
         fill(A("GTN", 0, 128, 16), 0.0)
         cp(A("BM0", 0, 128, 16), A("BO", 0, 128, 16))
         ts(A("Q4"), A("QC"), -1.0, MUL, 4.0, ADD)
-        for name, x, y in (("XU", 4.0, -30.0), ("XD", -4.0, 34.0), ("HB", 8.0, 20.0), ("PB", 8.0, 19.0)):
-            ts(A(name), A("QC"), x, MUL, y, ADD)
+        for j, x in ((1, 2.5), (2, -5.5)):
+            ts(A("M%d" % j), A("QC"), x, ADD)
+            ts(A("DM%d" % j), A("ID"), A("M%d" % j), MUL)
         ts(A("GT8"), A("BO"), A("EQ16", 8, 9), MUL)
-        for name, x in (("P64", 64.0), ("N64", -64.0), ("P32", 32.0), ("N32", -32.0), ("H9", 2.25), ("H1", -0.25)):
+        for name, x in (("I1", 1.0), ("I4", 4.0), ("N32", -32.0), ("P512", 512.0), ("P1K", 1024.0), ("N1K", -1024.0),
+                        ("I025", 0.25)):
             ts(A(name), A("ID"), x, MUL)
 
     def more_constants():
@@ -374,22 +383,38 @@ def rank_program(g, core, T, topo):
         b, s, o = ZAT[k]
         eng(A(b, 16 * s * i0 + o, 16 * s * i1 + o - s + 1, s), IND(A("X", 0, width), A("OFFZ", i0, i1)))
 
+    def table(k):
+        return ("K", 8, 10) if k == 1 else ("T" if k < 5 else "U", 16, 19 - k)
+
+    def heights(d, a, b):
+        for i in range(a, b):
+            act(A3(d + "A", 3 + i), A("ps6" if i < 7 else "psP", 64 * (i % 7), 64 * (i % 7) + 64), IDT, -0.25)
+
     def ustart(k):
         if k < 7:
-            mm(A("psW", 64, 128), A("NID"), A("DP%d" % k, 1, 128, 2), True, False)
-            mm(A("psW", 64, 128), A("ID"), A("N4C"), False, True)
-        mm(A("psW", 0, 64), A("NEG"), A("ONE"), True, False)
+            terms = [(A("DM%d" % min(k, 2)), A("ONE"))]
+            if k:
+                d = table(k)[0]
+                terms += [(A("I4"), A3(d + "B", 0)), (A("I4"), A3(d + "A", 2))]
+            for j, (l, r) in enumerate(terms):
+                mm(A("psW", 128, 192), l, r, j == 0, j == len(terms) - 1)
+        mm(A("psW", 0, 128), A("NEG"), A("ALT"), True, False)
 
     def uwrap(k):
         b, s, o = ZAT[k]
         for m in range(16):
-            mm(A("psW", 0, 64), A("Wm", m * 128, m * 128 + 128), A(b, s * m + o, 1024 * s + o - s + 1, 16 * s),
+            mm(A("psW", 1, 128, 2), A("Wm", m * 128, m * 128 + 128), A(b, s * m + o, 1024 * s + o - s + 1, 16 * s),
                False, m == 15)
 
-    def entries(k, src, off):
-        ts(A("CB4"), src, 4.0, MUL, 16383.75 + 4 * off, ADD)
+    def entries(k, src, off, on):
+        outs = [(A("CB"), 8.0, 2.0)]
         if k < 7:
-            ts(A("CA"), src, 2.0, MUL, 296.0 + 2 * off, ADD)
+            outs += [(A("AD", 0, 128, 2), 1.0, 148.5), (A("AD", 1, 128, 2), 6.0, 16680.75)]
+        for out, x, y in outs:
+            if on == "s":
+                act(out, src, IDT, y + x * off, x)
+            else:
+                ts(out, src, x, MUL, y + x * off, ADD)
 
     def maxima(j, q):
         if j < 2:
@@ -402,54 +427,47 @@ def rank_program(g, core, T, topo):
             scan(A("O2", *r), A("D2", *r), A("G2", *r), ADD, MAX)
 
     def arith(k, between):
-        nx = "DP%d" % (k + 1)
-        tt(A("DH"), A("psW", 0, 64), A("CB4"), ADD)
-        tt(A("psP", 0, 64), A("psW", 0, 64), A("CA"), MUL)
+        d = table(k + 1)[0]
+        scan(A("YI"), A("psW", 0, 128), A("AD"), MUL, ADD)
+        tt(A("DH"), A("psW", 1, 128, 2), A("CB"), ADD)
         between(0)
-        ts(A("N4"), A("DH"), 12, AND)
-        tt(A("YI"), A("psP", 0, 64), A("DH"), ADD)
+        ts(A("SI"), A("YI", 1, 128, 2), 2, SHR, W - 1, AND)
+        ts(A("N4"), A("DH"), 3, SHR, 3, AND)
         between(1)
-        tt(A(nx, 0, 128, 2), A("N4"), A("psW", 64, 128), GE)
-        entry = collect(lambda: (
-            tt(A(nx, 1, 128, 2), A("N4"), A("psW", 64, 128), SUB),
-            scan(A("QS"), A("L0"), A(nx), MUL, ADD)))
-        place = collect(lambda: (ts(A("SI"), A("YI"), 2, SHR, W - 1, AND), cp(A("OFFZ"), A("SI"))))
-        for pair in zip(entry, place) if k < 6 else zip(place, entry):
-            for call in pair:
-                run(*call)
-
-    def heights(k, between):
-        between(0)
-        if k > 1:
-            ts(A("UB", 0, 576, 9), A("QS", 1, 128, 2), A("XU"), ADD, 34.0, MIN)
-        d, s = ("D", 8) if k < 4 else ("E", 5)
-        ts(A(d + "B", 0, 64 * s, s), A("QS", 1, 128, 2), -1.0, MUL, A("XD"), ADD)
-        between(1)
+        cp(A("OFFZ"), A("SI"))
+        tt(A3(d + "A", 1), A("N4"), A("psW", 128, 192), LT)
+        ts(A3(d + "A", 2), A("N4"), -0.25, MUL)
 
     def stairs(k):
-        if k > 1:
-            scan(A("UO"), A("UA"), A("UB"), ADD, MAX)
-        d = "D" if k < 4 else "E"
+        d = table(k)[0]
         scan(A(d + "O"), A(d + "A"), A(d + "B"), ADD, MAX)
 
     def csum(k, C):
-        terms = [(A("GT8"), C)]
-        if k == 1:
-            terms += [(A("P32"), A("DB", 0, 512, 8))]
-        else:
-            terms += [(A("N32"), A("UB", 0, 576, 9))]
-            terms += [(A("P64" if j % 2 else "N64"), A("UO", j, 576, 9)) for j in range(1, 5 if k == 2 else 9)]
-        terms += [(A("N64" if j % 2 else "P64"), A("DO", j, 512, 8) if k < 4 else A("EO", j, 320, 5))
-                  for j in range(1, 9 - k)]
+        d, top, s = table(k)
+        terms = [(A("GT8"), C)] if k == 1 else []
+        terms += [(A("P512" if j == 2 else "N1K" if j % 2 else "P1K"), A3(d + "O", j)) for j in range(2, s)]
         for j, (l, r) in enumerate(terms):
             mm(A("psC", 0, 64), l, r, j == 0, j == len(terms) - 1)
+        return 960.0 - 2048.0 * ((s - 3) % 2)
 
-    def logmm(k):
-        mm(A("ps3", 0, 64), A("H9"), A("DP%d" % k, 1, 128, 2), True, False)
-        mm(A("ps3", 0, 64), A("H1"), A("DP%d" % (k + 1), 1, 128, 2), False, True)
+    def bases(k, LB):
+        d = table(k)[0]
+        was, less = A3(d + "B", 0), A3(d + "A", 2)
+        for j in range(2 if k < 7 else 1):
+            mm(A("ps3", j, 128, 2), A("I1"), was, True, False)
+            if j:
+                mm(A("ps3", j, 128, 2), A("I025"), LB, False, False)
+            mm(A("ps3", j, 128, 2), A("I1"), less, False, True)
+        mm(A("ps3", 128, 192), A("N32"), was, True, False)
+        mm(A("ps3", 128, 192), A("I4"), less, False, True)
 
     def logact(k):
-        act(A("LG", 8 - k, 640, 10), A("ps3", 0, 64), IDT, A("HB"))
+        if k < 6:
+            for j in range(2):
+                act(A3(table(k + 2)[0] + "B", j), A("ps3", j, 128, 2), IDT, 1.75 if k == 0 else -0.25)
+        else:
+            act(A("PRE"), A("ps3", 0, 128, 2), IDT, 55.0, -32.0)
+        act(A("LG", 8 - k, 640, 10), A("ps3", 128, 192), IDT, 8.0 * table(k + 1)[1] - 81)
 
     ysn = [0]
 
@@ -467,7 +485,6 @@ def rank_program(g, core, T, topo):
         C, LB, F = A("C%d" % t), A("LB%d" % t), A("F%d" % t)
         sndC, sndL = "SC%d" % t, "SL%d" % t
         ustart(0)
-        mm(A("ps5", 0, 512, 8), A("NEG"), A("ONE"))
         mm(A("psC", 0, 64), A("ID"), A("STH"), True, False)
         mm(A("psC", 0, 64), A("ID"), A("STL"), False, False)
         mm(A("psC", 0, 64), A("N512"), LB, False, False)
@@ -483,16 +500,13 @@ def rank_program(g, core, T, topo):
             late_constants(0)
         else:
             ts(A("OFFZ"), A("psC", 0, 64), A("ACOL"), ADD)
-        for j in range(1, 8):
-            mm(A("ps5", j, 512, 8), A("TL%d" % (j - 1)), C)
-        for h, ps in enumerate(("ps6", "ps3")):
-            mm(A(ps, 0, 288, 9), A("NEG"), A("ONE", 0, 32))
-            for j in range(1, 9):
-                mm(A(ps, j, 288, 9), A("TL%d" % (6 + j)), A("C%d" % t, 32 * h, 32 * h + 32))
-        ts(A("L0", 1, 128, 2), LB, -4.0, MUL, 16.0, ADD)
+        for ps, first in (("ps5", 8), ("ps6", 0), ("psP", 7)):
+            for j in range(7):
+                mm(A(ps, 64 * j, 64 * j + 64), A("TL%d" % (first + j + 1 if j or ps != "ps5" else 0)), C)
+        ts(A3("KB", 1), LB, 0.25, MUL, -1.125, ADD)
         ts(A("EQ0"), A("ps4", 0, 64), A("Q4"), EQ)
         if t == 0:
-            ts(A("Wm"), A("Gm"), A("WT"), MUL, 0.5 / 65536, MUL)
+            ts(A("Wm"), A("Gm"), A("WT"), MUL, 1.0 / 65536, MUL)
         gz(actcp, 0, 0, W + AGAIN if t else W)
         gz(cp, 0, 0, W + AGAIN if t else W)
         tt(A("SEL"), A("EQ0"), C, MUL)
@@ -500,10 +514,10 @@ def rank_program(g, core, T, topo):
         mm(A("ps4", 0, 64), A("GTN"), C, True, False)
         mm(A("ps4", 0, 64), A("BM0"), A("SEL"), False, True)
         uwrap(0)
-        ts(A("DA", 0, 256), A("ps5", 0, 256), -4.0, ADD)
-        entries(0, A("ps4", 0, 64), 0)
-        ts(A("DA", 256, 512), A("ps5", 256, 512), -4.0, ADD)
-        act(A("UA", 288, 576), A("ps3", 0, 288), IDT, -4.0)
+        entries(0, A("ps4", 0, 64), 0, "v")
+        for j in range(7):
+            ts(A3("KA", 3 + j), A("ps5", 64 * j, 64 * j + 64), -0.25, ADD)
+        heights("T", 0, 7)
         if t == 0:
             act(A("Z7", 1, 2049, 2), A("Gm", 0, 1024), IDT, 0.0, 0.0)
         for m in range(16):
@@ -512,40 +526,33 @@ def rank_program(g, core, T, topo):
             arith(k - 1, lambda piece: maxima(2, 3 + piece) if k == 7 else spare())
             for piece in range(len(Z_SCALAR[k]) - 1):
                 gz(actcp, k, piece)
-            ustart(k)
-            logmm(k - 1)
             if last:
                 ysum(19)
+            ustart(k)
+            bases(k, LB)
             if k == 6:
                 mm(A("ps4"), A("ID"), A("D2", 3, 2048, 4), True, False)
                 mm(A("ps5", 0, 256), A("ID"), A("D2", 2048 + 3, 3072, 4), True, False)
             if k == 7:
                 break
-            heights(k, lambda piece: gz(cp, k, 0) if piece else None)
+            gz(cp, k, 0)
             stairs(k)
             gz(cp, k, 1)
-            csum(k, C)
-            if k < 6:
-                logact(k - 1)
+            off = csum(k, C)
             uwrap(k)
+            logact(k - 1)
+            entries(k, A("psC", 0, 64), off, "s")
             for j, q in PLAN.get(k, ())[:-1]:
                 maxima(j, q)
-            if k < 6:
-                entries(k, A("psC", 0, 64), -64 if k == 1 else 64)
-            else:
-                act(A("CB4"), A("psC", 0, 64), IDT, 16383.75 + 4 * 64, 4.0)
-                act(A("CA"), A("psC", 0, 64), IDT, 296.0 + 2 * 64, 2.0)
-                logact(5)
+            if k in (2, 3):
+                heights("U", *{2: (0, 5), 3: (5, 11)}[k])
             if k == 1:
-                act(A("UA", 0, 288), A("ps6", 0, 288), IDT, -4.0)
+                heights("T", 7, 14)
                 act(A("LG", 9, 640, 10), LB, IDT, 4.0, -1.0)
                 if t and not last:
                     weave(lambda: starts(t + 1), 2)
             if k == 2 and t:
                 act(A("WD", 1, 128, 2), LB, EXP, 9.0, -3.0)
-            if k == 3:
-                for j in range(5):
-                    actcp(A("EA", j, 320, 5), A("DA", j, 512, 8))
             for j, q in PLAN.get(k, ())[-1:]:
                 maxima(j, q)
             if t == 0:
@@ -553,8 +560,8 @@ def rank_program(g, core, T, topo):
         mm(A("ps6", 0, 128), A("I256"), A("TH2"), True, False)
         mm(A("ps4"), A("I256"), A("O2", 3, 2048, 4), False, False)
         mm(A("psP", 0, 256), A("ID"), A("D2", 3072 + 3, 4096, 4), True, False)
-        heights(7, lambda piece: maxima(2, 5 + piece))
-        maxima(2, 7)
+        for q in (5, 6, 7):
+            maxima(2, q)
         gz(cp, 7, 0)
         stairs(7)
         mm(A("ps5", 0, 256), A("I256"), A("O2", 2048 + 3, 3072, 4), False, False)
@@ -565,18 +572,17 @@ def rank_program(g, core, T, topo):
         act(A("GEb", 0, 512), A("ps4"), SIGN, 256.5)
         for q, ps in ((2, "ps5"), (3, "psP")):
             ts(A("GEb", 256 * q, 256 * q + 256), A(ps, 0, 256), -256.5, GE, -0.5, ADD)
-        csum(7, C)
+        off = csum(7, C)
         uwrap(7)
-        entries(7, A("psC", 0, 64), 64)
+        entries(7, A("psC", 0, 64), off, "v")
         for m in range(16):
             mm(A("ps6", 0, 128, 2), A("Gm", m * 128, m * 128 + 128), A("GEb", m, 1024, 16), False, m == 15)
         logact(6)
-        act(A("PRE"), A("DP7", 1, 128, 2), IDT, A("PB"), 2.0)
         actcp(A("O2", 0, 4096, 64), F)
         if t == 0:
             late_constants(7)
-        tt(A("DH"), A("psW", 0, 64), A("CB4"), ADD)
-        ts(A("N4"), A("DH"), 2, SHR, 3, AND)
+        tt(A("DH"), A("psW", 1, 128, 2), A("CB"), ADD)
+        ts(A("N4"), A("DH"), 3, SHR, 3, AND)
         scan(A("WO"), A("WD"), A("ps6", 0, 128), MIN, MAX)
         tt(A("LG", 1, 640, 10), A("PRE"), A("N4"), SUB)
         mm(A("ps4", 0, 320), A("ID"), A("K5"), True, False)

@@ -5,10 +5,12 @@ ADD, SUB, MUL, MAX, MIN = AluOpType.add, AluOpType.subtract, AluOpType.mult, Alu
 GE, EQ, LT, GT, NE = AluOpType.is_ge, AluOpType.is_equal, AluOpType.is_lt, AluOpType.is_gt, AluOpType.not_equal
 SHR, AND = AluOpType.arith_shift_right, AluOpType.bitwise_and
 IDT, SIGN, ABS = ActivationFunctionType.Identity, ActivationFunctionType.Sign, ActivationFunctionType.Abs
-COPY, EXP = ActivationFunctionType.Copy, ActivationFunctionType.Exp
+COPY, SQUARE = ActivationFunctionType.Copy, ActivationFunctionType.Square
 RO, S, W = 4, 8, 8192
 AGAIN = 3072
+ROUND = 1.5 * 2 ** 23
 DUMP = 2 * W
+STAIRS = {"K": 11, "T": 18, "U": 15}
 
 SCRATCH = {}
 POOL = {}
@@ -26,56 +28,113 @@ def _pool(buf, names, cols, dtype):
 
 
 _d("X", DUMP + 2 * W, "bfloat16")
-_d("G0 G1 O0 O1", 3072, "bfloat16")
-_d("G2 O2 D2", 4096, "bfloat16")
-_d("Z7", 2050, "bfloat16")
+_d("G0 O0 O2", 3072, "bfloat16")
+_d("G1", 4096, "bfloat16")
+_d("ZV", 9218, "bfloat16")
+POOL.update(O1=("ZV", 0, 4096), G2=("ZV", 4096, 3072), Z7=("ZV", 7168, 2050))
 _d("GEb", 1024, "bfloat16")
-_d("M3", 768, "bfloat16")
+_d("M3", 384, "bfloat16")
+_d("M4", 512, "bfloat16")
+_d("V4 VO CM M8", 256, "bfloat16")
+_d("X1 MM", 256, "float32")
 _d("Gm Wm", 2048, "bfloat16")
 _pool("TL", " ".join("TL%d" % k for k in range(16)), 128, "bfloat16")
-_pool("MATS", "ID BO BO3 BO1 BON B256 WB1 SH1 SH2 SH3 SH4 GT0 GTN BM0 GT8 NEG ALT ONS I256 ALF TRI T255 MV I025 "
-              "N512 N101 tm7 tm8 TH2 WD WO DM0 DM1 DM2", 128, "bfloat16")
+_pool("MATS", "ID BO BO3 BO1 BON B256 WB1 SH1 SH2 SH3 SH4 GT0 GTN BM0 GT8 NEG ONS I256 I255 ALF TRI T255 MV "
+              "N256 W128 N512 N101 tm7 tm8 WD WO VP TH2 ALT", 128, "bfloat16")
 _pool("HMATS", "I1 I4 N32 P512 P1K N1K", 128, "float16")
-_pool("SMALL", "ONE SP0 NF EE PRE VV6 VV VW DIF DG DGX KX YL EQ0 SEL STH STL NOK", 64, "bfloat16")
-STAIRS = {"K": 10, "T": 17, "U": 14}
+_pool("SMALL", "ONE SP0 CH0 NF PRE DIF DG KX YL YB YC EQ0 SEL STH STL NOK GAP GAP0", 64, "bfloat16")
 for _n, _s in STAIRS.items():
     _d("%sA %sB %sO" % (_n, _n, _n), 64 * _s, "float16")
-_d("LG LM OHL", 640, "bfloat16")
+_d("LG OHL LM", 640, "bfloat16")
 _d("AS AO", 512, "bfloat16")
 _d("K5 M5 AL", 320, "bfloat16")
 _d("ALO", 320, "float16")
-_d("M8", 256, "bfloat16")
 _d("F0 F1 F2 F3 F4", 64, "bfloat16")
-for _t in range(RO):
-    _pool("LND%d" % _t, "LB%d C%d" % (_t, _t), 64, "bfloat16")
-    _pool("SND%d" % _t, "SL%d SC%d" % (_t, _t), 64, "bfloat16")
+_d("LND0 LND1 LND2 LND3 SND0 SND1 SND2", 128, "bfloat16")
 _d("WT", 1, "bfloat16")
 _d("ST0 ST1 ST2 ST3", 64, "int32")
-_pool("INTS", "N4 DH SI S0 HI HM FVI FH SIH SIL", 64, "int32")
+_pool("INTS", "N4 DH SI S0 FVI FH SIH SIL", 64, "int32")
 _d("YI", 128, "int32")
-_d("PI QI GI", 1, "int32")
+_d("PI QI GI RI TI", 1, "int32")
 _d("ROWF CQF CGF AD", 128, "float32")
-_d("QC GC PC QB MW Q4 CN C78 ACOL M0 M1 M2", 1, "float32")
+_pool("COLS", "QC GC PC QB MW Q4 CN C78 ACOL M0 M1 M2 RC TC GE1 GE2 GE3 SCA BIB SCL BIA WF WS", 1, "float32")
 _d("EQ16", 32, "float32")
-_d("CU", 16, "float32")
-_pool("FLTS", "CB PR M16F DIAG SD X1 X2 SD2", 64, "float32")
-_d("YS", 64, "float32")
+_d("CU CV SGN", 16, "float32")
+_pool("FLTS", "PR M16F M4F DIAG DIA4 SD X0 X2 SD2 W1 W2", 64, "float32")
+_d("YS CQ4", 64, "float32")
 _d("OFFZ", 64, "uint16")
-_d("OV OZ", 4, "uint16")
+_d("OV", 16, "uint16")
 _d("OX", 8, "uint16")
-_d("psW psC psP ps3 ps4 ps5 ps6 psY", 512, "float32", "psum")
+_d("psW0 psW1 psD0 psD1 psB0 psB1 psC psY", 512, "float32", "psum")
 
 SEMAPHORES = ["qv", "qs", "qt", "qg", "dX", "dW", "dC", "dL", "dS", "dF", "oC", "oL", "oF", "oS", "loc"]
 SEMAPHORES += ["%s%d" % (s, t) for s in ("st", "arr") for t in range(1, RO)]
 
-Z_SCALAR = {0: [0, 34], 1: [0, 40], 7: [0, 32, 46]}
-Z_VECTOR = {0: [34, 50, 64], 1: [40, 48, 64], 7: [46, 64]}
-for _k in range(2, 7):
-    Z_SCALAR[_k], Z_VECTOR[_k] = [0, 42] if _k % 2 else [0, 16, 42], [42, 46, 64]
+Z_SCALAR = [(20, 24), (28, 28), (32, 32), (32, 32), (32, 32), (32, 32), (32, 32), (32, 20)]
+PIECE = 64
+PARTS = (("psD0", 0, 32, "v"), ("psD1", 32, 48, "s"), ("psW0", 48, 64, "v"))
+WAIT, GATHER, REMOTE, FIRST, LOAD, TABLE = 230.0, 1.3, 3000.0, 2500.0, 1400.0, 4500.0
+ORDER = []
 
 
 class Ap(tuple):
     pass
+
+
+def meet(a, lo, hi, step):
+    return a[0] < hi and a[1] > lo and (a[0] - lo) % math.gcd(a[2], step) == 0
+
+
+def plan(calls):
+    before, seen, bank, behind, line = [], {}, {}, {}, {}
+    for i, (q, outs, ins, cost, late, call, fixed) in enumerate(calls):
+        need = set()
+        if fixed:
+            behind[i], line[q] = line.get(q), i
+        for w, group in ((True, outs), (False, ins)):
+            for x in group:
+                for name, lo, hi, step in x[1]:
+                    if name.startswith("ps"):
+                        was, now = bank.setdefault(name, ([], []))
+                        if now and calls[now[-1]][0] != q:
+                            was, now = bank[name] = now, []
+                        need.update(was + (now[-1:] if q == "t" else []))
+                        now.append(i)
+                    need.update(a[4] for a in seen.get(name, ()) if (w or a[3]) and meet(a, lo, hi, step))
+        for w, group in ((False, ins), (True, outs)):
+            for x in group:
+                for name, lo, hi, step in x[1]:
+                    lst = seen.setdefault(name, [])
+                    if w:
+                        lst[:] = [a for a in lst if not (lo <= a[0] and a[1] <= hi and a[2] % step == 0
+                                                         and (a[0] - lo) % step == 0)]
+                    lst.append((lo, hi, step, w, i))
+        need.discard(i)
+        if behind.get(i) is None or behind[i] in need:
+            behind[i] = None
+        else:
+            need.add(behind[i])
+        before.append(need)
+
+    def lag(j, i):
+        return calls[j][3] + (0 if behind[i] == j or calls[j][0] == calls[i][0] == "t" else calls[j][4] + WAIT)
+    way = [c[3] + c[4] + (1e6 if c[4] == FIRST else 0) for c in calls]
+    for i in range(len(calls) - 1, -1, -1):
+        for j in before[i]:
+            way[j] = max(way[j], lag(j, i) + way[i])
+    busy, start = {}, {}
+    for i in sorted(range(len(calls)), key=lambda i: (-way[i], i)):
+        t = max([0] + [start[j] + lag(j, i) for j in before[i]])
+        lst = busy.setdefault(calls[i][0], [])
+        k = len(lst)
+        while k and lst[k - 1][1] > t:
+            k -= 1
+        while k < len(lst) and lst[k][0] < t + calls[i][3]:
+            t = max(t, lst[k][1])
+            k += 1
+        lst.insert(k, (t, t + calls[i][3]))
+        start[i] = t
+    return sorted(start, key=lambda i: (start[i], -way[i], i))
 
 
 def rank_program(g, core, T, topo):
@@ -88,7 +147,8 @@ def rank_program(g, core, T, topo):
     known = {q: {} for q in queue}
     snap = {}
     seen = {}
-    held = []
+    calls = []
+    fixed = [False]
 
     def A(name, a=None, b=None, step=1):
         buf, off, cols = POOL[name] if name in POOL else (name, 0, SCRATCH[name][1][1])
@@ -97,8 +157,10 @@ def rank_program(g, core, T, topo):
         ap = T[buf][:, off + a:off + b] if step == 1 else T[buf][:, off + a:off + b:step]
         return Ap((ap, ((name, a, b, step),)))
 
-    def A3(name, a):
-        return A(name, a, None, SCRATCH[name][1][1] // 64)
+    def R(name, h, slot=None):
+        cols = POOL[name][2] if name in POOL else SCRATCH[name][1][1]
+        a, b = (0, cols) if h is None else (h * cols // 2, (h + 1) * cols // 2)
+        return A(name, a, b) if slot is None else A(name, a + slot, b, cols // 64)
 
     def IND(win, off):
         return Ap((win[0].indirect(off[0]), win[1] + off[1]))
@@ -119,7 +181,7 @@ def rank_program(g, core, T, topo):
                 for name, lo, hi, step in x[1]:
                     ps = name.startswith("ps")
                     for a in seen.get(name, ()):
-                        apart = a[0] >= hi or a[1] <= lo or (a[0] - lo) % math.gcd(a[2], step) != 0
+                        apart = not meet(a, lo, hi, step)
                         if apart and not ps:
                             continue
                         if a[4] == q:
@@ -144,96 +206,105 @@ def rank_program(g, core, T, topo):
                     lst[:] = [a for a in lst if not (a[4] == q and a[3] == w and a[:3] == [lo, hi, step])]
                     lst.append([lo, hi, step, w, q, sem, val])
 
-    def run(q, outs, ins, call):
-        if held:
-            held[0].append((q, outs, ins, call))
-            return
-        deps(q, outs, ins)
-        sem = "q" + q
-        count[q] += 1
-        snap[(sem, count[q])] = dict(known[q])
-        call().then_inc(T.sem[sem], 1)
-        record(q, outs, ins, sem, count[q])
+    def run(q, outs, ins, cost, call):
+        def issue():
+            deps(q, outs, ins)
+            sem = "q" + q
+            count[q] += 1
+            snap[(sem, count[q])] = dict(known[q])
+            call().then_inc(T.sem[sem], 1)
+            record(q, outs, ins, sem, count[q])
+        calls.append((q, outs, ins, cost, 0, issue, fixed[0]))
 
-    def collect(make):
-        held.append([])
-        make()
-        return held.pop()
-
-    def spaced(make, gap=4):
-        calls = collect(make)
-
-        def names(group):
-            return {r[0] for x in group for r in x[1]}
-        before = [[j for j in range(i) if names(calls[j][1]) & (names(c[1]) | names(c[2]))
-                   or names(calls[j][2]) & names(c[1])] for i, c in enumerate(calls)]
-        done = {}
-        while len(done) < len(calls):
-            free = [i for i in range(len(calls)) if i not in done and all(j in done for j in before[i])]
-            i = min(free, key=lambda i: (max([len(done)] + [done[j] + gap for j in before[i]]), i))
-            done[i] = len(done)
-        return [calls[i] for i in done]
-
-    def weave(make, gap=4):
-        for c in spaced(make, gap):
-            run(*c)
-
-    def dma(q, sem, out, in_, outs, ins):
-        deps(q, outs, ins)
-        snap[(sem, 16)] = dict(known[q])
-        queue[q].dma_start(out, in_).then_inc(T.sem[sem], 16)
-        record("dma" + sem, outs, ins, sem, 16)
+    def dma(q, sem, out, in_, outs, ins, late=LOAD):
+        def issue():
+            deps(q, outs, ins)
+            snap[(sem, 16)] = dict(known[q])
+            queue[q].dma_start(out, in_).then_inc(T.sem[sem], 16)
+            record("dma" + sem, outs, ins, sem, 16)
+        calls.append((q, outs, ins, 60, late, issue, False))
 
     def isap(s):
         return isinstance(s, Ap)
 
+    def size(x):
+        name, a, b, step = x[1][0]
+        return (b - a + step - 1) // step
+
+    def cycles(out, *ins):
+        if len(out[1]) > 1:
+            return 50 + 2.4 * GATHER * size(ins[0])
+        if len(ins[0][1]) > 1:
+            return 60 + GATHER * size(out)
+        wide = any(SCRATCH[POOL.get(x[1][0][0], x[1][0])[0]][2].endswith("32") for x in (out,) + ins)
+        return 0.83 * max(64, size(out) * (1 if wide else 0.5))
+
     def tt(out, a, b, op):
-        run("v", [out], [a, b], lambda: g.vector.tensor_tensor(out[0], a[0], b[0], op))
+        both = not any(x[1][0][0].startswith("ps") for x in (a, b))
+        cost = cycles(out, a) if len(a[1]) > 1 else 0.83 * max(64, size(out) * (2 if both else 1))
+        run("v", [out], [a, b], cost, lambda: g.vector.tensor_tensor(out[0], a[0], b[0], op))
 
     def ts(out, a, s1, op0, s2=None, op1=None):
         ins = [a] + [s for s in (s1, s2) if isap(s)]
         x1 = s1[0] if isap(s1) else s1
         x2 = s2[0] if isap(s2) else s2
         if op1 is None:
-            run("v", [out], ins, lambda: g.vector.tensor_scalar(out[0], a[0], x1, None, op0))
+            run("v", [out], ins, cycles(out, a), lambda: g.vector.tensor_scalar(out[0], a[0], x1, None, op0))
         else:
-            run("v", [out], ins, lambda: g.vector.tensor_scalar(out[0], a[0], x1, x2, op0, op1))
+            run("v", [out], ins, cycles(out, a), lambda: g.vector.tensor_scalar(out[0], a[0], x1, x2, op0, op1))
 
     def cp(out, a):
-        run("v", [out], [a], lambda: g.vector.tensor_copy(out[0], a[0]))
+        run("v", [out], [a], cycles(out, a), lambda: g.vector.tensor_copy(out[0], a[0]))
 
     def fill(out, x):
-        run("v", [out], [], lambda: g.vector.memset(out[0], x))
+        run("v", [out], [], cycles(out, out), lambda: g.vector.memset(out[0], x))
 
     def scan(out, d0, d1, op0, op1):
-        run("v", [out], [d0, d1], lambda: g.vector.tensor_tensor_scan(out[0], d0[0], d1[0], 0.0, op0, op1))
+        run("v", [out], [d0, d1], cycles(out, d0, d1),
+            lambda: g.vector.tensor_tensor_scan(out[0], d0[0], d1[0], 0.0, op0, op1))
 
     def act(out, a, func, bias=0.0, scale=1.0, acc=None):
         b = bias[0] if isap(bias) else bias
-        ins = [a] + ([bias] if isap(bias) else [])
+        x = scale[0] if isap(scale) else scale
+        ins = [a] + [c for c in (bias, scale) if isap(c)]
         if acc is None:
-            run("s", [out], ins, lambda: g.scalar.activation(out[0], a[0], func, bias=b, scale=scale))
+            run("s", [out], ins, 0.83 * max(64, size(out)),
+                lambda: g.scalar.activation(out[0], a[0], func, bias=b, scale=x))
         else:
-            run("s", [out, acc], ins,
-                lambda: g.scalar.activation(out[0], a[0], func, bias=b, scale=scale, accum_out=acc[0]))
+            run("s", [out, acc], ins, 75,
+                lambda: g.scalar.activation(out[0], a[0], func, bias=b, scale=x, accum_out=acc[0]))
 
     def actcp(out, a):
-        run("s", [out], [a], lambda: g.scalar.activation(out[0], a[0], COPY))
+        run("s", [out], [a], cycles(out, a) if len(a[1]) > 1 else 0.83 * max(64, size(out)),
+            lambda: g.scalar.activation(out[0], a[0], COPY))
 
     def mm(out, l, r, start=True, stop=True):
-        run("t", [out], [l, r], lambda: g.tensor.matmul(out[0], l[0], r[0], start, stop))
+        run("t", [out], [l, r], 0.42 * max(64, size(out)), lambda: g.tensor.matmul(out[0], l[0], r[0], start, stop))
+
+    def together(first):
+        part = calls[first:]
+        calls[first:] = [(part[0][0], sum((c[1] for c in part), []), sum((c[2] for c in part), []),
+                          sum(c[3] for c in part), 0, lambda: [c[5]() for c in part], fixed[0])]
+
+    def msum(out, terms, start=True, stop=True):
+        first = len(calls)
+        for j, (l, r) in enumerate(terms):
+            mm(out, l if isap(l) else A(l), r, start and j == 0, stop and j == len(terms) - 1)
+        together(first)
 
     def iota(out, pattern, cm=0, base=0):
         if SCRATCH[out[1][0][0]][2] == "int32":
-            run("g", [out], [], lambda: g.iota(out[0], pattern, base, cm))
+            run("g", [out], [], 130 + 1.66 * size(out), lambda: g.iota(out[0], pattern, base, cm))
         else:
-            run("g", [out], [], lambda: g.iota(out[0], pattern, base, cm, allow_small_or_imprecise_dtypes=True))
+            run("g", [out], [], 130 + 1.66 * size(out),
+                lambda: g.iota(out[0], pattern, base, cm, allow_small_or_imprecise_dtypes=True))
 
     def pick(out, a, pattern, op, other, base, cm):
-        run("g", [out], [a], lambda: g.affine_select(out[0], a[0], pattern, op, other, base, cm))
+        run("g", [out], [a], 170 + 1.66 * size(out),
+            lambda: g.affine_select(out[0], a[0], pattern, op, other, base, cm))
 
-    def gcp(out, a, cols):
-        pick(out, a, [[0, cols]], GE, 0.0, 0, 0)
+    def gcp(out, a):
+        pick(out, a, [[0, size(out)]], GE, 0.0, 0, 0)
 
     def resets(name, cols, step, first, other):
         iota(A(name), [[0, cols]], 0, other)
@@ -241,26 +312,33 @@ def rank_program(g, core, T, topo):
 
     sent = [0]
 
-    def send(src, name, sem, hop, ins, outs):
-        dst = T.cores[(rank + hop) % n]
-        rid, pid, _ = topo.addr(dst)
-        deps("g", [], ins)
-        g.remote_dma(out_ap=T[name][:], in_ap=T[src][:], remote_sem=T.sem[sem], local_sem=T.sem.loc,
-                     pid=pid, routing_id=rid, dma_engine_mask=topo.mask(core, dst))
-        sent[0] += len(topo.engines(core, dst))
-        record("net" + sem, outs, [], sem, len(topo.engines(T.cores[(rank - hop) % n], core)))
+    def send(src, dst, sem, hop, cost=300, late=REMOTE):
+        to = T.cores[(rank + hop) % n]
+        rid, pid, _ = topo.addr(to)
+
+        def issue():
+            deps("g", [], [src])
+            g.remote_dma(out_ap=dst[0], in_ap=src[0], remote_sem=T.sem[sem], local_sem=T.sem.loc,
+                         pid=pid, routing_id=rid, dma_engine_mask=topo.mask(core, to))
+            sent[0] += len(topo.engines(core, to))
+            record("net" + sem, [dst], [], sem, len(topo.engines(T.cores[(rank - hop) % n], core)))
+        calls.append(("g", [dst], [src], cost, late, issue, False))
 
     dma("y", "dS", T["ST0"][:], T.st[:], [A("ST0")], [])
     dma("s", "dL", A("SP0")[0], T.sp[:], [A("SP0")], [])
-    dma("y", "dX", T["X"][:, 0:W], T.x[:], [A("X", 0, W)], [])
+    dma("y", "dX", T["X"][:, 0:W], T.x[:], [A("X", 0, W)], [], TABLE)
     dma("s", "dW", T["WT"][:], T.wt[:], [A("WT")], [])
-    dma("s", "dC", A("C0")[0], T.ch[:], [A("C0")], [])
+    dma("s", "dC", A("CH0")[0], T.ch[:], [A("CH0")], [])
     dma("s", "dF", T["F0"][:], T.fl[:], [A("F0")], [])
+    for call in calls:
+        call[5]()
+    loads = len(calls)
 
     iota(A("PI"), [[1, 1]], 1)
     iota(A("CGF"), [[1, 8], [0, 16]])
     iota(A("ROWF"), [[1, 128]])
     iota(A("CQF"), [[0, 8], [1, 16]])
+    iota(A("CQ4"), [[0, 16], [1, 4]])
 
     def starts(t):
         ts(A("SIH"), A("ST%d" % t), W - 128, AND)
@@ -268,412 +346,344 @@ def rank_program(g, core, T, topo):
         cp(A("STH"), A("SIH"))
         cp(A("STL"), A("SIL"))
 
-    def constants():
-        fill(A("Gm"), 0.0)
-        ts(A("GI"), A("PI"), 4, SHR)
-        ts(A("QI"), A("PI"), 15, AND)
-        cp(A("PC"), A("PI"))
-        cp(A("GC"), A("GI"))
-        cp(A("QC"), A("QI"))
-        ts(A("BO"), A("CGF"), A("GC"), EQ)
-        ts(A("ID"), A("ROWF"), A("PC"), EQ)
-        ts(A("B256"), A("BO"), 256.0, MUL)
-        ts(A("EQ16"), A("ROWF", 0, 32), A("QC"), EQ)
-        for name, x in (("ONE", 1.0), ("ALT", 1.0), ("ACOL", 4.0 * 613), ("BM0", 0.0)):
-            fill(A(name), x)
-        fill(A("ALT", 0, 128, 2), 0.0)
-        ts(A("CN"), A("PC"), 0.0, EQ, -2.0, MUL)
-        ts(A("NEG"), A("ROWF"), 0.0, MUL, A("CN"), ADD)
-        ts(A("NEG"), A("NEG"), -256.0, ADD)
-        fill(A("Z7", 0, 2050, 2049), 0.0)
-        for name, x in (("N512", -512.0), ("N101", -101.0)):
-            ts(A(name), A("ID"), x, MUL)
-        ts(A("M0"), A("QC"), -1.0, ADD)
-        ts(A("DM0"), A("ID"), A("M0"), MUL)
-        ts(A("GT0"), A("BO"), A("EQ16", 0, 1), MUL)
-        ts(A("LB0"), A("SP0"), -1.0, MUL, 4.0, ADD)
-        starts(0)
-
-    def first_places():
-        ts(A("S0"), A("psC", 0, 64), A("ACOL"), ADD)
-        ts(A("SI"), A("S0"), W - 1, AND)
-        cp(A("OFFZ"), A("SI"))
-
-    def step_constants():
-        tt(A("CU"), A("EQ16", 0, 16), A("EQ16", 2, 18), SUB)
-        tt(A("C78"), A("EQ16", 7, 8), A("EQ16", 8, 9), SUB)
-        for i in range(16):
-            ts(A("TL%d" % i), A("BO"), A("CU", 16 - i, 17 - i) if i else A("C78"), MUL, (-1.0) ** max(i, 1) / 1024, MUL)
-        for d in STAIRS:
-            fill(A(d + "B"), -2.0)
-            fill(A3(d + "A", 0), -64.0)
-            fill(A3(d + "B", 2), -1.875)
-        fill(A3("KB", 0), -1.125)
-        ts(A("GTN"), A("BO"), A("EQ16", 0, 1), MUL)
-        fill(A("GTN", 0, 128, 16), 0.0)
-        cp(A("BM0", 0, 128, 16), A("BO", 0, 128, 16))
-        ts(A("Q4"), A("QC"), -1.0, MUL, 4.0, ADD)
-        for j, x in ((1, 2.5), (2, -5.5)):
-            ts(A("M%d" % j), A("QC"), x, ADD)
-            ts(A("DM%d" % j), A("ID"), A("M%d" % j), MUL)
-        ts(A("GT8"), A("BO"), A("EQ16", 8, 9), MUL)
-        for name, x in (("I1", 1.0), ("I4", 4.0), ("N32", -32.0), ("P512", 512.0), ("P1K", 1024.0), ("N1K", -1024.0),
-                        ("I025", 0.25)):
-            ts(A(name), A("ID"), x, MUL)
-
-    def more_constants():
-        ts(A("QB"), A("QC"), -8.0, MUL, -16.0, ADD)
-        ts(A("MW"), A("QC"), 4.0 / 256, MUL, 2.0 / 256, ADD)
-        ts(A("MV"), A("BO"), A("MW"), MUL)
-        ts(A("WB1"), A("BO"), A("WT"), MUL)
-        ts(A("DIAG"), A("CQF", 0, 64), A("QC"), EQ)
-        for name, x, y, tmp in (("DG", 64.0, 0.0, "X1"), ("DGX", 128.0, DUMP, "X2")):
-            ts(A(tmp), A("ROWF", 0, 64), x, MUL, y + 32768.0, ADD)
-            tt(A(tmp), A(tmp), A("DIAG"), MUL)
-            ts(A(name), A(tmp), -32768.0, ADD)
-        for name, x in (("ONS", 1.0 / 256), ("KX", 16.0), ("M16F", 1.0), ("TH2", 0.0)):
-            fill(A(name), x)
-        fill(A("WD", 0, 128, 2), -4194304.0)
-        ts(A("I256"), A("ID"), 256.0, MUL)
-        ts(A("T255"), A("TRI"), 255.0 / 256, MUL)
-        for name, x in (("BO3", 3.0 / 256), ("BO1", 1.0 / 256), ("BON", -DUMP / 256)):
-            ts(A(name), A("BO"), x, MUL)
-        fill(A("M16F", 0, 64, 16), 0.0)
-        fill(A("TH2", 0, 64, 2), -768.0)
-        fill(A("TH2", 64, 128, 2), -384.0)
-        starts(1)
-    weave(constants)
+    fill(A("Gm"), 0.0)
+    ts(A("GI"), A("PI"), 4, SHR)
+    ts(A("QI"), A("PI"), 15, AND)
+    cp(A("PC"), A("PI"))
+    cp(A("GC"), A("GI"))
+    cp(A("QC"), A("QI"))
+    ts(A("BO"), A("CGF"), A("GC"), EQ)
+    ts(A("ID"), A("ROWF"), A("PC"), EQ)
+    ts(A("B256"), A("BO"), 256.0, MUL)
+    ts(A("EQ16"), A("ROWF", 0, 32), A("QC"), EQ)
+    for name, x in (("ONE", 1.0), ("ALT", 1.0), ("ACOL", 4.0 * 613), ("BM0", 0.0), ("SGN", 1.0 / 1024)):
+        fill(A(name), x)
+    fill(A("ALT", 0, 128, 2), 0.0)
+    fill(A("SGN", 1, 16, 2), -1.0 / 1024)
+    ts(A("CN"), A("PC"), 0.0, EQ, 2.5, MUL)
+    ts(A("NEG"), A("ROWF"), 0.0, MUL, A("CN"), ADD)
+    ts(A("NEG"), A("NEG"), 64.0, ADD)
+    ts(R("LND0", None, 0), A("SP0"), -1.0, MUL, 4.0, ADD)
+    starts(0)
+    cp(R("LND0", None, 1), A("CH0"))
+    cp(A("WF"), A("WT"))
+    tt(A("CU"), A("EQ16", 0, 16), A("EQ16", 2, 18), SUB)
+    tt(A("C78"), A("EQ16", 8, 9), A("EQ16", 7, 8), SUB)
+    tt(A("CV"), A("CU"), A("SGN"), MUL)
+    ts(A("CV", 0, 1), A("C78"), 1.0 / 1024, MUL)
+    for j, x in enumerate((4.0, 0.5, 8.5)):
+        ts(A("M%d" % j), A("QC"), -1.0, MUL, x, ADD)
+    ts(A("WS"), A("WF"), 1.0 / 128, MUL)
+    ts(A("MW"), A("QC"), 4.0 / 256, MUL, 2.0 / 256, ADD)
+    for d in STAIRS:
+        for h in range(2):
+            fill(R(d + "B", h), -2.0)
+        for buf, slot, x in (("A", 0, -64.0), ("A", 1, 0.0), ("B", 2, -64.0), ("B", 3, -1.875)):
+            fill(R(d + buf, None, slot), x)
+    fill(R("KA", None, 2), -1.125)
+    ts(A("GAP0"), A("ONE"), A("M0"), MUL)
+    ts(A("GTN"), A("BO"), A("EQ16", 0, 1), MUL)
+    fill(A("GTN", 0, 128, 16), 0.0)
+    cp(A("BM0", 0, 128, 16), A("BO", 0, 128, 16))
+    ts(A("Q4"), A("QC"), -1.0, MUL, 4.0, ADD)
     for m in range(16):
         act(A("Gm", m * 129, m * 128 + 128, 16), A("BO", 0, 128, 16), IDT, 0.0, 65536.0)
+    for h in range(2):
+        ts(R("Wm", h), R("Gm", h), A("WT"), MUL, -0.25 / 65536, MUL)
+    for i in range(16):
+        act(A("TL%d" % i), A("BO"), IDT, 0.0, A("CV", (16 - i) % 16, (16 - i) % 16 + 1))
+    for name, x in (("GT0", A("EQ16", 0, 1)), ("GT8", A("EQ16", 8, 9)), ("MV", A("MW")), ("WB1", A("WF")),
+                    ("W128", A("WS")), ("BO3", 3.0 / 256), ("BO1", 1.0 / 256), ("BON", -DUMP / 256)):
+        act(A(name), A("BO"), IDT, 0.0, x)
+    for name, x in (("P512", 512.0), ("P1K", 1024.0), ("N1K", -1024.0), ("I1", 1.0), ("I4", 4.0), ("N32", -32.0),
+                    ("N256", -256.0), ("I255", 255.0), ("I256", 256.0), ("N512", -512.0), ("N101", -101.0)):
+        act(A(name), A("ID"), IDT, 0.0, x)
+    for s in (3, 4):
+        fill(A("M%d" % s), 1.0)
+        fill(A("M%d" % s, 0, 128 * s, s), 0.0)
+    fill(A("Z7", 0, 2050, 2049), 0.0)
+    for q in range(4):
+        fill(A("Z7", 512 * q + 1, 512 * q + 513, 2), 0.0)
+    ts(A("QB"), A("QC"), -8.0, MUL, -16.0, ADD)
+    ts(A("DIAG"), A("CQF", 0, 64), A("QC"), EQ)
+    ts(A("RI"), A("QI"), 2, SHR)
+    ts(A("TI"), A("QI"), 3, AND)
+    cp(A("RC"), A("RI"))
+    cp(A("TC"), A("TI"))
+    ts(A("DIA4"), A("CQ4"), A("RC"), EQ)
+    for j in (1, 2, 3):
+        ts(A("GE%d" % j), A("TC"), float(j), GE)
+    ts(A("SCA"), A("GE1"), -0.25, MUL, 1.0, ADD)
+    ts(A("BIB"), A("GE1"), 4095.5, MUL, A("GE2"), ADD)
+    ts(A("SCL"), A("GE3"), -0.25, MUL, A("SCA"), ADD)
+    ts(A("BIA"), A("GE3"), 3072.5, MUL, A("BIB"), ADD)
+    for out, x, y, tmp, diag in ((A("DG"), 64.0, 0.0, "X0", "DIA4"), (R("CM", None, 3), 128.0, DUMP, "X2", "DIAG")):
+        ts(A(tmp), A("ROWF", 0, 64), x, MUL, y + 32768.0, ADD)
+        tt(A(tmp), A(tmp), A(diag), MUL)
+        ts(out, A(tmp), -32768.0, ADD)
+    for j, (x, y) in enumerate(((-127.0 / 256, 0.0), (ROUND, 1.0), (-ROUND, 1.0), (None, -128.0))):
+        if x:
+            fill(R("CM", None, j), x)
+        fill(R("MM", None, j), y)
+    for name, x in (("ONS", 1.0 / 256), ("KX", 16.0), ("M16F", 1.0), ("M4F", 1.0), ("TH2", 0.0)):
+        fill(A(name), x)
+    fill(A("M4F", 0, 64, 4), 0.0)
+    fill(A("WD", 0, 128, 2), -4194304.0)
+    fill(A("M16F", 0, 64, 16), 0.0)
+    for ps, a, b, on in PARTS:
+        fill(A("TH2", 2 * a, 2 * b, 2), -768.0 if on == "s" else -384.0)
     pick(A("TRI"), A("B256"), [[1, 128]], GE, 0.0, 0, -1)
     pick(A("tm7"), A("BO"), [[1, 128]], GT, 1.0 / 16, 0, -1)
     pick(A("tm8"), A("tm7"), [[1, 128]], NE, -31.0 / 32, 0, -1)
-    for t in range(1, RO):
-        send("ST0", "ST%d" % t, "st%d" % t, t, [A("ST0")], [A("ST%d" % t)])
-    resets("M3", 768, 3, 0, 1)
+    tt(A("ALF"), A("tm8"), A("BO"), MUL)
+    ts(A("T255"), A("TRI"), 255.0 / 256, MUL)
     for l in range(1, 5):
         pick(A("SH%d" % l), A("BO"), [[-1, 128]], EQ, 0.0, -l, 1)
     iota(A("K5"), [[0, 64], [-256, 5]])
     resets("M5", 320, 5, 0, 1)
     resets("M8", 256, 8, 1024, 0)
     resets("LM", 640, 10, 1024, 0)
-    waiting = spaced(more_constants)
+    for t in range(1, RO):
+        send(A("ST0"), A("ST%d" % t), "st%d" % t, t, FIRST if t == 1 else 300, FIRST)
+    msum(A("psC", 0, 64), [("ID", A("STH")), ("ID", A("STL")), ("N512", R("LND0", None, 0)),
+                           ("N101", R("LND0", None, 0))])
+    ts(A("S0"), A("psC", 0, 64), A("ACOL"), ADD)
+    ts(A("SI"), A("S0"), W - 1, AND)
+    cp(A("OFFZ"), A("SI"))
 
-    def spare():
-        for _ in range(min(2, len(waiting))):
-            run(*waiting.pop(0))
-
-    def late_constants(k):
-        if k == 1:
-            tt(A("ALF"), A("tm8"), A("BO"), MUL)
-            spare()
-            spare()
-        if k in (0, 1, 2, 4):
-            name, slot, x = {0: ("D2", 0, -1024.0), 1: ("D2", 1, 0.0), 2: ("D2", 2, 0.0), 4: ("G2", 3, -1.0)}[k]
-            act(A(name, slot, 4096, 4), A("Gm", 0, 1024), IDT, x, 0.0)
-        if k >= 5:
-            a = 1024 * (k - 5)
-            actcp(A("X", W + a, W + a + 1024), A("X", a, a + 1024))
-
-    ZAT = [("G0", 3, 0), ("G0", 3, 1), ("G0", 3, 2), ("G1", 3, 1), ("G1", 3, 2), ("G2", 4, 1), ("G2", 4, 2),
+    ZAT = [("G0", 3, 0), ("G0", 3, 1), ("G0", 3, 2), ("G1", 4, 1), ("G1", 4, 2), ("G2", 3, 1), ("G2", 3, 2),
            ("Z7", 2, 2)]
 
-    def gz(eng, k, piece, width=W):
-        i0, i1 = (Z_SCALAR if eng is actcp else Z_VECTOR)[k][piece:piece + 2]
-        b, s, o = ZAT[k]
-        eng(A(b, 16 * s * i0 + o, 16 * s * i1 + o - s + 1, s), IND(A("X", 0, width), A("OFFZ", i0, i1)))
+    def Z(k, a, b, step=1):
+        buf, s, o = ZAT[k]
+        return A(buf, s * a + o, s * b + o - s + 1, s * step)
+
+    def gather(k, h, width=W):
+        x = Z_SCALAR[k][h]
+        for eng, i0, i1 in ((actcp, 0, x), (cp, x, 32)):
+            if i1 > i0:
+                i0, i1 = 32 * h + i0, 32 * h + i1
+                eng(Z(k, 16 * i0, 16 * i1), IND(A("X", 0, width), A("OFFZ", i0, i1)))
 
     def table(k):
-        return ("K", 8, 10) if k == 1 else ("T" if k < 5 else "U", 16, 19 - k)
+        return ("K", 8, 11) if k == 1 else ("T" if k < 5 else "U", 16, 20 - k)
 
-    def heights(d, a, b):
-        for i in range(a, b):
-            act(A3(d + "A", 3 + i), A("ps6" if i < 7 else "psP", 64 * (i % 7), 64 * (i % 7) + 64), IDT, -0.25)
+    def steps_at(i):
+        return A("psD1" if i < 7 else "psY", 64 * (i % 7), 64 * (i % 7) + 64)
 
-    def ustart(k):
-        if k < 7:
-            terms = [(A("DM%d" % min(k, 2)), A("ONE"))]
-            if k:
-                d = table(k)[0]
-                terms += [(A("I4"), A3(d + "B", 0)), (A("I4"), A3(d + "A", 2))]
-            for j, (l, r) in enumerate(terms):
-                mm(A("psW", 128, 192), l, r, j == 0, j == len(terms) - 1)
-        mm(A("psW", 0, 128), A("NEG"), A("ALT"), True, False)
+    def uwrap(k, ps, a, b):
+        msum(A(ps, 1, (b - a) // 8, 2), [(A("Wm", m * 128, m * 128 + 128), Z(k, a + m, b, 16)) for m in range(16)],
+             False)
 
-    def uwrap(k):
-        b, s, o = ZAT[k]
-        for m in range(16):
-            mm(A("psW", 1, 128, 2), A("Wm", m * 128, m * 128 + 128), A(b, s * m + o, 1024 * s + o - s + 1, 16 * s),
-               False, m == 15)
-
-    def entries(k, src, off, on):
-        outs = [(A("CB"), 8.0, 2.0)]
-        if k < 7:
-            outs += [(A("AD", 0, 128, 2), 1.0, 148.5), (A("AD", 1, 128, 2), 6.0, 16680.75)]
-        for out, x, y in outs:
-            if on == "s":
-                act(out, src, IDT, y + x * off, x)
-            else:
-                ts(out, src, x, MUL, y + x * off, ADD)
-
-    def maxima(j, q):
-        if j < 2:
-            r = (768 * q, 768 * q + 768)
-            scan(A("O%d" % j, *r), A("M3"), A("G%d" % j, *r), MUL, MAX)
-            s = 3 + j
-            gcp(A("G%d" % (j + 1), 256 * s * q, 256 * s * (q + 1), s), A("O%d" % j, r[0] + 2, r[1], 3), 256)
-        else:
-            r = (512 * q, 512 * q + 512)
-            scan(A("O2", *r), A("D2", *r), A("G2", *r), ADD, MAX)
-
-    def arith(k, between):
-        d = table(k + 1)[0]
-        scan(A("YI"), A("psW", 0, 128), A("AD"), MUL, ADD)
-        tt(A("DH"), A("psW", 1, 128, 2), A("CB"), ADD)
-        between(0)
-        ts(A("SI"), A("YI", 1, 128, 2), 2, SHR, W - 1, AND)
-        ts(A("N4"), A("DH"), 3, SHR, 3, AND)
-        between(1)
-        cp(A("OFFZ"), A("SI"))
-        tt(A3(d + "A", 1), A("N4"), A("psW", 128, 192), LT)
-        ts(A3(d + "A", 2), A("N4"), -0.25, MUL)
-
-    def stairs(k):
-        d = table(k)[0]
-        scan(A(d + "O"), A(d + "A"), A(d + "B"), ADD, MAX)
-
-    def csum(k, C):
+    def entry(k, h, C):
         d, top, s = table(k)
-        terms = [(A("GT8"), C)] if k == 1 else []
-        terms += [(A("P512" if j == 2 else "N1K" if j % 2 else "P1K"), A3(d + "O", j)) for j in range(2, s)]
-        for j, (l, r) in enumerate(terms):
-            mm(A("psC", 0, 64), l, r, j == 0, j == len(terms) - 1)
-        return 960.0 - 2048.0 * ((s - 3) % 2)
+        src = A("psC", 0, 64) if h is None else A("psC", 32 * h, 32 * h + 32)
+        msum(src, ([("GT8", C)] if k == 1 else [])
+             + [("P512" if j == 3 else "P1K" if j % 2 else "N1K", R(d + "O", h, j)) for j in range(3, s)])
+        return src, 960.0 - 2048.0 * (s % 2)
 
-    def bases(k, LB):
+    def entries(k, h, src, off):
+        for slot, x, y in ((1, 14.0, 17868.75), (0, -4.0, -594.0))[:2 if k < 7 else 1]:
+            act(R("AD", h, slot), src, IDT, y + x * off, x)
+
+    def maxima(j, h):
+        s, s1 = (3, 4, 3)[j], 4 - j
+        for a in range(512 * h, 512 * h + 512, PIECE):
+            r = (s * a, s * (a + PIECE))
+            scan(A("O%d" % j, *r), A("M%d" % s, 0, s * PIECE), A("G%d" % j, *r), MUL, MAX)
+        for a in range(512 * h, 512 * h + 512 if j < 2 else 0, 256):
+            gcp(A("G%d" % (j + 1), s1 * a, s1 * (a + 256), s1), A("O%d" % j, s * a + s - 1, s * (a + 256), s))
+
+    def bases(k, h, height, log):
         d = table(k)[0]
-        was, less = A3(d + "B", 0), A3(d + "A", 2)
-        for j in range(2 if k < 7 else 1):
-            mm(A("ps3", j, 128, 2), A("I1"), was, True, False)
-            if j:
-                mm(A("ps3", j, 128, 2), A("I025"), LB, False, False)
-            mm(A("ps3", j, 128, 2), A("I1"), less, False, True)
-        mm(A("ps3", 128, 192), A("N32"), was, True, False)
-        mm(A("ps3", 128, 192), A("I4"), less, False, True)
+        was, less = R(d + "A", h, 2), R(d + "A", h, 3)
+        msum(height, [("I1", was), ("I1", less)])
+        msum(log, [("N32", was), ("I4", less)])
 
-    def logact(k):
-        if k < 6:
-            for j in range(2):
-                act(A3(table(k + 2)[0] + "B", j), A("ps3", j, 128, 2), IDT, 1.75 if k == 0 else -0.25)
+    def head(t):
+        LB, C = R("LND%d" % t, None, 0), R("LND%d" % t, None, 1)
+        if t:
+            msum(A("psC", 0, 64), [("ID", A("STH")), ("ID", A("STL"))], True, False)
+            msum(A("psC", 0, 64), [("N512", LB), ("N101", LB)], False)
+        mm(A("psB1", 128, 192), A("GT0"), LB)
+        fixed[0] = True
+        if t:
+            ts(A("OFFZ"), A("psC", 0, 64), A("ACOL"), ADD)
+        ts(A("EQ0"), A("psB1", 128, 192), A("Q4"), EQ)
+        ts(R("KB", None, 1), LB, 0.25, MUL)
+        tt(A("SEL"), A("EQ0"), C, MUL)
+        for h in range(2):
+            gather(0, h, W + AGAIN if t else W)
+        fixed[0] = False
+        for j in range(7):
+            mm(A("psD0", 64 * j, 64 * j + 64), A("TL%d" % (9 + j if j else 0)), C)
+        msum(A("psB0", 128, 192), [("GTN", C), ("BM0", A("SEL"))])
+        entries(0, None, A("psB0", 128, 192), 0)
+        for h in range(2):
+            mm(A("psW%d" % h, 0, 64), A("NEG"), A("ALT", 0, 64), True, False)
+            uwrap(0, "psW%d" % h, 512 * h, 512 * h + 512)
+        for j in range(7):
+            ts(R("KA", None, 4 + j), A("psD0", 64 * j, 64 * j + 64), -0.25, ADD)
+        for i in range(14):
+            mm(steps_at(i), A("TL%d" % (i + 1)), C)
+        for i in range(14):
+            ts(R("TA", None, 4 + i), steps_at(i), -0.25, ADD)
+        for i in range(11):
+            gcp(R("UA", None, 4 + i), R("TA", None, 4 + i))
+        for d in "TU":
+            act(R(d + "B", None, 1), LB, IDT, 0.0, 0.25)
+        act(A("W1"), LB, SQUARE, 3.1, -1.0)
+        act(A("W2"), A("W1"), SQUARE)
+        act(R("WD", None, 1), A("W2"), SQUARE)
+        act(R("LG", None, 9), LB, IDT, 4.0, -1.0)
+
+    def beat(t, k, h):
+        C, ps, pb = R("LND%d" % t, h, 1), "psW%d" % h, "psB%d" % h
+        d, top, s = table(k)
+        fixed[0] = True
+        scan(R("YI", h), A(ps, 0, 64), R("AD", h), MUL, ADD)
+        tt(R("DH", h), A(ps, 1, 64, 2), R("AD", h, 1), ADD)
+        ts(R("SI", h), R("YI", h, 1), 2, SHR, W - 1, AND)
+        ts(R("N4", h), R("DH", h), 1, SHR, 3, AND)
+        cp(R("OFFZ", h), R("SI", h))
+        tt(R(d + "B", h, 0), R("N4", h), R("GAP" if k > 1 else "GAP0", h), GT)
+        ts(R(d + "A", h, 3), R("N4", h), 0.25, MUL, -0.75, ADD)
+        gather(k, h)
+        if k < 7:
+            mm(A(ps, 0, 64), A("NEG"), A("ALT", 0, 64), True, False)
+            bases(k, h, A(pb, 0, 32), A(pb, 64, 96))
+            scan(R(d + "O", h), R(d + "A", h), R(d + "B", h), ADD, MAX)
+            c = entry(k, h, C)
+            act(R("GAP", h), A(pb, 0, 32), IDT, A("M%d" % min(k, 2)), -4.0)
+            act(R(table(k + 1)[0] + "A", h, 2), A(pb, 0, 32), IDT, 1.75 if k == 1 else -0.25)
+            act(R("LG", h, 9 - k), A(pb, 64, 96), IDT, 8.0 * top - 81)
+            entries(k, h, *c)
+            uwrap(k, ps, 512 * h, 512 * h + 512)
+        fixed[0] = False
+        if k in (2, 4, 6):
+            maxima(k // 2 - 1, h)
+
+    def tail(t):
+        last = t == RO - 1
+        LB, C, F = R("LND%d" % t, None, 0), R("LND%d" % t, None, 1), A("F%d" % t)
+        OH, VV = R("LG", None, 0), R("VO", None, 3)
+        bases(7, None, A("psB0", 0, 64), A("psB0", 64, 128))
+        act(A("PRE"), A("psB0", 0, 64), IDT, 52.0, -32.0)
+        act(R("LG", None, 2), A("psB0", 64, 128), IDT, 47.0)
+        mm(A("psW1", 0, 128), A("NEG"), A("ALT"), True, False)
+        mm(A("psB1", 128, 256), A("I256"), A("TH2"), True, False)
+        for ps, a, b, on in PARTS:
+            mm(A(ps, 0, 16 * (b - a)), A("N256"), A("G1", 64 * a + 3, 64 * b, 4), True, False)
+            mm(A(ps, 0, 16 * (b - a)), A("I255"), A("O2", 48 * a + 2, 48 * b, 3), False, False)
+        fixed[0] = True
+        for j, (ps, a, b, on) in enumerate(PARTS):
+            a, b = 16 * a, 16 * b
+            mm(A(ps, 0, b - a), A("ID"), Z(7, a, b), False, True)
+            if on == "s":
+                act(A("GEb", a, b), A(ps, 0, b - a), SIGN, -0.5)
+            else:
+                ts(A("GEb", a, b), A(ps, 0, b - a), 0.5, GE, -0.5, ADD)
+            if j == 0:
+                scan(A("UO"), A("UA"), A("UB"), ADD, MAX)
+        uwrap(7, "psW1", 0, 1024)
+        c = entry(7, None, C)
+        msum(A("psB1", 128, 256, 2), [(A("Gm", m * 128, m * 128 + 128), A("GEb", m, 1024, 16)) for m in range(16)],
+             False)
+        fixed[0] = False
+        entries(7, None, *c)
+        actcp(A("O1", 0, 4096, 64), F)
+        act(A("G2", 0, 3072, 48), F, IDT, 0.0, 0.0)
+        tt(A("DH"), A("psW1", 1, 128, 2), R("AD", None, 1), ADD)
+        ts(A("N4"), A("DH"), 1, SHR, 3, AND)
+        mm(A("psW1", 128, 192), A("ID"), A("DG"), True, False)
+        mm(A("psB0", 0, 320), A("ID"), A("K5"), True, False)
+        for l in range(5):
+            mm(A("psB0", l, 320, 5), A("SH%d" % l if l else "ID"), C, False, False)
+        mm(A("psW0", 0, 256), A("ID"), A("CM"), True, False)
+        scan(A("WO"), A("WD"), A("psB1", 128, 256), MIN, MAX)
+        tt(R("LG", None, 1), A("PRE"), A("N4"), ADD)
+        mm(A("psD0", 0, 64), A("ALF"), R("WO", None, 1))
+        ts(OH, A("psD0", 0, 64), 0.0, LT, 256.0, MUL)
+        mm(A("psW1", 128, 192), A("MV"), OH, False, True)
+        mm(A("psW1", 192, 256), A("BO3"), OH)
+        mm(A("psC", 128, 192), A("BO1" if last else "ONS"), OH)
+        mm(A("psW0", 3, 256, 4), A("BON"), A("KX") if last else OH, False, False)
+        scan(A("OHL"), A("LM"), A("LG"), ADD, MIN)
+        fixed[0] = True
+        for s in range(8):
+            mm(A("psD1", s, 512, 8), A("BO"), R("OHL", None, 1 + s))
+        together(-8)
+        for l in range(5):
+            mm(A("psB0", l, 320, 5), A("TRI"), R("OHL", None, 9), False, l == 4)
+        mm(A("psB0", 320, 384), A("T255"), R("OHL", None, 9))
+        together(-6)
+        fixed[0] = False
+        scan(A("SD"), A("M4F"), A("psW1", 128, 192), MUL, MAX)
+        tt(A("psC", 192, 256), A("psW1", 192, 256), LB, MAX)
+        if last:
+            actcp(A("NOK"), A("psC", 128, 192))
         else:
-            act(A("PRE"), A("ps3", 0, 128, 2), IDT, 55.0, -32.0)
-        act(A("LG", 8 - k, 640, 10), A("ps3", 128, 192), IDT, 8.0 * table(k + 1)[1] - 81)
-
-    ysn = [0]
-
-    def ysum(cnt):
-        for _ in range(min(cnt, 128 - ysn[0])):
-            c = ysn[0]
-            mm(A("psY", 0, 64), A("ID"), A("X", c, W, 128), c == 0, c == 127)
-            ysn[0] += 1
-
-    PLAN = {2: [(0, 0), (0, 1)], 3: [(0, 2), (0, 3)], 4: [(1, 0), (1, 1)], 5: [(1, 2), (1, 3)],
-            6: [(2, 0), (2, 1), (2, 2)]}
+            act(A("PR"), A("psC", 128, 192), IDT, 4 * 613 / 64, 1.0, A("ACOL"))
+        for h in range(2):
+            act(R("AS", h), R("psD1", h), ABS, A("QB"))
+            scan(R("AO", h), A("M8"), R("AS", h), ADD, MIN)
+        ts(A("OV"), A("SD", 3, 64, 4), A("SCL"), MUL, A("BIA"), ADD)
+        cp(A("V4"), IND(Ap((T["ZV"][:], A("O1")[1] + A("G2")[1] + A("Z7")[1])), A("OV")))
+        ts(A("AL"), A("psB0", 0, 320), 0.0, MAX, 255.0, MIN)
+        scan(A("ALO"), A("M5"), A("AL"), MUL, ADD)
+        scan(A("VO"), A("M4", 0, 256), A("V4"), MUL, MAX)
+        mm(A("psW0", 0, 256, 4), A("W128"), VV, False, False)
+        mm(A("psW0", 3, 256, 4), A("WB1"), VV, False, True)
+        tt(A("YB") if last else R("SND%d" % t, None, 0), R("AO", None, 7), A("psC", 192, 256), MIN)
+        tt(A("YC") if last else R("SND%d" % t, None, 1), R("ALO", None, 4), A("psB0", 320, 384), SUB)
+        if last:
+            act(A("YL"), A("YB"), IDT, 4.0, -1.0)
+            tt(A("DIF"), VV, A("psC", 128, 192), MUL)
+        else:
+            send(A("SND%d" % t), A("LND%d" % (t + 1)), "arr%d" % (t + 1), 1)
+            for h in range(2):
+                actcp(R("VP", h), VV)
+        scan(A("X1"), A("MM"), A("psW0", 0, 256), MUL, ADD)
+        tt(A("FVI"), F, VV, ADD)
+        scan(A("SD2"), A("M16F"), R("X1", None, 3), MUL, MAX)
+        ts(A("FH"), A("FVI"), 1, SHR)
+        cp(A("OX", 0, 4), A("SD2", 15, 64, 16))
+        cp(A("F%d" % (t + 1)), A("FH"))
+        if last:
+            tt(A("psW1", 0, 64), A("psY", 0, 64), A("DIF"), ADD)
+            tt(A("SEL"), IND(A("X", 0, W), A("OX", 0, 4)), A("NOK"), MUL)
+            tt(A("YS"), A("psW1", 0, 64), A("SEL"), SUB)
+        else:
+            ts(A("OX", 4, 8), A("SD2", 15, 64, 16), float(W), ADD)
+            cp(IND(A("X"), A("OX")), A("VP"))
 
     for t in range(RO):
-        last = t == RO - 1
-        C, LB, F = A("C%d" % t), A("LB%d" % t), A("F%d" % t)
-        sndC, sndL = "SC%d" % t, "SL%d" % t
-        ustart(0)
-        mm(A("psC", 0, 64), A("ID"), A("STH"), True, False)
-        mm(A("psC", 0, 64), A("ID"), A("STL"), False, False)
-        mm(A("psC", 0, 64), A("N512"), LB, False, False)
-        mm(A("psC", 0, 64), A("N101"), LB, False, True)
-        mm(A("ps4", 0, 64), A("GT0"), LB)
-        act(A("NF"), F, IDT, 0.0, -1.0)
-        if t == 0:
-            rest = spaced(step_constants)
-            for j, call in enumerate(collect(first_places)):
-                for c in [call] + rest[4 * j:4 * j + 4 if j < 2 else None]:
-                    run(*c)
-            act(A("WD", 1, 128, 2), LB, EXP, 9.0, -3.0)
-            late_constants(0)
-        else:
-            ts(A("OFFZ"), A("psC", 0, 64), A("ACOL"), ADD)
-        for ps, first in (("ps5", 8), ("ps6", 0), ("psP", 7)):
-            for j in range(7):
-                mm(A(ps, 64 * j, 64 * j + 64), A("TL%d" % (first + j + 1 if j or ps != "ps5" else 0)), C)
-        ts(A3("KB", 1), LB, 0.25, MUL, -1.125, ADD)
-        ts(A("EQ0"), A("ps4", 0, 64), A("Q4"), EQ)
-        if t == 0:
-            ts(A("Wm"), A("Gm"), A("WT"), MUL, 1.0 / 65536, MUL)
-        gz(actcp, 0, 0, W + AGAIN if t else W)
-        gz(cp, 0, 0, W + AGAIN if t else W)
-        tt(A("SEL"), A("EQ0"), C, MUL)
-        gz(cp, 0, 1, W + AGAIN if t else W)
-        mm(A("ps4", 0, 64), A("GTN"), C, True, False)
-        mm(A("ps4", 0, 64), A("BM0"), A("SEL"), False, True)
-        uwrap(0)
-        entries(0, A("ps4", 0, 64), 0, "v")
-        for j in range(7):
-            ts(A3("KA", 3 + j), A("ps5", 64 * j, 64 * j + 64), -0.25, ADD)
-        heights("T", 0, 7)
-        if t == 0:
-            act(A("Z7", 1, 2049, 2), A("Gm", 0, 1024), IDT, 0.0, 0.0)
+        act(A("NF"), A("F%d" % t), IDT, -1.0)
         for m in range(16):
-            gcp(A("D2", 4 * m + 3, 4096, 64), A("NF"), 64)
+            gcp(A("G1", 4 * m + 3, 4096, 64), A("NF"))
+        head(t)
+        if t == 0:
+            for a in range(0, AGAIN, 256):
+                actcp(A("X", W + a, W + a + 256), A("X", a, a + 256))
+        if t < RO - 1:
+            starts(t + 1)
+        else:
+            for c in range(128):
+                mm(A("psY", 0, 64), A("ID"), A("X", c, W, 128), c == 0, c == 127)
         for k in range(1, 8):
-            arith(k - 1, lambda piece: maxima(2, 3 + piece) if k == 7 else spare())
-            for piece in range(len(Z_SCALAR[k]) - 1):
-                gz(actcp, k, piece)
-            if last:
-                ysum(19)
-            ustart(k)
-            bases(k, LB)
-            if k == 6:
-                mm(A("ps4"), A("ID"), A("D2", 3, 2048, 4), True, False)
-                mm(A("ps5", 0, 256), A("ID"), A("D2", 2048 + 3, 3072, 4), True, False)
-            if k == 7:
-                break
-            gz(cp, k, 0)
-            stairs(k)
-            gz(cp, k, 1)
-            off = csum(k, C)
-            uwrap(k)
-            logact(k - 1)
-            entries(k, A("psC", 0, 64), off, "s")
-            for j, q in PLAN.get(k, ())[:-1]:
-                maxima(j, q)
-            if k in (2, 3):
-                heights("U", *{2: (0, 5), 3: (5, 11)}[k])
-            if k == 1:
-                heights("T", 7, 14)
-                act(A("LG", 9, 640, 10), LB, IDT, 4.0, -1.0)
-                if t and not last:
-                    weave(lambda: starts(t + 1), 2)
-            if k == 2 and t:
-                act(A("WD", 1, 128, 2), LB, EXP, 9.0, -3.0)
-            for j, q in PLAN.get(k, ())[-1:]:
-                maxima(j, q)
-            if t == 0:
-                late_constants(k)
-        mm(A("ps6", 0, 128), A("I256"), A("TH2"), True, False)
-        mm(A("ps4"), A("I256"), A("O2", 3, 2048, 4), False, False)
-        mm(A("psP", 0, 256), A("ID"), A("D2", 3072 + 3, 4096, 4), True, False)
-        for q in (5, 6, 7):
-            maxima(2, q)
-        gz(cp, 7, 0)
-        stairs(7)
-        mm(A("ps5", 0, 256), A("I256"), A("O2", 2048 + 3, 3072, 4), False, False)
-        mm(A("ps4"), A("ID"), A("Z7", 2, 1025, 2), False, True)
-        mm(A("psP", 0, 256), A("I256"), A("O2", 3072 + 3, 4096, 4), False, False)
-        for q, ps in ((2, "ps5"), (3, "psP")):
-            mm(A(ps, 0, 256), A("ID"), A("Z7", 512 * q + 2, 512 * q + 513, 2), False, True)
-        act(A("GEb", 0, 512), A("ps4"), SIGN, 256.5)
-        for q, ps in ((2, "ps5"), (3, "psP")):
-            ts(A("GEb", 256 * q, 256 * q + 256), A(ps, 0, 256), -256.5, GE, -0.5, ADD)
-        off = csum(7, C)
-        uwrap(7)
-        entries(7, A("psC", 0, 64), off, "v")
-        for m in range(16):
-            mm(A("ps6", 0, 128, 2), A("Gm", m * 128, m * 128 + 128), A("GEb", m, 1024, 16), False, m == 15)
-        logact(6)
-        actcp(A("O2", 0, 4096, 64), F)
-        if t == 0:
-            late_constants(7)
-        tt(A("DH"), A("psW", 1, 128, 2), A("CB"), ADD)
-        ts(A("N4"), A("DH"), 3, SHR, 3, AND)
-        scan(A("WO"), A("WD"), A("ps6", 0, 128), MIN, MAX)
-        tt(A("LG", 1, 640, 10), A("PRE"), A("N4"), SUB)
-        mm(A("ps4", 0, 320), A("ID"), A("K5"), True, False)
-        mm(A("psW", 0, 64), A("ID"), A("DG"), True, False)
-        mm(A("psC", 0, 64), A("ALF"), A("WO", 1, 128, 2))
-        OH = A("LG", 0, 640, 10)
-        ts(OH, A("psC", 0, 64), 0.0, LT, 256.0, MUL)
-        for l in range(5):
-            mm(A("ps4", l, 320, 5), A("SH%d" % l if l else "ID"), C, False, False)
-        mm(A("ps6", 0, 64), A("ID"), A("DGX"), True, False)
-        mm(A("psW", 0, 64), A("MV"), OH, False, True)
-        mm(A("psW", 64, 128), A("BO3"), OH)
-        mm(A("ps6", 0, 64), A("BON"), A("KX") if last else OH, False, True)
-        mm(A("psP", 0, 64), A("BO1" if last else "ONS"), OH)
-
-        def choose():
-            scan(A("OHL"), A("LM"), A("LG"), ADD, MIN)
-            for s in range(8):
-                mm(A("ps5", s, 512, 8), A("BO"), A("OHL", 1 + s, 640, 10))
-            for l in range(5):
-                mm(A("ps4", l, 320, 5), A("TRI"), A("OHL", 9, 640, 10), False, l == 4)
-            mm(A("ps4", 320, 384), A("T255"), A("OHL", 9, 640, 10))
             for h in range(2):
-                act(A("AS", 256 * h, 256 * h + 256), A("ps5", 256 * h, 256 * h + 256), ABS, A("QB"))
+                beat(t, k, h)
+        tail(t)
+    dma("y", "oC", T.yc[:], A("YC")[0], [], [A("YC")])
+    dma("s", "oL", T.yl[:], A("YL")[0], [], [A("YL")])
+    dma("y", "oF", T.yf[:], T["F4"][:], [], [A("F4")])
+    dma("y", "oS", T.ys[:], T["YS"][:], [], [A("YS")])
 
-        def spans(h):
-            scan(A("AO", 256 * h, 256 * h + 256), A("M8"), A("AS", 256 * h, 256 * h + 256), ADD, MIN)
-
-        if not last:
-            choose()
-            scan(A("SD"), A("M16F"), A("psW", 0, 64), MUL, MAX)
-            tt(A("ps3", 0, 64), A("psW", 64, 128), LB, MAX)
-            cp(A("OV"), A("SD", 15, 64, 16))
-            ts(A("OZ"), A("SD", 15, 64, 16), 0.5, MUL, 1.0, ADD)
-            act(A("PR"), A("psP", 0, 64), IDT, 4 * 613 / 64, 1.0, A("ACOL"))
-            cp(A("VV6"), IND(A("O2"), A("OV")))
-            ts(A("AL"), A("ps4", 0, 320), 0.0, MAX, 255.0, MIN)
-            tt(A("VV"), IND(A("Z7"), A("OZ")), A("VV6"), MAX)
-            mm(A("psC", 0, 64), A("WB1"), A("VV"))
-            spans(0)
-            scan(A("ALO"), A("M5"), A("AL"), MUL, ADD)
-            spans(1)
-            actcp(A("VW"), A("VV"))
-            tt(A(sndC), A("ALO", 4, 320, 5), A("ps4", 320, 384), SUB)
-            cp(A("HI"), A("psC", 0, 64))
-            tt(A(sndL), A("AO", 7, 512, 8), A("ps3", 0, 64), MIN)
-            send("SND%d" % t, "LND%d" % (t + 1), "arr%d" % (t + 1), 1, [A(sndL), A(sndC)],
-                 [A("LB%d" % (t + 1)), A("C%d" % (t + 1))])
-            ts(A("HM"), A("HI"), 127, AND)
-            tt(A("FVI"), F, A("VV"), ADD)
-            tt(A("X1"), A("ps6", 0, 64), A("HM"), ADD)
-            ts(A("FH"), A("FVI"), 1, SHR)
-            scan(A("SD2"), A("M16F"), A("X1"), MUL, MAX)
-            cp(A("F%d" % (t + 1)), A("FH"))
-            cp(A("OX", 0, 4), A("SD2", 15, 64, 16))
-            ts(A("OX", 4, 8), A("SD2", 15, 64, 16), float(W), ADD)
-            twice = Ap((T["SMALL"][:, POOL["VV"][1]:POOL["VV"][1] + 128], A("VV")[1] + A("VW")[1]))
-            cp(IND(A("X"), A("OX")), twice)
-        else:
-            scan(A("SD"), A("M16F"), A("psW", 0, 64), MUL, MAX)
-            choose()
-            cp(A("OV"), A("SD", 15, 64, 16))
-            ts(A("OZ"), A("SD", 15, 64, 16), 0.5, MUL, 1.0, ADD)
-            tt(A("EE"), A("psW", 64, 128), LB, MAX)
-            cp(A("VV6"), IND(A("O2"), A("OV")))
-            cp(A("NOK"), A("psP", 0, 64))
-            tt(A("VV"), IND(A("Z7"), A("OZ")), A("VV6"), MAX)
-            mm(A("psC", 0, 64), A("WB1"), A("VV"))
-            ts(A("AL"), A("ps4", 0, 320), 0.0, MAX, 255.0, MIN)
-            tt(A("FVI"), F, A("VV"), ADD)
-            cp(A("HI"), A("psC", 0, 64))
-            spans(0)
-            ts(A("FH"), A("FVI"), 1, SHR)
-            ts(A("HM"), A("HI"), 127, AND)
-            tt(A("DIF"), A("VV"), A("psP", 0, 64), MUL)
-            spans(1)
-            tt(A("X1"), A("ps6", 0, 64), A("HM"), ADD)
-            cp(A("F4"), A("FH"))
-            scan(A("ALO"), A("M5"), A("AL"), MUL, ADD)
-            scan(A("SD2"), A("M16F"), A("X1"), MUL, MAX)
-            tt(A(sndL), A("AO", 7, 512, 8), A("EE"), MIN)
-            tt(A(sndC), A("ALO", 4, 320, 5), A("ps4", 320, 384), SUB)
-            cp(A("OX", 0, 4), A("SD2", 15, 64, 16))
-            tt(A("psP", 64, 128), A("psY", 0, 64), A("DIF"), ADD)
-            act(A("YL"), A(sndL), IDT, 4.0, -1.0)
-            tt(A("SEL"), IND(A("X", 0, W), A("OX", 0, 4)), A("NOK"), MUL)
-            tt(A("YS"), A("psP", 64, 128), A("SEL"), SUB)
-            dma("y", "oF", T.yf[:], T["F4"][:], [], [A("F4")])
-            dma("y", "oC", T.yc[:], A(sndC)[0], [], [A(sndC)])
-            dma("s", "oL", T.yl[:], A("YL")[0], [], [A("YL")])
-            dma("y", "oS", T.ys[:], T["YS"][:], [], [A("YS")])
+    if not ORDER:
+        ORDER.extend(plan(calls))
+    for i in ORDER:
+        if i >= loads:
+            calls[i][5]()
 
     wait("g", "loc", sent[0])
     for t in range(1, RO):

@@ -42,12 +42,13 @@ _pool("TL", " ".join("TL%d" % k for k in range(16)), 128, "bfloat16")
 _pool("MATS", "ID BO BO3 BO1 BON B256 WB1 SH1 SH2 SH3 SH4 GT0 GTN BM0 GT8 NEG ONS I256 I255 ALF TRI T255 MV "
               "N256 W128 N512 N101 tm7 tm8 WD WO VP TH2 ALT", 128, "bfloat16")
 _pool("HMATS", "I1 I4 N32 P512 P1K N1K", 128, "float16")
-_pool("SMALL", "ONE SP0 CH0 NF PRE DIF DG KX YL YB YC EQ0 SEL STH STL NOK GAP GAP0", 64, "bfloat16")
+_pool("SMALL", "ONE SP0 CH0 NF EE PRE DIF DG KX YL YB YC EQ0 SEL STH STL NOK GAP GAP0", 64, "bfloat16")
 for _n, _s in STAIRS.items():
     _d("%sA %sB %sO" % (_n, _n, _n), 64 * _s, "float16")
-_d("LG OHL LM", 640, "bfloat16")
+_d("LG OHL", 640, "bfloat16")
 _d("AS AO", 512, "bfloat16")
-_d("K5 M5 AL", 320, "bfloat16")
+_d("K5 M5", 160, "bfloat16")
+_d("LM AL", 320, "bfloat16")
 _d("ALO", 320, "float16")
 _d("F0 F1 F2 F3 F4", 64, "bfloat16")
 _d("LND0 LND1 LND2 LND3 SND0 SND1 SND2", 128, "bfloat16")
@@ -68,12 +69,13 @@ _d("OX", 8, "uint16")
 _d("psW0 psW1 psD0 psD1 psB0 psB1 psC psY", 512, "float32", "psum")
 
 SEMAPHORES = ["qv", "qs", "qt", "qg", "dX", "dW", "dC", "dL", "dS", "dF", "oC", "oL", "oF", "oS", "loc"]
-SEMAPHORES += ["%s%d" % (s, t) for s in ("st", "arr") for t in range(1, RO)]
+SEMAPHORES += ["st%d" % t for t in range(1, RO)] + ["arr%d%d" % (t, h) for t in range(1, RO) for h in range(2)]
 
-Z_SCALAR = [(20, 24), (28, 28), (32, 32), (32, 32), (32, 32), (32, 32), (32, 32), (32, 20)]
+Z_SCALAR = [(18, 24), (28, 28), (32, 32), (32, 32), (32, 32), (32, 32), (32, 32), (32, 16)]
 PIECE = 64
-PARTS = (("psD0", 0, 32, "v"), ("psD1", 32, 48, "s"), ("psW0", 48, 64, "v"))
-WAIT, GATHER, REMOTE, FIRST, LOAD, TABLE = 230.0, 1.3, 3000.0, 2500.0, 1400.0, 4500.0
+PARTS = (("psD0", 0, 32, "s"), ("psD1", 32, 48, "s"), ("psW0", 48, 64, "v"))
+LISTS = ("psB0", "psC")
+WAIT, GATHER, REMOTE, FIRST, LOAD, TABLE = 230.0, 1.3, 2000.0, 2500.0, 1400.0, 5000.0
 ORDER = []
 
 
@@ -376,8 +378,8 @@ def rank_program(g, core, T, topo):
     ts(A("WS"), A("WF"), 1.0 / 128, MUL)
     ts(A("MW"), A("QC"), 4.0 / 256, MUL, 2.0 / 256, ADD)
     for d in STAIRS:
-        for h in range(2):
-            fill(R(d + "B", h), -2.0)
+        for q in range(4):
+            fill(A(d + "B", 16 * q * STAIRS[d], 16 * (q + 1) * STAIRS[d]), -2.0)
         for buf, slot, x in (("A", 0, -64.0), ("A", 1, 0.0), ("B", 2, -64.0), ("B", 3, -1.875)):
             fill(R(d + buf, None, slot), x)
     fill(R("KA", None, 2), -1.125)
@@ -399,7 +401,8 @@ def rank_program(g, core, T, topo):
                     ("N256", -256.0), ("I255", 255.0), ("I256", 256.0), ("N512", -512.0), ("N101", -101.0)):
         act(A(name), A("ID"), IDT, 0.0, x)
     for s in (3, 4):
-        fill(A("M%d" % s), 1.0)
+        for h in range(2):
+            fill(R("M%d" % s, h), 1.0)
         fill(A("M%d" % s, 0, 128 * s, s), 0.0)
     fill(A("Z7", 0, 2050, 2049), 0.0)
     for q in range(4):
@@ -439,10 +442,10 @@ def rank_program(g, core, T, topo):
     ts(A("T255"), A("TRI"), 255.0 / 256, MUL)
     for l in range(1, 5):
         pick(A("SH%d" % l), A("BO"), [[-1, 128]], EQ, 0.0, -l, 1)
-    iota(A("K5"), [[0, 64], [-256, 5]])
-    resets("M5", 320, 5, 0, 1)
+    iota(A("K5"), [[0, 32], [-256, 5]])
+    resets("M5", 160, 5, 0, 1)
     resets("M8", 256, 8, 1024, 0)
-    resets("LM", 640, 10, 1024, 0)
+    resets("LM", 320, 10, 1024, 0)
     for t in range(1, RO):
         send(A("ST0"), A("ST%d" % t), "st%d" % t, t, FIRST if t == 1 else 300, FIRST)
     msum(A("psC", 0, 64), [("ID", A("STH")), ("ID", A("STL")), ("N512", R("LND0", None, 0)),
@@ -469,7 +472,8 @@ def rank_program(g, core, T, topo):
         return ("K", 8, 11) if k == 1 else ("T" if k < 5 else "U", 16, 20 - k)
 
     def steps_at(i):
-        return A("psD1" if i < 7 else "psY", 64 * (i % 7), 64 * (i % 7) + 64)
+        ps, a = ("psD%d" % (i // 4), 256 + 64 * (i % 4)) if i < 8 else ("psY", 64 * (i - 8))
+        return A(ps, a, a + 64)
 
     def uwrap(k, ps, a, b):
         msum(A(ps, 1, (b - a) // 8, 2), [(A("Wm", m * 128, m * 128 + 128), Z(k, a + m, b, 16)) for m in range(16)],
@@ -500,30 +504,32 @@ def rank_program(g, core, T, topo):
         msum(height, [("I1", was), ("I1", less)])
         msum(log, [("N32", was), ("I4", less)])
 
-    def head(t):
-        LB, C = R("LND%d" % t, None, 0), R("LND%d" % t, None, 1)
+    def head(t, h):
+        LB, C, ps = R("LND%d" % t, h, 0), R("LND%d" % t, h, 1), "psW%d" % h
         if t:
-            msum(A("psC", 0, 64), [("ID", A("STH")), ("ID", A("STL"))], True, False)
-            msum(A("psC", 0, 64), [("N512", LB), ("N101", LB)], False)
-        mm(A("psB1", 128, 192), A("GT0"), LB)
-        fixed[0] = True
+            msum(A(ps, 128, 160), [("ID", R("STH", h)), ("ID", R("STL", h))], True, False)
+            msum(A(ps, 128, 160), [("N512", LB), ("N101", LB)], False)
+        mm(A("psB%d" % h, 192, 224), A("GT0"), LB)
+        fixed[0] = h == 0
         if t:
-            ts(A("OFFZ"), A("psC", 0, 64), A("ACOL"), ADD)
-        ts(A("EQ0"), A("psB1", 128, 192), A("Q4"), EQ)
-        ts(R("KB", None, 1), LB, 0.25, MUL)
-        tt(A("SEL"), A("EQ0"), C, MUL)
-        for h in range(2):
-            gather(0, h, W + AGAIN if t else W)
+            ts(R("OFFZ", h), A(ps, 128, 160), A("ACOL"), ADD)
+        ts(R("EQ0", h), A("psB%d" % h, 192, 224), A("Q4"), EQ)
+        ts(R("KB", h, 1), LB, 0.25, MUL)
+        tt(R("SEL", h), R("EQ0", h), C, MUL)
+        gather(0, h, W + AGAIN if t else W)
         fixed[0] = False
         for j in range(7):
-            mm(A("psD0", 64 * j, 64 * j + 64), A("TL%d" % (9 + j if j else 0)), C)
-        msum(A("psB0", 128, 192), [("GTN", C), ("BM0", A("SEL"))])
-        entries(0, None, A("psB0", 128, 192), 0)
-        for h in range(2):
-            mm(A("psW%d" % h, 0, 64), A("NEG"), A("ALT", 0, 64), True, False)
-            uwrap(0, "psW%d" % h, 512 * h, 512 * h + 512)
+            mm(A("psD%d" % h, 32 * j, 32 * j + 32), A("TL%d" % (9 + j if j else 0)), C)
+        together(-7)
+        msum(A("psB%d" % h, 128, 160), [("GTN", C), ("BM0", R("SEL", h))])
+        entries(0, h, A("psB%d" % h, 128, 160), 0)
+        mm(A(ps, 0, 64), A("NEG"), A("ALT", 0, 64), True, False)
+        uwrap(0, ps, 512 * h, 512 * h + 512)
         for j in range(7):
-            ts(R("KA", None, 4 + j), A("psD0", 64 * j, 64 * j + 64), -0.25, ADD)
+            ts(R("KA", h, 4 + j), A("psD%d" % h, 32 * j, 32 * j + 32), -0.25, ADD)
+
+    def tables(t):
+        LB, C = R("LND%d" % t, None, 0), R("LND%d" % t, None, 1)
         for i in range(14):
             mm(steps_at(i), A("TL%d" % (i + 1)), C)
         for i in range(14):
@@ -596,9 +602,10 @@ def rank_program(g, core, T, topo):
         tt(A("DH"), A("psW1", 1, 128, 2), R("AD", None, 1), ADD)
         ts(A("N4"), A("DH"), 1, SHR, 3, AND)
         mm(A("psW1", 128, 192), A("ID"), A("DG"), True, False)
-        mm(A("psB0", 0, 320), A("ID"), A("K5"), True, False)
-        for l in range(5):
-            mm(A("psB0", l, 320, 5), A("SH%d" % l if l else "ID"), C, False, False)
+        for h, ps in enumerate(LISTS):
+            mm(A(ps, 0, 160), A("ID"), A("K5"), True, False)
+            for l in range(5):
+                mm(A(ps, l, 160, 5), A("SH%d" % l if l else "ID"), R("LND%d" % t, h, 1), False, False)
         mm(A("psW0", 0, 256), A("ID"), A("CM"), True, False)
         scan(A("WO"), A("WD"), A("psB1", 128, 256), MIN, MAX)
         tt(R("LG", None, 1), A("PRE"), A("N4"), ADD)
@@ -606,43 +613,49 @@ def rank_program(g, core, T, topo):
         ts(OH, A("psD0", 0, 64), 0.0, LT, 256.0, MUL)
         mm(A("psW1", 128, 192), A("MV"), OH, False, True)
         mm(A("psW1", 192, 256), A("BO3"), OH)
-        mm(A("psC", 128, 192), A("BO1" if last else "ONS"), OH)
+        mm(A("psB1", 0, 64), A("BO1" if last else "ONS"), OH)
         mm(A("psW0", 3, 256, 4), A("BON"), A("KX") if last else OH, False, False)
-        scan(A("OHL"), A("LM"), A("LG"), ADD, MIN)
         fixed[0] = True
-        for s in range(8):
-            mm(A("psD1", s, 512, 8), A("BO"), R("OHL", None, 1 + s))
-        together(-8)
-        for l in range(5):
-            mm(A("psB0", l, 320, 5), A("TRI"), R("OHL", None, 9), False, l == 4)
-        mm(A("psB0", 320, 384), A("T255"), R("OHL", None, 9))
-        together(-6)
+        for h in range(2):
+            scan(R("OHL", h), A("LM"), R("LG", h), ADD, MIN)
+        for h in range(2):
+            for s in range(8):
+                mm(A("psD%d" % h, 128 + s, 384, 8), A("BO"), R("OHL", h, 1 + s))
+            together(-8)
+            for l in range(5):
+                mm(A(LISTS[h], l, 160, 5), A("TRI"), R("OHL", h, 9), False, l == 4)
+            mm(A(LISTS[h], 160, 192), A("T255"), R("OHL", h, 9))
+            together(-6)
         fixed[0] = False
         scan(A("SD"), A("M4F"), A("psW1", 128, 192), MUL, MAX)
-        tt(A("psC", 192, 256), A("psW1", 192, 256), LB, MAX)
-        if last:
-            actcp(A("NOK"), A("psC", 128, 192))
-        else:
-            act(A("PR"), A("psC", 128, 192), IDT, 4 * 613 / 64, 1.0, A("ACOL"))
-        for h in range(2):
-            act(R("AS", h), R("psD1", h), ABS, A("QB"))
-            scan(R("AO", h), A("M8"), R("AS", h), ADD, MIN)
+        tt(A("EE"), A("psW1", 192, 256), LB, MAX)
         ts(A("OV"), A("SD", 3, 64, 4), A("SCL"), MUL, A("BIA"), ADD)
-        cp(A("V4"), IND(Ap((T["ZV"][:], A("O1")[1] + A("G2")[1] + A("Z7")[1])), A("OV")))
-        ts(A("AL"), A("psB0", 0, 320), 0.0, MAX, 255.0, MIN)
-        scan(A("ALO"), A("M5"), A("AL"), MUL, ADD)
+        if last:
+            actcp(A("NOK"), A("psB1", 0, 64))
+        else:
+            act(A("PR"), A("psB1", 0, 64), IDT, 4 * 613 / 64, 1.0, A("ACOL"))
+        for h in range(2):
+            fixed[0] = True
+            act(R("AS", h), A("psD%d" % h, 128, 384), ABS, A("QB"))
+            if h == 0:
+                (cp if last else actcp)(A("V4"), IND(Ap((T["ZV"][:], A("O1")[1] + A("G2")[1] + A("Z7")[1])), A("OV")))
+            fixed[0] = False
+            ts(R("AL", h), A(LISTS[h], 0, 160), 0.0, MAX, 255.0, MIN)
+            scan(R("AO", h), A("M8"), R("AS", h), ADD, MIN)
+            scan(R("ALO", h), A("M5"), R("AL", h), MUL, ADD)
+            tt(R("YB", h) if last else R("SND%d" % t, h, 0), R("AO", h, 7), R("EE", h), MIN)
+            tt(R("YC", h) if last else R("SND%d" % t, h, 1), R("ALO", h, 4), A(LISTS[h], 160, 192), SUB)
+            if not last:
+                send(R("SND%d" % t, h), R("LND%d" % (t + 1), h), "arr%d%d" % (t + 1, h), 1)
         scan(A("VO"), A("M4", 0, 256), A("V4"), MUL, MAX)
         mm(A("psW0", 0, 256, 4), A("W128"), VV, False, False)
         mm(A("psW0", 3, 256, 4), A("WB1"), VV, False, True)
-        tt(A("YB") if last else R("SND%d" % t, None, 0), R("AO", None, 7), A("psC", 192, 256), MIN)
-        tt(A("YC") if last else R("SND%d" % t, None, 1), R("ALO", None, 4), A("psB0", 320, 384), SUB)
         if last:
             act(A("YL"), A("YB"), IDT, 4.0, -1.0)
-            tt(A("DIF"), VV, A("psC", 128, 192), MUL)
+            tt(A("DIF"), VV, A("psB1", 0, 64), MUL)
         else:
-            send(A("SND%d" % t), A("LND%d" % (t + 1)), "arr%d" % (t + 1), 1)
-            for h in range(2):
-                actcp(R("VP", h), VV)
+            actcp(A("VP", 0, 64), VV)
+            actcp(A("VP", 64, 96), R("VO", 0, 3))
         scan(A("X1"), A("MM"), A("psW0", 0, 256), MUL, ADD)
         tt(A("FVI"), F, VV, ADD)
         scan(A("SD2"), A("M16F"), R("X1", None, 3), MUL, MAX)
@@ -654,14 +667,16 @@ def rank_program(g, core, T, topo):
             tt(A("SEL"), IND(A("X", 0, W), A("OX", 0, 4)), A("NOK"), MUL)
             tt(A("YS"), A("psW1", 0, 64), A("SEL"), SUB)
         else:
-            ts(A("OX", 4, 8), A("SD2", 15, 64, 16), float(W), ADD)
-            cp(IND(A("X"), A("OX")), A("VP"))
+            ts(A("OX", 4, 6), A("SD2", 15, 32, 16), float(W), ADD)
+            cp(IND(A("X"), A("OX", 0, 6)), A("VP", 0, 96))
 
     for t in range(RO):
         act(A("NF"), A("F%d" % t), IDT, -1.0)
         for m in range(16):
             gcp(A("G1", 4 * m + 3, 4096, 64), A("NF"))
-        head(t)
+        for h in range(2):
+            head(t, h)
+        tables(t)
         if t == 0:
             for a in range(0, AGAIN, 256):
                 actcp(A("X", W + a, W + a + 256), A("X", a, a + 256))
@@ -688,7 +703,8 @@ def rank_program(g, core, T, topo):
     wait("g", "loc", sent[0])
     for t in range(1, RO):
         wait("g", "st%d" % t, len(topo.engines(T.cores[(rank - t) % n], core)))
-        wait("g", "arr%d" % t, len(topo.engines(T.cores[(rank - 1) % n], core)))
+        for h in range(2):
+            wait("g", "arr%d%d" % (t, h), len(topo.engines(T.cores[(rank - 1) % n], core)))
     for s in ("dX", "dW", "dC", "dL", "dS", "dF"):
         wait("g", s, 16)
     for q in "gtsv":

import math
from concourse.mybir import dt, AluOpType, AxisListType, ActivationFunctionType

ADD, SUB, MUL, MAX, MIN = AluOpType.add, AluOpType.subtract, AluOpType.mult, AluOpType.max, AluOpType.min
GE, EQ, LT, GT, NE = AluOpType.is_ge, AluOpType.is_equal, AluOpType.is_lt, AluOpType.is_gt, AluOpType.not_equal
SHR, AND = AluOpType.arith_shift_right, AluOpType.bitwise_and
IDT, SIGN, ABS = ActivationFunctionType.Identity, ActivationFunctionType.Sign, ActivationFunctionType.Abs
COPY, SQUARE = ActivationFunctionType.Copy, ActivationFunctionType.Square
RO, S, W = 4, 8, 8192
AGAIN = 3072
ROUND = 1.5 * 2 ** 23
DUMP = 2 * W
STAIRS = {"K": 11, "T": 18, "U": 15}

SCRATCH = {}
POOL = {}


def _d(names, cols, dtype, where="sbuf"):
    for n in names.split():
        SCRATCH[n] = (where, [128, cols], dtype)


def _pool(buf, names, cols, dtype):
    for k, n in enumerate(names.split()):
        POOL[n] = (buf, k * cols, cols)
    SCRATCH[buf] = ("sbuf", [128, len(names.split()) * cols], dtype)


_d("X", DUMP + 2 * W, "bfloat16")
_d("G0 O0 O2", 3072, "bfloat16")
_d("G1", 4096, "bfloat16")
_d("ZV", 9218, "bfloat16")
POOL.update(O1=("ZV", 0, 4096), G2=("ZV", 4096, 3072), Z7=("ZV", 7168, 2050))
_d("GEb", 1024, "bfloat16")
_d("M3", 384, "bfloat16")
_d("M4", 512, "bfloat16")
_d("V4 VO CM M8", 256, "bfloat16")
_d("X1 MM", 256, "float32")
_d("Gm Wm", 2048, "bfloat16")
_pool("TL", " ".join("TL%d" % k for k in range(16)), 128, "bfloat16")
_pool("MATS", "ID BO BO3 BO1 BON B256 WB1 SH1 SH2 SH3 SH4 GT0 GTN BM0 GT8 NEG ONS I256 I255 ALF TRI T255 MV "
              "N256 W128 N512 N101 tm7 tm8 WD WO VP TH2 ALT", 128, "bfloat16")
_pool("HMATS", "I1 I4 N32 P512 P1K N1K", 128, "float16")
_pool("SMALL", "ONE SP0 CH0 NF EE PRE DIF DG KX YL YB YC EQ0 SEL STH STL NOK GAP GAP0", 64, "bfloat16")
for _n, _s in STAIRS.items():
    _d("%sA %sB %sO" % (_n, _n, _n), 64 * _s, "float16")
_d("LG OHL", 640, "bfloat16")
_d("AS AO", 512, "bfloat16")
_d("K5 M5", 160, "bfloat16")
_d("LM AL", 320, "bfloat16")
_d("ALO", 320, "float16")
_d("F0 F1 F2 F3 F4", 64, "bfloat16")
_d("LND0 LND1 LND2 LND3 SND0 SND1 SND2", 128, "bfloat16")
_d("WT", 1, "bfloat16")
_d("ST0 ST1 ST2 ST3", 64, "int32")
_pool("INTS", "N4 DH SI S0 FVI FH SIH SIL", 64, "int32")
_d("YI", 128, "int32")
_d("PI QI GI RI TI", 1, "int32")
_d("ROWF CQF CGF AD", 128, "float32")
_pool("COLS", "QC GC PC QB MW Q4 CN C78 ACOL M0 M1 M2 RC TC GE1 GE2 GE3 SCA BIB SCL BIA WF WS", 1, "float32")
_d("EQ16", 32, "float32")
_d("CU CV SGN", 16, "float32")
_pool("FLTS", "PR M16F M4F DIAG DIA4 SD X0 X2 SD2 W1 W2", 64, "float32")
_d("YS CQ4", 64, "float32")
_d("OFFZ", 64, "uint16")
_d("OV", 16, "uint16")
_d("OX", 8, "uint16")
_d("psW0 psW1 psD0 psD1 psB0 psB1 psC psY", 512, "float32", "psum")

SEMAPHORES = ["qv", "qs", "qt", "qg", "dX", "dW", "dC", "dL", "dS", "dF", "oC", "oL", "oF", "oS", "loc"]
SEMAPHORES += ["st%d" % t for t in range(1, RO)] + ["arr%d%d" % (t, h) for t in range(1, RO) for h in range(2)]

Z_SCALAR = [(18, 24), (28, 28), (32, 32), (32, 32), (32, 32), (32, 32), (32, 32), (32, 16)]
PIECE = 64
PARTS = (("psD0", 0, 32, "s"), ("psD1", 32, 48, "s"), ("psW0", 48, 64, "v"))
LISTS = ("psB0", "psC")
WAIT, GATHER, REMOTE, FIRST, LOAD, TABLE = 230.0, 1.3, 2000.0, 2500.0, 1400.0, 5000.0
ORDER = []


class Ap(tuple):
    pass


def meet(a, lo, hi, step):
    return a[0] < hi and a[1] > lo and (a[0] - lo) % math.gcd(a[2], step) == 0


def plan(calls):
    before, seen, bank, behind, line = [], {}, {}, {}, {}
    for i, (q, outs, ins, cost, late, call, fixed) in enumerate(calls):
        need = set()
        if fixed:
            behind[i], line[q] = line.get(q), i
        for w, group in ((True, outs), (False, ins)):
            for x in group:
                for name, lo, hi, step in x[1]:
                    if name.startswith("ps"):
                        was, now = bank.setdefault(name, ([], []))
                        if now and calls[now[-1]][0] != q:
                            was, now = bank[name] = now, []
                        need.update(was + (now[-1:] if q == "t" else []))
                        now.append(i)
                    need.update(a[4] for a in seen.get(name, ()) if (w or a[3]) and meet(a, lo, hi, step))
        for w, group in ((False, ins), (True, outs)):
            for x in group:
                for name, lo, hi, step in x[1]:
                    lst = seen.setdefault(name, [])
                    if w:
                        lst[:] = [a for a in lst if not (lo <= a[0] and a[1] <= hi and a[2] % step == 0
                                                         and (a[0] - lo) % step == 0)]
                    lst.append((lo, hi, step, w, i))
        need.discard(i)
        if behind.get(i) is None or behind[i] in need:
            behind[i] = None
        else:
            need.add(behind[i])
        before.append(need)

    def lag(j, i):
        return calls[j][3] + (0 if behind[i] == j or calls[j][0] == calls[i][0] == "t" else calls[j][4] + WAIT)
    way = [c[3] + c[4] + (1e6 if c[4] == FIRST else 0) for c in calls]
    for i in range(len(calls) - 1, -1, -1):
        for j in before[i]:
            way[j] = max(way[j], lag(j, i) + way[i])
    busy, start = {}, {}
    for i in sorted(range(len(calls)), key=lambda i: (-way[i], i)):
        t = max([0] + [start[j] + lag(j, i) for j in before[i]])
        lst = busy.setdefault(calls[i][0], [])
        k = len(lst)
        while k and lst[k - 1][1] > t:
            k -= 1
        while k < len(lst) and lst[k][0] < t + calls[i][3]:
            t = max(t, lst[k][1])
            k += 1
        lst.insert(k, (t, t + calls[i][3]))
        start[i] = t
    return sorted(start, key=lambda i: (start[i], -way[i], i))


def rank_program(g, core, T, topo):
    rank = T.rank_of(core)
    if rank is None:
        return
    n = len(T.cores)
    queue = {"v": g.vector, "s": g.scalar, "t": g.tensor, "g": g, "y": g.sync}
    count = {"v": 0, "s": 0, "t": 0, "g": 0}
    known = {q: {} for q in queue}
    snap = {}
    seen = {}
    calls = []
    fixed = [False]

    def A(name, a=None, b=None, step=1):
        buf, off, cols = POOL[name] if name in POOL else (name, 0, SCRATCH[name][1][1])
        a = 0 if a is None else a
        b = cols if b is None else b
        ap = T[buf][:, off + a:off + b] if step == 1 else T[buf][:, off + a:off + b:step]
        return Ap((ap, ((name, a, b, step),)))

    def R(name, h, slot=None):
        cols = POOL[name][2] if name in POOL else SCRATCH[name][1][1]
        a, b = (0, cols) if h is None else (h * cols // 2, (h + 1) * cols // 2)
        return A(name, a, b) if slot is None else A(name, a + slot, b, cols // 64)

    def IND(win, off):
        return Ap((win[0].indirect(off[0]), win[1] + off[1]))

    def wait(q, sem, val):
        if known[q].get(sem, 0) >= val:
            return
        queue[q].wait_ge(T.sem[sem], val)
        known[q][sem] = val
        for s, c in snap.get((sem, val), {}).items():
            if known[q].get(s, 0) < c:
                known[q][s] = c

    def deps(q, outs, ins):
        need = {}
        for w, group in ((True, outs), (False, ins)):
            for x in group:
                for name, lo, hi, step in x[1]:
                    ps = name.startswith("ps")
                    for a in seen.get(name, ()):
                        apart = not meet(a, lo, hi, step)
                        if apart and not ps:
                            continue
                        if a[4] == q:
                            if q == "t" or apart or not (w or a[3]):
                                continue
                        elif not ps and not (w or a[3]):
                            continue
                        need[a[5]] = max(need.get(a[5], 0), a[6])
        for s in sorted(need):
            wait(q, s, need[s])

    def record(q, outs, ins, sem, val):
        k = known.get(q, {})
        for w, group in ((False, ins), (True, outs)):
            for x in group:
                for name, lo, hi, step in x[1]:
                    lst = seen.setdefault(name, [])
                    if w:
                        lst[:] = [a for a in lst if not (
                            lo <= a[0] and a[1] <= hi and a[2] % step == 0 and (a[0] - lo) % step == 0
                            and k.get(a[5], 0) >= a[6])]
                    lst[:] = [a for a in lst if not (a[4] == q and a[3] == w and a[:3] == [lo, hi, step])]
                    lst.append([lo, hi, step, w, q, sem, val])

    def run(q, outs, ins, cost, call):
        def issue():
            deps(q, outs, ins)
            sem = "q" + q
            count[q] += 1
            snap[(sem, count[q])] = dict(known[q])
            call().then_inc(T.sem[sem], 1)
            record(q, outs, ins, sem, count[q])
        calls.append((q, outs, ins, cost, 0, issue, fixed[0]))

    def dma(q, sem, out, in_, outs, ins, late=LOAD):
        def issue():
            deps(q, outs, ins)
            snap[(sem, 16)] = dict(known[q])
            queue[q].dma_start(out, in_).then_inc(T.sem[sem], 16)
            record("dma" + sem, outs, ins, sem, 16)
        calls.append((q, outs, ins, 60, late, issue, False))

    def isap(s):
        return isinstance(s, Ap)

    def size(x):
        name, a, b, step = x[1][0]
        return (b - a + step - 1) // step

    def cycles(out, *ins):
        if len(out[1]) > 1:
            return 50 + 2.4 * GATHER * size(ins[0])
        if len(ins[0][1]) > 1:
            return 60 + GATHER * size(out)
        wide = any(SCRATCH[POOL.get(x[1][0][0], x[1][0])[0]][2].endswith("32") for x in (out,) + ins)
        return 0.83 * max(64, size(out) * (1 if wide else 0.5))

    def tt(out, a, b, op):
        both = not any(x[1][0][0].startswith("ps") for x in (a, b))
        cost = cycles(out, a) if len(a[1]) > 1 else 0.83 * max(64, size(out) * (2 if both else 1))
        run("v", [out], [a, b], cost, lambda: g.vector.tensor_tensor(out[0], a[0], b[0], op))

    def ts(out, a, s1, op0, s2=None, op1=None):
        ins = [a] + [s for s in (s1, s2) if isap(s)]
        x1 = s1[0] if isap(s1) else s1
        x2 = s2[0] if isap(s2) else s2
        if op1 is None:
            run("v", [out], ins, cycles(out, a), lambda: g.vector.tensor_scalar(out[0], a[0], x1, None, op0))
        else:
            run("v", [out], ins, cycles(out, a), lambda: g.vector.tensor_scalar(out[0], a[0], x1, x2, op0, op1))

    def cp(out, a):
        run("v", [out], [a], cycles(out, a), lambda: g.vector.tensor_copy(out[0], a[0]))

    def fill(out, x):
        run("v", [out], [], cycles(out, out), lambda: g.vector.memset(out[0], x))

    def scan(out, d0, d1, op0, op1):
        run("v", [out], [d0, d1], cycles(out, d0, d1),
            lambda: g.vector.tensor_tensor_scan(out[0], d0[0], d1[0], 0.0, op0, op1))

    def act(out, a, func, bias=0.0, scale=1.0, acc=None):
        b = bias[0] if isap(bias) else bias
        x = scale[0] if isap(scale) else scale
        ins = [a] + [c for c in (bias, scale) if isap(c)]
        if acc is None:
            run("s", [out], ins, 0.83 * max(64, size(out)),
                lambda: g.scalar.activation(out[0], a[0], func, bias=b, scale=x))
        else:
            run("s", [out, acc], ins, 75,
                lambda: g.scalar.activation(out[0], a[0], func, bias=b, scale=x, accum_out=acc[0]))

    def actcp(out, a):
        run("s", [out], [a], cycles(out, a) if len(a[1]) > 1 else 0.83 * max(64, size(out)),
            lambda: g.scalar.activation(out[0], a[0], COPY))

    def mm(out, l, r, start=True, stop=True):
        run("t", [out], [l, r], 0.42 * max(64, size(out)), lambda: g.tensor.matmul(out[0], l[0], r[0], start, stop))

    def together(first):
        part = calls[first:]
        calls[first:] = [(part[0][0], sum((c[1] for c in part), []), sum((c[2] for c in part), []),
                          sum(c[3] for c in part), 0, lambda: [c[5]() for c in part], fixed[0])]

    def msum(out, terms, start=True, stop=True):
        first = len(calls)
        for j, (l, r) in enumerate(terms):
            mm(out, l if isap(l) else A(l), r, start and j == 0, stop and j == len(terms) - 1)
        together(first)

    def iota(out, pattern, cm=0, base=0):
        if SCRATCH[out[1][0][0]][2] == "int32":
            run("g", [out], [], 130 + 1.66 * size(out), lambda: g.iota(out[0], pattern, base, cm))
        else:
            run("g", [out], [], 130 + 1.66 * size(out),
                lambda: g.iota(out[0], pattern, base, cm, allow_small_or_imprecise_dtypes=True))

    def pick(out, a, pattern, op, other, base, cm):
        run("g", [out], [a], 170 + 1.66 * size(out),
            lambda: g.affine_select(out[0], a[0], pattern, op, other, base, cm))

    def gcp(out, a):
        pick(out, a, [[0, size(out)]], GE, 0.0, 0, 0)

    def resets(name, cols, step, first, other):
        iota(A(name), [[0, cols]], 0, other)
        iota(A(name, 0, cols, step), [[0, cols // step]], 0, first)

    sent = [0]

    def send(src, dst, sem, hop, cost=300, late=REMOTE):
        to = T.cores[(rank + hop) % n]
        rid, pid, _ = topo.addr(to)

        def issue():
            deps("g", [], [src])
            g.remote_dma(out_ap=dst[0], in_ap=src[0], remote_sem=T.sem[sem], local_sem=T.sem.loc,
                         pid=pid, routing_id=rid, dma_engine_mask=topo.mask(core, to))
            sent[0] += len(topo.engines(core, to))
            record("net" + sem, [dst], [], sem, len(topo.engines(T.cores[(rank - hop) % n], core)))
        calls.append(("g", [dst], [src], cost, late, issue, False))

    dma("y", "dS", T["ST0"][:], T.st[:], [A("ST0")], [])
    dma("s", "dL", A("SP0")[0], T.sp[:], [A("SP0")], [])
    dma("y", "dX", T["X"][:, 0:W], T.x[:], [A("X", 0, W)], [], TABLE)
    dma("s", "dW", T["WT"][:], T.wt[:], [A("WT")], [])
    dma("s", "dC", A("CH0")[0], T.ch[:], [A("CH0")], [])
    dma("s", "dF", T["F0"][:], T.fl[:], [A("F0")], [])
    for call in calls:
        call[5]()
    loads = len(calls)

    iota(A("PI"), [[1, 1]], 1)
    iota(A("CGF"), [[1, 8], [0, 16]])
    iota(A("ROWF"), [[1, 128]])
    iota(A("CQF"), [[0, 8], [1, 16]])
    iota(A("CQ4"), [[0, 16], [1, 4]])

    def starts(t):
        ts(A("SIH"), A("ST%d" % t), W - 128, AND)
        ts(A("SIL"), A("ST%d" % t), 127, AND)
        cp(A("STH"), A("SIH"))
        cp(A("STL"), A("SIL"))

    fill(A("Gm"), 0.0)
    ts(A("GI"), A("PI"), 4, SHR)
    ts(A("QI"), A("PI"), 15, AND)
    cp(A("PC"), A("PI"))
    cp(A("GC"), A("GI"))
    cp(A("QC"), A("QI"))
    ts(A("BO"), A("CGF"), A("GC"), EQ)
    ts(A("ID"), A("ROWF"), A("PC"), EQ)
    ts(A("B256"), A("BO"), 256.0, MUL)
    ts(A("EQ16"), A("ROWF", 0, 32), A("QC"), EQ)
    for name, x in (("ONE", 1.0), ("ALT", 1.0), ("ACOL", 4.0 * 613), ("BM0", 0.0), ("SGN", 1.0 / 1024)):
        fill(A(name), x)
    fill(A("ALT", 0, 128, 2), 0.0)
    fill(A("SGN", 1, 16, 2), -1.0 / 1024)
    ts(A("CN"), A("PC"), 0.0, EQ, 2.5, MUL)
    ts(A("NEG"), A("ROWF"), 0.0, MUL, A("CN"), ADD)
    ts(A("NEG"), A("NEG"), 64.0, ADD)
    ts(R("LND0", None, 0), A("SP0"), -1.0, MUL, 4.0, ADD)
    starts(0)
    cp(R("LND0", None, 1), A("CH0"))
    cp(A("WF"), A("WT"))
    tt(A("CU"), A("EQ16", 0, 16), A("EQ16", 2, 18), SUB)
    tt(A("C78"), A("EQ16", 8, 9), A("EQ16", 7, 8), SUB)
    tt(A("CV"), A("CU"), A("SGN"), MUL)
    ts(A("CV", 0, 1), A("C78"), 1.0 / 1024, MUL)
    for j, x in enumerate((4.0, 0.5, 8.5)):
        ts(A("M%d" % j), A("QC"), -1.0, MUL, x, ADD)
    ts(A("WS"), A("WF"), 1.0 / 128, MUL)
    ts(A("MW"), A("QC"), 4.0 / 256, MUL, 2.0 / 256, ADD)
    for d in STAIRS:
        for q in range(4):
            fill(A(d + "B", 16 * q * STAIRS[d], 16 * (q + 1) * STAIRS[d]), -2.0)
        for buf, slot, x in (("A", 0, -64.0), ("A", 1, 0.0), ("B", 2, -64.0), ("B", 3, -1.875)):
            fill(R(d + buf, None, slot), x)
    fill(R("KA", None, 2), -1.125)
    ts(A("GAP0"), A("ONE"), A("M0"), MUL)
    ts(A("GTN"), A("BO"), A("EQ16", 0, 1), MUL)
    fill(A("GTN", 0, 128, 16), 0.0)
    cp(A("BM0", 0, 128, 16), A("BO", 0, 128, 16))
    ts(A("Q4"), A("QC"), -1.0, MUL, 4.0, ADD)
    for m in range(16):
        act(A("Gm", m * 129, m * 128 + 128, 16), A("BO", 0, 128, 16), IDT, 0.0, 65536.0)
    for h in range(2):
        ts(R("Wm", h), R("Gm", h), A("WT"), MUL, -0.25 / 65536, MUL)
    for i in range(16):
        act(A("TL%d" % i), A("BO"), IDT, 0.0, A("CV", (16 - i) % 16, (16 - i) % 16 + 1))
    for name, x in (("GT0", A("EQ16", 0, 1)), ("GT8", A("EQ16", 8, 9)), ("MV", A("MW")), ("WB1", A("WF")),
                    ("W128", A("WS")), ("BO3", 3.0 / 256), ("BO1", 1.0 / 256), ("BON", -DUMP / 256)):
        act(A(name), A("BO"), IDT, 0.0, x)
    for name, x in (("P512", 512.0), ("P1K", 1024.0), ("N1K", -1024.0), ("I1", 1.0), ("I4", 4.0), ("N32", -32.0),
                    ("N256", -256.0), ("I255", 255.0), ("I256", 256.0), ("N512", -512.0), ("N101", -101.0)):
        act(A(name), A("ID"), IDT, 0.0, x)
    for s in (3, 4):
        for h in range(2):
            fill(R("M%d" % s, h), 1.0)
        fill(A("M%d" % s, 0, 128 * s, s), 0.0)
    fill(A("Z7", 0, 2050, 2049), 0.0)
    for q in range(4):
        fill(A("Z7", 512 * q + 1, 512 * q + 513, 2), 0.0)
    ts(A("QB"), A("QC"), -8.0, MUL, -16.0, ADD)
    ts(A("DIAG"), A("CQF", 0, 64), A("QC"), EQ)
    ts(A("RI"), A("QI"), 2, SHR)
    ts(A("TI"), A("QI"), 3, AND)
    cp(A("RC"), A("RI"))
    cp(A("TC"), A("TI"))
    ts(A("DIA4"), A("CQ4"), A("RC"), EQ)
    for j in (1, 2, 3):
        ts(A("GE%d" % j), A("TC"), float(j), GE)
    ts(A("SCA"), A("GE1"), -0.25, MUL, 1.0, ADD)
    ts(A("BIB"), A("GE1"), 4095.5, MUL, A("GE2"), ADD)
    ts(A("SCL"), A("GE3"), -0.25, MUL, A("SCA"), ADD)
    ts(A("BIA"), A("GE3"), 3072.5, MUL, A("BIB"), ADD)
    for out, x, y, tmp, diag in ((A("DG"), 64.0, 0.0, "X0", "DIA4"), (R("CM", None, 3), 128.0, DUMP, "X2", "DIAG")):
        ts(A(tmp), A("ROWF", 0, 64), x, MUL, y + 32768.0, ADD)
        tt(A(tmp), A(tmp), A(diag), MUL)
        ts(out, A(tmp), -32768.0, ADD)
    for j, (x, y) in enumerate(((-127.0 / 256, 0.0), (ROUND, 1.0), (-ROUND, 1.0), (None, -128.0))):
        if x:
            fill(R("CM", None, j), x)
        fill(R("MM", None, j), y)
    for name, x in (("ONS", 1.0 / 256), ("KX", 16.0), ("M16F", 1.0), ("M4F", 1.0), ("TH2", 0.0)):
        fill(A(name), x)
    fill(A("M4F", 0, 64, 4), 0.0)
    fill(A("WD", 0, 128, 2), -4194304.0)
    fill(A("M16F", 0, 64, 16), 0.0)
    for ps, a, b, on in PARTS:
        fill(A("TH2", 2 * a, 2 * b, 2), -768.0 if on == "s" else -384.0)
    pick(A("TRI"), A("B256"), [[1, 128]], GE, 0.0, 0, -1)
    pick(A("tm7"), A("BO"), [[1, 128]], GT, 1.0 / 16, 0, -1)
    pick(A("tm8"), A("tm7"), [[1, 128]], NE, -31.0 / 32, 0, -1)
    tt(A("ALF"), A("tm8"), A("BO"), MUL)
    ts(A("T255"), A("TRI"), 255.0 / 256, MUL)
    for l in range(1, 5):
        pick(A("SH%d" % l), A("BO"), [[-1, 128]], EQ, 0.0, -l, 1)
    iota(A("K5"), [[0, 32], [-256, 5]])
    resets("M5", 160, 5, 0, 1)
    resets("M8", 256, 8, 1024, 0)
    resets("LM", 320, 10, 1024, 0)
    for t in range(1, RO):
        send(A("ST0"), A("ST%d" % t), "st%d" % t, t, FIRST if t == 1 else 300, FIRST)
    msum(A("psC", 0, 64), [("ID", A("STH")), ("ID", A("STL")), ("N512", R("LND0", None, 0)),
                           ("N101", R("LND0", None, 0))])
    ts(A("S0"), A("psC", 0, 64), A("ACOL"), ADD)
    ts(A("SI"), A("S0"), W - 1, AND)
    cp(A("OFFZ"), A("SI"))

    ZAT = [("G0", 3, 0), ("G0", 3, 1), ("G0", 3, 2), ("G1", 4, 1), ("G1", 4, 2), ("G2", 3, 1), ("G2", 3, 2),
           ("Z7", 2, 2)]

    def Z(k, a, b, step=1):
        buf, s, o = ZAT[k]
        return A(buf, s * a + o, s * b + o - s + 1, s * step)

    def gather(k, h, width=W):
        x = Z_SCALAR[k][h]
        for eng, i0, i1 in ((actcp, 0, x), (cp, x, 32)):
            if i1 > i0:
                i0, i1 = 32 * h + i0, 32 * h + i1
                eng(Z(k, 16 * i0, 16 * i1), IND(A("X", 0, width), A("OFFZ", i0, i1)))

    def table(k):
        return ("K", 8, 11) if k == 1 else ("T" if k < 5 else "U", 16, 20 - k)

    def steps_at(i):
        ps, a = ("psD%d" % (i // 4), 256 + 64 * (i % 4)) if i < 8 else ("psY", 64 * (i - 8))
        return A(ps, a, a + 64)

    def uwrap(k, ps, a, b):
        msum(A(ps, 1, (b - a) // 8, 2), [(A("Wm", m * 128, m * 128 + 128), Z(k, a + m, b, 16)) for m in range(16)],
             False)

    def entry(k, h, C):
        d, top, s = table(k)
        src = A("psC", 0, 64) if h is None else A("psC", 32 * h, 32 * h + 32)
        msum(src, ([("GT8", C)] if k == 1 else [])
             + [("P512" if j == 3 else "P1K" if j % 2 else "N1K", R(d + "O", h, j)) for j in range(3, s)])
        return src, 960.0 - 2048.0 * (s % 2)

    def entries(k, h, src, off):
        for slot, x, y in ((1, 14.0, 17868.75), (0, -4.0, -594.0))[:2 if k < 7 else 1]:
            act(R("AD", h, slot), src, IDT, y + x * off, x)

    def maxima(j, h):
        s, s1 = (3, 4, 3)[j], 4 - j
        for a in range(512 * h, 512 * h + 512, PIECE):
            r = (s * a, s * (a + PIECE))
            scan(A("O%d" % j, *r), A("M%d" % s, 0, s * PIECE), A("G%d" % j, *r), MUL, MAX)
        for a in range(512 * h, 512 * h + 512 if j < 2 else 0, 256):
            gcp(A("G%d" % (j + 1), s1 * a, s1 * (a + 256), s1), A("O%d" % j, s * a + s - 1, s * (a + 256), s))

    def bases(k, h, height, log):
        d = table(k)[0]
        was, less = R(d + "A", h, 2), R(d + "A", h, 3)
        msum(height, [("I1", was), ("I1", less)])
        msum(log, [("N32", was), ("I4", less)])

    def head(t, h):
        LB, C, ps = R("LND%d" % t, h, 0), R("LND%d" % t, h, 1), "psW%d" % h
        if t:
            msum(A(ps, 128, 160), [("ID", R("STH", h)), ("ID", R("STL", h))], True, False)
            msum(A(ps, 128, 160), [("N512", LB), ("N101", LB)], False)
        mm(A("psB%d" % h, 192, 224), A("GT0"), LB)
        fixed[0] = h == 0
        if t:
            ts(R("OFFZ", h), A(ps, 128, 160), A("ACOL"), ADD)
        ts(R("EQ0", h), A("psB%d" % h, 192, 224), A("Q4"), EQ)
        ts(R("KB", h, 1), LB, 0.25, MUL)
        tt(R("SEL", h), R("EQ0", h), C, MUL)
        gather(0, h, W + AGAIN if t else W)
        fixed[0] = False
        for j in range(7):
            mm(A("psD%d" % h, 32 * j, 32 * j + 32), A("TL%d" % (9 + j if j else 0)), C)
        together(-7)
        msum(A("psB%d" % h, 128, 160), [("GTN", C), ("BM0", R("SEL", h))])
        entries(0, h, A("psB%d" % h, 128, 160), 0)
        mm(A(ps, 0, 64), A("NEG"), A("ALT", 0, 64), True, False)
        uwrap(0, ps, 512 * h, 512 * h + 512)
        for j in range(7):
            ts(R("KA", h, 4 + j), A("psD%d" % h, 32 * j, 32 * j + 32), -0.25, ADD)

    def tables(t):
        LB, C = R("LND%d" % t, None, 0), R("LND%d" % t, None, 1)
        for i in range(14):
            mm(steps_at(i), A("TL%d" % (i + 1)), C)
        for i in range(14):
            ts(R("TA", None, 4 + i), steps_at(i), -0.25, ADD)
        for i in range(11):
            gcp(R("UA", None, 4 + i), R("TA", None, 4 + i))
        for d in "TU":
            act(R(d + "B", None, 1), LB, IDT, 0.0, 0.25)
        act(A("W1"), LB, SQUARE, 3.1, -1.0)
        act(A("W2"), A("W1"), SQUARE)
        act(R("WD", None, 1), A("W2"), SQUARE)
        act(R("LG", None, 9), LB, IDT, 4.0, -1.0)

    def beat(t, k, h):
        C, ps, pb = R("LND%d" % t, h, 1), "psW%d" % h, "psB%d" % h
        d, top, s = table(k)
        fixed[0] = True
        scan(R("YI", h), A(ps, 0, 64), R("AD", h), MUL, ADD)
        tt(R("DH", h), A(ps, 1, 64, 2), R("AD", h, 1), ADD)
        ts(R("SI", h), R("YI", h, 1), 2, SHR, W - 1, AND)
        ts(R("N4", h), R("DH", h), 1, SHR, 3, AND)
        cp(R("OFFZ", h), R("SI", h))
        tt(R(d + "B", h, 0), R("N4", h), R("GAP" if k > 1 else "GAP0", h), GT)
        ts(R(d + "A", h, 3), R("N4", h), 0.25, MUL, -0.75, ADD)
        gather(k, h)
        if k < 7:
            mm(A(ps, 0, 64), A("NEG"), A("ALT", 0, 64), True, False)
            bases(k, h, A(pb, 0, 32), A(pb, 64, 96))
            scan(R(d + "O", h), R(d + "A", h), R(d + "B", h), ADD, MAX)
            c = entry(k, h, C)
            act(R("GAP", h), A(pb, 0, 32), IDT, A("M%d" % min(k, 2)), -4.0)
            act(R(table(k + 1)[0] + "A", h, 2), A(pb, 0, 32), IDT, 1.75 if k == 1 else -0.25)
            act(R("LG", h, 9 - k), A(pb, 64, 96), IDT, 8.0 * top - 81)
            entries(k, h, *c)
            uwrap(k, ps, 512 * h, 512 * h + 512)
        fixed[0] = False
        if k in (2, 4, 6):
            maxima(k // 2 - 1, h)

    def tail(t):
        last = t == RO - 1
        LB, C, F = R("LND%d" % t, None, 0), R("LND%d" % t, None, 1), A("F%d" % t)
        OH, VV = R("LG", None, 0), R("VO", None, 3)
        bases(7, None, A("psB0", 0, 64), A("psB0", 64, 128))
        act(A("PRE"), A("psB0", 0, 64), IDT, 52.0, -32.0)
        act(R("LG", None, 2), A("psB0", 64, 128), IDT, 47.0)
        mm(A("psW1", 0, 128), A("NEG"), A("ALT"), True, False)
        mm(A("psB1", 128, 256), A("I256"), A("TH2"), True, False)
        for ps, a, b, on in PARTS:
            mm(A(ps, 0, 16 * (b - a)), A("N256"), A("G1", 64 * a + 3, 64 * b, 4), True, False)
            mm(A(ps, 0, 16 * (b - a)), A("I255"), A("O2", 48 * a + 2, 48 * b, 3), False, False)
        fixed[0] = True
        for j, (ps, a, b, on) in enumerate(PARTS):
            a, b = 16 * a, 16 * b
            mm(A(ps, 0, b - a), A("ID"), Z(7, a, b), False, True)
            if on == "s":
                act(A("GEb", a, b), A(ps, 0, b - a), SIGN, -0.5)
            else:
                ts(A("GEb", a, b), A(ps, 0, b - a), 0.5, GE, -0.5, ADD)
            if j == 0:
                scan(A("UO"), A("UA"), A("UB"), ADD, MAX)
        uwrap(7, "psW1", 0, 1024)
        c = entry(7, None, C)
        msum(A("psB1", 128, 256, 2), [(A("Gm", m * 128, m * 128 + 128), A("GEb", m, 1024, 16)) for m in range(16)],
             False)
        fixed[0] = False
        entries(7, None, *c)
        actcp(A("O1", 0, 4096, 64), F)
        act(A("G2", 0, 3072, 48), F, IDT, 0.0, 0.0)
        tt(A("DH"), A("psW1", 1, 128, 2), R("AD", None, 1), ADD)
        ts(A("N4"), A("DH"), 1, SHR, 3, AND)
        mm(A("psW1", 128, 192), A("ID"), A("DG"), True, False)
        for h, ps in enumerate(LISTS):
            mm(A(ps, 0, 160), A("ID"), A("K5"), True, False)
            for l in range(5):
                mm(A(ps, l, 160, 5), A("SH%d" % l if l else "ID"), R("LND%d" % t, h, 1), False, False)
        mm(A("psW0", 0, 256), A("ID"), A("CM"), True, False)
        scan(A("WO"), A("WD"), A("psB1", 128, 256), MIN, MAX)
        tt(R("LG", None, 1), A("PRE"), A("N4"), ADD)
        mm(A("psD0", 0, 64), A("ALF"), R("WO", None, 1))
        ts(OH, A("psD0", 0, 64), 0.0, LT, 256.0, MUL)
        mm(A("psW1", 128, 192), A("MV"), OH, False, True)
        mm(A("psW1", 192, 256), A("BO3"), OH)
        mm(A("psB1", 0, 64), A("BO1" if last else "ONS"), OH)
        mm(A("psW0", 3, 256, 4), A("BON"), A("KX") if last else OH, False, False)
        fixed[0] = True
        for h in range(2):
            scan(R("OHL", h), A("LM"), R("LG", h), ADD, MIN)
        for h in range(2):
            for s in range(8):
                mm(A("psD%d" % h, 128 + s, 384, 8), A("BO"), R("OHL", h, 1 + s))
            together(-8)
            for l in range(5):
                mm(A(LISTS[h], l, 160, 5), A("TRI"), R("OHL", h, 9), False, l == 4)
            mm(A(LISTS[h], 160, 192), A("T255"), R("OHL", h, 9))
            together(-6)
        fixed[0] = False
        scan(A("SD"), A("M4F"), A("psW1", 128, 192), MUL, MAX)
        tt(A("EE"), A("psW1", 192, 256), LB, MAX)
        ts(A("OV"), A("SD", 3, 64, 4), A("SCL"), MUL, A("BIA"), ADD)
        if last:
            actcp(A("NOK"), A("psB1", 0, 64))
        else:
            act(A("PR"), A("psB1", 0, 64), IDT, 4 * 613 / 64, 1.0, A("ACOL"))
        for h in range(2):
            fixed[0] = True
            act(R("AS", h), A("psD%d" % h, 128, 384), ABS, A("QB"))
            if h == 0:
                (cp if last else actcp)(A("V4"), IND(Ap((T["ZV"][:], A("O1")[1] + A("G2")[1] + A("Z7")[1])), A("OV")))
            fixed[0] = False
            ts(R("AL", h), A(LISTS[h], 0, 160), 0.0, MAX, 255.0, MIN)
            scan(R("AO", h), A("M8"), R("AS", h), ADD, MIN)
            scan(R("ALO", h), A("M5"), R("AL", h), MUL, ADD)
            tt(R("YB", h) if last else R("SND%d" % t, h, 0), R("AO", h, 7), R("EE", h), MIN)
            tt(R("YC", h) if last else R("SND%d" % t, h, 1), R("ALO", h, 4), A(LISTS[h], 160, 192), SUB)
            if not last:
                send(R("SND%d" % t, h), R("LND%d" % (t + 1), h), "arr%d%d" % (t + 1, h), 1)
        scan(A("VO"), A("M4", 0, 256), A("V4"), MUL, MAX)
        mm(A("psW0", 0, 256, 4), A("W128"), VV, False, False)
        mm(A("psW0", 3, 256, 4), A("WB1"), VV, False, True)
        if last:
            act(A("YL"), A("YB"), IDT, 4.0, -1.0)
            tt(A("DIF"), VV, A("psB1", 0, 64), MUL)
        else:
            actcp(A("VP", 0, 64), VV)
            actcp(A("VP", 64, 96), R("VO", 0, 3))
        scan(A("X1"), A("MM"), A("psW0", 0, 256), MUL, ADD)
        tt(A("FVI"), F, VV, ADD)
        scan(A("SD2"), A("M16F"), R("X1", None, 3), MUL, MAX)
        ts(A("FH"), A("FVI"), 1, SHR)
        cp(A("OX", 0, 4), A("SD2", 15, 64, 16))
        cp(A("F%d" % (t + 1)), A("FH"))
        if last:
            tt(A("psW1", 0, 64), A("psY", 0, 64), A("DIF"), ADD)
            tt(A("SEL"), IND(A("X", 0, W), A("OX", 0, 4)), A("NOK"), MUL)
            tt(A("YS"), A("psW1", 0, 64), A("SEL"), SUB)
        else:
            ts(A("OX", 4, 6), A("SD2", 15, 32, 16), float(W), ADD)
            cp(IND(A("X"), A("OX", 0, 6)), A("VP", 0, 96))

    for t in range(RO):
        act(A("NF"), A("F%d" % t), IDT, -1.0)
        for m in range(16):
            gcp(A("G1", 4 * m + 3, 4096, 64), A("NF"))
        for h in range(2):
            head(t, h)
        tables(t)
        if t == 0:
            for a in range(0, AGAIN, 256):
                actcp(A("X", W + a, W + a + 256), A("X", a, a + 256))
        if t < RO - 1:
            starts(t + 1)
        else:
            for c in range(128):
                mm(A("psY", 0, 64), A("ID"), A("X", c, W, 128), c == 0, c == 127)
        for k in range(1, 8):
            for h in range(2):
                beat(t, k, h)
        tail(t)
    dma("y", "oC", T.yc[:], A("YC")[0], [], [A("YC")])
    dma("s", "oL", T.yl[:], A("YL")[0], [], [A("YL")])
    dma("y", "oF", T.yf[:], T["F4"][:], [], [A("F4")])
    dma("y", "oS", T.ys[:], T["YS"][:], [], [A("YS")])

    if not ORDER:
        ORDER.extend(plan(calls))
    for i in ORDER:
        if i >= loads:
            calls[i][5]()

    wait("g", "loc", sent[0])
    for t in range(1, RO):
        wait("g", "st%d" % t, len(topo.engines(T.cores[(rank - t) % n], core)))
        for h in range(2):
            wait("g", "arr%d%d" % (t, h), len(topo.engines(T.cores[(rank - 1) % n], core)))
    for s in ("dX", "dW", "dC", "dL", "dS", "dF"):
        wait("g", s, 16)
    for q in "gtsv":
        wait("g", "q" + q, count[q])
    for s in ("oF", "oC", "oL", "oS"):
        wait("g", s, 16)
